import numpy as np, ml_dtypes
CORES = [23,119,17,113]
N = 4
import mx_ref
BF = ml_dtypes.bfloat16
def gcols(t, e):
    v = np.concatenate([t.reshape(8, 16, -1, 4), np.zeros((8, 16, 1, 4), BF)], axis=2)
    return np.ascontiguousarray(np.stack([v[g][:, e[g]] for g in range(8)])).reshape(128, -1)
def cut(t, i, w=512):
    return t[:, w * i:w * i + w]
def pick(q, e):
    c = np.concatenate([q[0].reshape(128, -1, 4), np.zeros((128, 1, 4), np.uint8)], axis=1); s = np.concatenate([q[1], np.ones((16, 1), np.uint8)], axis=1)
    return (np.ascontiguousarray(c[:, e].reshape(128, -1)), np.ascontiguousarray(s[:, e]))
def join(*qs):
    return (np.concatenate([q[0] for q in qs], axis=1), np.concatenate([q[1] for q in qs], axis=1))
def put(q, e, v):
    c, s = q[0].reshape(128, -1, 4).copy(), q[1].copy(); c[:, e] = v[0].reshape(128, -1, 4); s[:, e] = v[1]
    return (c.reshape(128, -1), s)
def pk(c, s):
    return (np.ascontiguousarray(c), mx_ref.live(s))
def emit(q):
    return q[0], q[1]
def packed(v, rng):
    q = [mx_ref.quantize(np.ascontiguousarray(v[r])) for r in range(N)]
    return np.stack([a for a, b in q]), np.stack([mx_ref.plane(b, rng) for a, b in q])
def values_of_codes():
    e, c = np.zeros((128, 128, 4), np.float32), np.zeros((128, 2, 4), np.uint8)
    e[np.arange(128), np.arange(128), 0] = 1
    c[:127, :, 0] = np.arange(256).reshape(2, 128).T[:127]
    return mx_ref.matmul(mx_ref.quantize(e.reshape(128, 512).astype(BF)), (c.reshape(128, 8), np.full((16, 2), 127, np.uint8))).T.reshape(-1).astype(np.float64)
CODE_VALUE, SCALE_VALUE = values_of_codes(), 2.0 ** (np.arange(256) - 127.0)
def decode(q):
    return (CODE_VALUE[q[0]].reshape(16, 8, -1, 4) * SCALE_VALUE[q[1]][:, None, :, None] + 0.0).reshape(128, -1).astype(np.float32)
def f(rng, *shape):
    return mx_ref.flush((rng.standard_normal(shape, dtype=np.float32) * np.exp2(rng.integers(-2, 3, shape[:-1] + (1,)))).astype(BF))
def wide(rng, *shape, cols=0):
    v = rng.standard_normal(shape, dtype=np.float32) * np.exp2(rng.integers(-12, 13, shape)).astype(np.float32)
    if cols: v *= np.repeat(np.exp2(rng.integers(-cols, cols + 1, shape[:-2] + (1, shape[-1] // 4))) * (rng.random(shape[:-2] + (1, shape[-1] // 4)) > 0.0625), 4, axis=-1).astype(np.float32)
    return mx_ref.flush(v.astype(BF))
C, K, M, R = 448, 160, 24, 3
STEP = [1, 2, 1]
def order(s, k):
    s, k = s + np.float32(0.0), k + np.float32(0.0)
    best = np.argsort(-s[:, 1:], axis=1, kind="stable")[:, :M - 1] + 1
    head = np.sort(np.concatenate([np.zeros((8, 1), np.int64), best], axis=1), axis=1)
    last = np.concatenate([head[:, 1:] - 1, np.full((8, 1), C - 1)], axis=1)
    key = np.take_along_axis(k, head, axis=1)
    turn = key < np.take_along_axis(k, last, axis=1)
    run = np.argsort(-key, axis=1, kind="stable")
    return np.stack([np.concatenate([np.arange(head[g, n], last[g, n] + 1)[::-1 if turn[g, n] else 1] for n in run[g]]) for g in range(8)])
def strip(v):
    v = v.astype(np.float32)
    v[np.abs(v) < np.float32(2.0 ** -16)] = 0
    return v.astype(BF)
def numbers_of(rng):
    return {"x": strip(f(rng, N, 128, 4 * C)), "u": np.array(f(rng, N, 128, 512)), "v": np.array(f(rng, N, 128, 512))}
def weights(rng, e=slice(0, 0)):
    w = np.array(f(rng, N, 128, 2048)).reshape(N, 8, 16, 4, 8, 16, 4)
    w[:, :, e] = 0
    w[:, :, :, :, :, e] = 0
    c, p = packed(w.reshape(N, 128, 2048), rng)
    return {"wc": c, "ws": p}
def signs(rng):
    return np.stack([rng.permutation(8) % 2 * 2.0 - 1.0 for r in range(N)])
def small(rng):
    return np.where(rng.permutation(N) < N // 2, 2.0 ** -30, 1.0).astype(np.float32)
def setup_inputs(rng):
    return {**numbers_of(rng), **weights(rng)}
def setup_inputs_ties(rng):
    d = numbers_of(rng)
    e = rng.permutation(N)
    x = d["x"].reshape(N, 8, 16, C, 4)
    for r in range(N):
        k = np.zeros(C, int) if r == e[0] else rng.permutation(C) % 3
        a = x[r][:, :8, :3].copy()
        a[:, :, 2] = 0
        x[r][:, :8] = a[:, :, k]
    x[e[1]] = 0
    u = d["u"].reshape(N, 128, 128, 4)
    for g in range(0, 128, 16):
        for h in (g, g + 1):
            a = u[:, g:g + 8, h].copy()
            u[:, :, h] = 0
            u[:, g:g + 8, h] = a
    return {"x": x.reshape(N, 128, 4 * C), "u": u.reshape(N, 128, 512), "v": d["v"], **weights(rng, slice(0, 8))}
def setup_inputs_near(rng):
    d = numbers_of(rng)
    x = d["x"].astype(np.float32).reshape(N, 8, 16, C, 4)
    s = np.zeros((N, 8, C), np.int64)
    s[:, :, 1:] = (1 + np.argsort(rng.random((N, 8, C - 1)), axis=2)) // 2
    k = rng.integers(0, 12, (N, 8, C))
    digit = np.exp2(np.arange(8) - 23.0)
    a = ((s[..., None] >> np.arange(8)) & 1) * digit
    x[:, :, 0] = 0
    x[:, :, 0, :, 0] = signs(rng)[:, :, None]
    x[:, :, 8] = a[..., :4]
    x[:, :, 9] = a[..., 4:]
    x[:, :, 10] = ((k[..., None] >> np.arange(4)) & 1) * digit[:4]
    x[:, :, 11:] = rng.integers(4, 8, (N, 8, 5, C, 4)) * rng.choice([-1.0, 1.0], (N, 8, 5, C, 4)) * 2.0 ** -20
    u = d["u"].reshape(N, 128, 128, 4)
    one = small(rng).astype(BF)
    u[:, :, ::16] = 0
    u[:, :, 1::16] = 0
    for h in range(0, 128, 16):
        u[:, h, h, 0] = one
        u[:, h, h + 1, 0] = one
        u[:, h + 8:h + 10, h] = one[:, None, None]
        u[:, h + 10, h + 1] = one[:, None]
    return {"x": x.reshape(N, 128, 4 * C).astype(BF), "u": u.reshape(N, 128, 512), "v": d["v"], **weights(rng, np.r_[0, 8:16])}
def setup_inputs_runs(rng):
    d = numbers_of(rng)
    x = d["x"].astype(np.float32).reshape(N, 8, 16, C, 4)
    x[:, :, :8] = rng.integers(1, 4, (N, 8, 8, C, 4))
    x[:, :, :2] = 0
    for r in range(N):
        kind = rng.permutation(8)
        for g in range(8):
            i = kind[g] % 4
            lo, hi = ((1, M), (C - M + 1, C), (K + 1, C), (1, C))[i]
            e = lo + rng.permutation(hi - lo)[:M - 1]
            s = rng.integers(-1, 2, C) * 1.0
            s[e] = 1.25
            s[0] = 3
            k = rng.integers(-4, 4, C)
            if i == 0: k = 3 - np.arange(C) * 8 // C
            if i == 1: k = np.arange(C) * 8 // C - 4
            if i == 2:
                k = rng.integers(-4, 2, C) * 1.0
                k[0] = 2
                if kind[g] > 3: k[np.min(e) - 1] = 2.5
            x[r, g, 0, :, 0] = s
            x[r, g, 1, :, 0] = k
    one = small(rng)
    x[:, :, :8] *= one[:, None, None, None, None]
    u = d["u"].reshape(N, 128, 128, 4)
    u[:, :, ::16] = 0
    u[:, :, 1::16] = 0
    for h in range(0, 128, 16):
        u[:, h, h, 0] = one.astype(BF)
        u[:, h + 1, h + 1, 0] = one.astype(BF)
    return {"x": x.reshape(N, 128, 4 * C).astype(BF), "u": u.reshape(N, 128, 512), "v": d["v"], **weights(rng, slice(0, 8))}
def setup_inputs_huge(rng):
    d = numbers_of(rng)
    o = rng.permutation(N)
    x = 0.8 + 0.2 * rng.random((N, 128, C, 4))
    most = np.where(rng.random((128, C, 4)) < 0.03125, 0.9375, 1.0)
    most[:, rng.permutation(C) % 4 == 0] = 1
    x[o == 0] = most
    c = np.stack([rng.permutation(C) % 2 * 2.0 - 1.0 for r in range(N)])
    c[o < N // 2] = 1
    x *= 2.0 ** 30 * c[:, None, :, None]
    u = d["u"].reshape(N, 128, 128, 4)
    for i in range(2):
        a = 1 - 0.125 * rng.random((N, 128, 8, 4))
        a[o == 0] = 1
        a *= 2.0 ** 30 * signs(rng)[:, None, :, None]
        u[:, :, i::16] = a.astype(np.float32).astype(BF)
    return {"x": x.astype(np.float32).reshape(N, 128, 4 * C).astype(BF), "u": u.reshape(N, 128, 512), "v": d["v"], **weights(rng, slice(0, 16))}
def setup_inputs_spread(rng):
    d = setup_inputs(rng)
    d["x"] = strip(wide(rng, N, 128, 4 * C, cols=6))
    return d
def check_inputs(d):
    b = []
    for k in ("x", "u", "v"):
        a = np.abs(d[k].astype(np.float32))
        if not (np.isfinite(a).all() and ((a == 0) | (a >= 2.0 ** -30) & (a <= 2.0 ** 30)).all()): b.append("a value of " + k)
    return b
def reference(x, u, v, wc, ws):
    qu = [mx_ref.quantize(u[r]) for r in range(N)]
    lay = [pk(wc[r], ws[r]) for r in range(N)]
    now = [x[r] for r in range(N)]
    for t in range(R):
        o, border = [], []
        for r in range(N):
            p = mx_ref.matmul(qu[r], mx_ref.quantize(now[r]))
            o.append(order(p[::16], p[1::16]))
            border.append(mx_ref.quantize(gcols(now[r], o[r][:, :K])))
        came = decode(join(*border)).astype(BF)
        for r in range(N):
            e = np.concatenate([cut(came, r ^ STEP[t], 4 * K), gcols(now[r], o[r][:, K:])], axis=1)
            q = mx_ref.quantize(np.ascontiguousarray(e))
            h = [np.maximum(mx_ref.matmul(pick(lay[r], np.arange(128 * b, 128 * b + 128)), q), np.float32(0.0)) * np.float32(0.015625) for b in range(4)]
            now[r] = (e.astype(np.float32) + np.stack(h, axis=2).reshape(128, -1)).astype(BF)
    y, ol = np.zeros((N, 128, C), np.float32), np.zeros((N, 8, C), np.float32)
    oc, osc = np.zeros((N, 128, 4 * C), np.uint8), np.zeros((N, 16, C), np.uint8)
    for r in range(N):
        q = mx_ref.quantize(now[r])
        y[r] = mx_ref.matmul(mx_ref.quantize(v[r]), q)
        ol[r] = o[r]
        oc[r], osc[r] = emit(q)
    return {"y": y, "ol": ol, "oc": oc, "osc": osc}

@@ -1,0 +1,494 @@
+from concourse.mybir import dt, AluOpType, AxisListType, ActivationFunctionType
+
+C, K, R = 448, 160, 3
+STEP = [1, 2, 1]
+F32, BF, I32, U16, U8, X4 = "float32", "bfloat16", "int32", "uint16", "uint8", "float8_e4m3fn_x4"
+BIG = 1e29
+TINY = 1e-32
+STEPK = 512.0
+BASE = 2048.0 * 480
+MAGIC = 1.5 * 2.0 ** 34
+
+_SB = {
+    "ut": (512, BF), "vt": (512, BF), "qu": (128, X4), "su": (128, U8), "qu2": (256, X4), "su2": (256, U8),
+    "qv": (128, X4), "sv": (128, U8), "qw": (512, X4), "sw": (512, U8),
+    "Et": (4 * C, BF), "qe": (C, X4), "se": (C, U8), "Rr": (4 * C, F32), "Dp": (4 * C, BF),
+    "pint": (2, I32), "iint": (2, I32), "pf": (2, F32), "fi": (2, F32), "fg": (2, F32), "ni": (2, F32), "kn": (2, F32),
+    "J": (464, F32), "J16": (C, BF), "Jg": (512, BF), "Jb": (128, BF), "oui": (16, I32), "ou": (16, U16),
+    "mask": (C, BF), "rs16": (112, BF), "tie": (112, F32), "tie2": (64, F32), "one": (464, BF),
+    "rsM": (C, BF), "dec": (C, F32), "r2": (C, F32), "zer": (512, BF), "ident": (128, BF),
+    "Wt": (512, BF), "qo": (128, X4), "so": (128, U8), "Ut": (2048, BF), "qd": (512, X4), "sd": (512, U8),
+    "Ms": (C, F32), "Mm": (112, F32), "own": (112, F32), "dd": (112, F32), "sg": (192, BF), "F1": (1024, BF), "F2": (1024, BF),
+    "qf": (256, X4), "sf": (256, U8), "sel1": (120, BF), "sel2": (104, BF), "Rp": (256, BF), "cap1": (256, BF),
+    "cap2": (256, F32), "off1": (2, U16), "off2": (2, U16), "Sp": (512, F32), "Kw": (456, F32), "Kp": (456, F32),
+    "Cd": (128, F32), "cc": (128, F32), "key": (32, F32), "kp": (32, F32), "H1": (40, F32), "W2": (32, F32),
+    "km": (32, F32), "ko": (32, F32), "LL": (64, F32), "dk": (64, F32), "FL": (64, F32), "PR": (64, F32), "turn": (24, F32),
+    "c1": (24, F32), "cod": (32, F32), "Pp": (2, F32), "off3": (2, U16), "Ww": (456, F32), "us": (C, F32),
+    "wr": (C, F32), "rr": (28, F32), "ya": (28, F32), "yb": (28, F32), "oo": (28, F32), "offo": (72, U16),
+    "olt": (C, F32), "yt": (C, F32),
+}
+for _r in range(R + 1):
+    _SB["X%d" % _r] = (4 * C, BF)
+    _SB["qx%d" % _r] = (C, X4)
+    _SB["sx%d" % _r] = (C, U8)
+for _r in range(R):
+    _SB["lq%d" % _r] = (C, X4)
+    _SB["ls%d" % _r] = (C, U8)
+    _SB["lst%d" % _r] = (16, U16)
+    _SB["ord%d" % _r] = (28, U16)
+SCRATCH = {k: ("sbuf", [128, n], d) for k, (n, d) in _SB.items()}
+SCRATCH["ps"] = ("psum", [128, 4096], F32)
+SEMAPHORES = (["sV", "sS", "sP", "sG", "sent"] + ["dm%d" % i for i in range(20)]
+              + ["arr%d" % r for r in range(R)] + ["lis%d" % r for r in range(R)])
+
+
+def rank_program(g, core, T, topo):
+    rank = T.rank_of(core)
+    if rank is None:
+        return
+    A, ACT = AluOpType, ActivationFunctionType
+    queue = {"V": g.vector, "S": g.scalar, "P": g.tensor, "G": g, "Y": g.sync}
+    ops, acc, ndma, sent = [], {}, [0], [0]
+
+    def v(name, a=0, b=None, s=1):
+        return (name, a, _SB[name][0] if b is None else b, s)
+
+    def bank(k, a, b, s=1):
+        return ("ps", 512 * k + a, 512 * k + b, s)
+
+    def ind(w, o):
+        return ("@", w, o)
+
+    def ap(x):
+        if not isinstance(x, tuple):
+            return x
+        if x[0] == "@":
+            return ap(x[1]).indirect(ap(x[2]))
+        return T[x[0]][:, x[1]:x[2]] if x[3] == 1 else T[x[0]][:, x[1]:x[2]:x[3]]
+
+    def bits(x):
+        if x[0] == "ps":
+            return 1 << (x[1] // 512)
+        if x[3] == 1:
+            return ((1 << (x[2] - x[1])) - 1) << x[1]
+        m = 0
+        for c in range(x[1], x[2], x[3]):
+            m |= 1 << c
+        return m
+
+    def record(q, fn, outs, ins, sem=None, count=0):
+        rd, wr = [], []
+        for x in ins:
+            if isinstance(x, tuple):
+                rd.extend([x[1], x[2]] if x[0] == "@" else [x])
+        for x in outs:
+            if x[0] == "@":
+                wr.append(x[1])
+                rd.append(x[2])
+            else:
+                wr.append(x)
+        me, deps = len(ops), set()
+        for lst, w in ((rd, False), (wr, True)):
+            for x in lst:
+                m = bits(x)
+                for (o, m2, w2) in acc.get(x[0], []):
+                    if not m & m2:
+                        continue
+                    if x[0] == "ps":
+                        if ops[o]["q"] != q:
+                            deps.add(o)
+                    elif w or w2:
+                        deps.add(o)
+        for lst, w in ((rd, False), (wr, True)):
+            for x in lst:
+                acc.setdefault(x[0], []).append((me, bits(x), w))
+        ops.append({"q": q, "fn": fn, "deps": deps, "sem": sem, "count": count})
+        return me
+
+    def ts(o, i, s1, s2, op0, op1=None):
+        if op1 is None:
+            record("V", lambda: g.vector.tensor_scalar(ap(o), ap(i), ap(s1), None, op0), [o], [i, s1])
+        else:
+            record("V", lambda: g.vector.tensor_scalar(ap(o), ap(i), ap(s1), ap(s2), op0, op1), [o], [i, s1, s2])
+
+    def tt(o, a, b, op):
+        record("V", lambda: g.vector.tensor_tensor(ap(o), ap(a), ap(b), op), [o], [a, b])
+
+    def cp(o, i):
+        record("V", lambda: g.vector.tensor_copy(ap(o), ap(i)), [o], [i])
+
+    def scan(o, d0, d1, init, op0, op1):
+        record("V", lambda: g.vector.tensor_tensor_scan(ap(o), ap(d0), ap(d1), ap(init), op0, op1), [o], [d0, d1, init])
+
+    def red(o, i):
+        record("V", lambda: g.vector.tensor_reduce(ap(o), ap(i), AxisListType.X, A.add), [o], [i])
+
+    def fill(o, c):
+        record("V", lambda: g.vector.memset(ap(o), c), [o], [])
+
+    def quant(q, s, i):
+        record("V", lambda: g.vector.quantize_mx(ap(q), ap(s), ap(i)), [q, s], [i])
+
+    def act(o, i, f, bias=None, scale=None):
+        kw = {}
+        if bias is not None:
+            kw["bias"] = ap(bias)
+        if scale is not None:
+            kw["scale"] = scale
+        record("S", lambda: g.scalar.activation(ap(o), ap(i), f, **kw), [o], [i, bias])
+
+    def mm(o, wq, ws_, xq, xs, start=True, stop=True):
+        record("P", lambda: g.tensor.matmul_mx(ap(o), ap(wq), ap(ws_), ap(xq), ap(xs), start, stop), [o], [wq, ws_, xq, xs])
+
+    def iota(o, pat, base, ch, small=False):
+        if small:
+            record("G", lambda: g.iota(ap(o), pat, base, ch, allow_small_or_imprecise_dtypes=True), [o], [])
+        else:
+            record("G", lambda: g.iota(ap(o), pat, base, ch), [o], [])
+
+    def dma(q, out, in_, outs, ins):
+        s = "dm%d" % ndma[0]
+        ndma[0] += 1
+        return record(q, lambda: queue[q].dma_start(out(), in_()), outs, ins, sem=s, count=16)
+
+    def partner(r):
+        return T.cores[rank ^ STEP[r]]
+
+    def remote(r, dst, src, sem, codes):
+        p = partner(r)
+        rid, pid, _ = topo.addr(p)
+        n = len(topo.engines(core, p))
+        sent[0] += n
+
+        def go():
+            o, i = ap(dst), ap(src)
+            if codes:
+                o, i = o.bitcast(dt.uint8), i.bitcast(dt.uint8)
+            g.remote_dma(o, i, T.sem[sem], T.sem.sent, pid, rid, topo.mask(core, p))
+        record("G", go, [], [src], sem="none")
+
+    def arrival(r, outs, sem, writes):
+        record("-", None, outs, [], sem=sem, count=writes * len(topo.engines(partner(r), core)))
+
+    PARTS = {"A": (K, C, 4), "B": (0, K, 0)}
+
+    dma("S", lambda: T.ut[:], lambda: T.u[:], [v("ut")], [])
+    dma("Y", lambda: T.X0[:, 4 * K:4 * C], lambda: T.x[:, 4 * K:4 * C], [v("X0", 4 * K, 4 * C)], [])
+    dma("S", lambda: T.X0[:, 0:4 * K], lambda: T.x[:, 0:4 * K], [v("X0", 0, 4 * K)], [])
+    dma("Y", lambda: T.qw[:].bitcast(dt.uint8), lambda: T.wc[:], [v("qw")], [v("X0")])
+    dma("Y", lambda: T.sw[:], lambda: T.ws[:], [v("sw")], [])
+    dma("Y", lambda: T.vt[:], lambda: T.v[:], [v("vt")], [])
+    for r in range(R):
+        arrival(r, [v("lq%d" % r), v("ls%d" % r)], "arr%d" % r, 4)
+        arrival(r, [v("lst%d" % r)], "lis%d" % r, 1)
+
+    iota(v("pint"), [[16, 2]], 0, 1)
+    iota(v("oui"), [[1, 2], [16, 8]], 0, 0)
+    iota(v("J16"), [[0, C // 16], [1, 16]], 0, 0, True)
+    iota(v("Jg"), [[16, 8], [0, 64]], 0, 0, True)
+    fill(v("zer"), 0.0)
+    fill(v("one"), 1.0)
+    fill(v("rsM"), 0.0)
+    for b in range(4):
+        act(v("Ut", 512 * b, 512 * b + 512), v("zer"), ACT.Copy)
+    ts(v("iint", 0, 1), v("pint", 0, 1), 15, None, A.bitwise_and)
+    cp(v("pf", 0, 1), v("pint", 0, 1))
+    scan(v("J"), v("one"), v("zer", 0, 464), -1.0, A.add, A.add)
+    cp(v("fi", 0, 1), v("iint", 0, 1))
+    fill(v("rsM", 4, C, 4), -4 * BIG)
+    ts(v("ident"), v("J", 0, 128), v("pf", 0, 1), None, A.is_equal)
+    for q in range(2):
+        ts(v("ni", q, q + 1), v("fi", 0, 1), 16.0 * q, None, A.add)
+    tt(v("fg", 0, 1), v("pf", 0, 1), v("fi", 0, 1), A.subtract)
+    cp(v("ou"), v("oui"))
+    ts(v("kn"), v("ni"), 1.0, STEPK, A.add, A.mult)
+    fill(v("F1"), 0.0)
+    ts(v("mask"), v("J16"), v("fi", 0, 1), None, A.is_equal)
+    for b in range(4):
+        act(v("Ut", 513 * b, 512 * b + 512, 4), v("ident"), ACT.Copy)
+    quant(v("qu"), v("su"), v("ut"))
+    ts(v("rs16"), v("J16", 0, 112), 0.0, None, A.not_equal)
+    record("V", lambda: g.vector.tensor_copy(T.qu2[:, 0:256].bitcast(dt.uint32), T.qu[:, 0:128].bitcast(dt.uint32).indirect(T.ou[:, 0:16])),
+           [v("qu2")], [v("qu"), v("ou")])
+    act(v("su2"), ind(v("su"), v("ou")), ACT.Copy)
+    for h in range(2):
+        act(v("F2", 512 * h, 512 * h + 512), v("zer"), ACT.Copy)
+
+    def late0():
+        ts(v("Wt"), v("Jg"), v("fg", 0, 1), None, A.is_equal)
+        fill(v("Sp", 0, 1), BIG)
+        ts(v("tie"), v("J16", 0, 112), v("fi", 0, 1), -TINY, A.is_gt, A.mult)
+
+    def late1():
+        fill(v("sel1", 112, 120), -STEPK)
+        cp(v("Jb"), v("J", 0, 128))
+        cp(v("Rp", 0, 129, 128), v("kn"))
+        fill(v("sel2", 96, 104), -STEPK)
+        fill(v("H1", 32, 33), BASE + 456.0)
+        for e in range(4):
+            act(v("Sp", 128 * e + 112, 128 * e + 120), v("zer", 0, 8), ACT.Copy)
+        act(v("Kw", C, 456), v("zer", 0, 8), ACT.Identity, bias=-BIG)
+        act(v("Kp", 0, 1), v("zer", 0, 1), ACT.Copy)
+        act(v("Kp", C + 1, 456), v("zer", 0, 7), ACT.Copy)
+        act(v("cod", 24, 32), v("zer", 0, 8), ACT.Copy)
+
+    def late2():
+        quant(v("qd"), v("sd"), v("Ut"))
+        for q in range(2):
+            ts(v("tie2", 32 * q, 32 * q + 32), v("J", 0, 32), v("ni", q, q + 1), -TINY, A.is_lt, A.mult)
+        act(v("dec"), v("zer", 0, C), ACT.Identity, bias=-2047.0)
+        act(v("r2"), v("mask"), ACT.Identity, bias=-2048.0, scale=4194304.0)
+
+    def state_quant(r, part):
+        a, b, k = PARTS[part]
+        qx, sx = v("qx%d" % r, a, b), v("sx%d" % r, a, b)
+        quant(qx, sx, v("X%d" % r, 4 * a, 4 * b))
+        if r < R:
+            remote(r, v("lq%d" % r, a, b), qx, "arr%d" % r, True)
+            remote(r, v("ls%d" % r, a, b), sx, "arr%d" % r, False)
+            for j, c in ((0, 0), (1, 0), (2, 128)):
+                mm(bank(k + j, 0, b - a), v("qu2", c, c + 128), v("su2", c, c + 128), qx, sx)
+        else:
+            mm(bank(k, 0, b - a), v("qv"), v("sv"), qx, sx)
+
+    def maxima(part):
+        a, b, k = PARTS[part]
+        scan(v("Ms", a, b), v("rsM", a, b), bank(k, 0, b - a), BIG if a == 0 else 0.0, A.add, A.max)
+
+    def score_copies(part):
+        a, b, k = PARTS[part]
+        for e in range(4):
+            s = 1 if a == 0 and e == 0 else 0
+            act(v("Sp", 128 * e + a // 4 + s, 128 * e + b // 4), bank(k + 1, e + 4 * s, b - a, 4), ACT.Copy)
+
+    def key_copies(part):
+        a, b, k = PARTS[part]
+        act(v("Kw", a, b), bank(k + 2, 0, b - a), ACT.Copy)
+        act(v("Kp", a + 1, b + 1), bank(k + 2, 0, b - a), ACT.Copy)
+
+    def part_of(src, c0, c1):
+        name, a0, s0 = src
+        return (name, a0 + s0 * c0, a0 + s0 * (c1 - 1) + 1, s0)
+
+    def masked(src, c0, c1):
+        tt(v("Mm", c0, c1), part_of(src, c0, c1), v("mask", c0, c1), A.mult)
+
+    def owned(c0, c1):
+        scan(v("own", c0, c1), v("rs16", c0, c1), v("Mm", c0, c1), 0.0, A.mult, A.add)
+
+    BLOCKS, COLUMNS = ("Ms", 3, 4), ("Cd", 0, 1)
+
+    def block_maxima(between):
+        maxima("A")
+        between()
+        masked(BLOCKS, 48, 112)
+        maxima("B")
+        owned(48, 112)
+        masked(BLOCKS, 0, 48)
+        owned(0, 48)
+
+    def select(src, nq, F, sel, w, vals, cap, off, gap):
+        n = 16 * nq
+        place = {q: q - 1 for q in range(1, nq - 1)}
+        place.update({0: nq - 2, nq - 1: nq - 1, "tie": nq})
+
+        def slot(q, c0, c1):
+            o = 512 * (place[q] // 4) + place[q] % 4
+            return v(F, o + 4 * c0, o + 4 * (c1 - 1) + 1, 4)
+
+        def me(q):
+            return v("own", 16 * q + 15, 16 * q + 16)
+        for q in reversed(range(nq)):
+            act(v("dd", 16 * q, 16 * q + 16), part_of(src, 16 * q, 16 * q + 16), ACT.Identity, bias=me(q), scale=-1.0)
+        act(v("sg", 0, n - 16), part_of(src, 16, n), ACT.Sign, bias=me(0), scale=-1.0)
+        act(v("sg", 96, 96 + n - 16), part_of(src, 0, n - 16), ACT.Sign, bias=me(nq - 1), scale=-1.0)
+        act(slot(0, 16, n), v("sg", 0, n - 16), ACT.Sign, bias=1.0)
+        act(slot(nq - 1, 0, n - 16), v("sg", 96, 96 + n - 16), ACT.Relu)
+        for q in (3, 4, 1, 2, 5)[:nq - 2]:
+            ts(slot(q, 0, 16 * q), part_of(src, 0, 16 * q), me(q), None, A.is_lt)
+            ts(slot(q, 16 * q + 16, n), part_of(src, 16 * q + 16, n), me(q), None, A.is_le)
+        tt(slot("tie", 0, n), v("dd", 0, n), v("tie", 0, n), A.is_gt)
+        for h in range(2):
+            quant(v("qf", 128 * h, 128 * h + 128), v("sf", 128 * h, 128 * h + 128), v(F, 512 * h, 512 * h + 512))
+            mm(bank(3, 0, 128), v("qo"), v("so"), v("qf", 128 * h, 128 * h + 128), v("sf", 128 * h, 128 * h + 128), h == 0, h == 1)
+        gap()
+        ts(v(sel, 0, n), bank(3, 0, n), 23.5, -STEPK, A.is_lt, A.mult)
+        for q in range(2):
+            scan(v("Rp", 128 * q + 1, 128 * q + w), v(sel, 0, w - 1), v("zer", 0, w - 1), v("kn", q, q + 1), A.add, A.max)
+        for q in range(2):
+            scan(v(cap, 128 * q, 128 * q + w), v("Rp", 128 * q, 128 * q + w), v(vals, 0, w), 0.0, A.add, A.min)
+        cp(v(off), v(cap, w - 1, w + 128, 128))
+
+    def order(r):
+        def gap1():
+            key_copies("B")
+            if r == 0:
+                late1()
+
+        def gap2():
+            if r == 0:
+                late2()
+            act(v("Ww"), v("zer", 0, 456), ACT.Copy)
+            for b in range(4):
+                mm(bank(4 + b, 0, C), v("qd", 128 * b, 128 * b + 128), v("sd", 128 * b, 128 * b + 128), v("lq%d" % r), v("ls%d" % r))
+        select(BLOCKS, 7, "F1", "sel1", 120, "Jb", "cap1", "off1", gap1)
+        for e in range(4):
+            o, i = v("Cd", e, 128, 4), ind(v("Sp", 128 * e, 128 * e + 120), v("off1"))
+            if e < 2:
+                cp(o, i)
+            else:
+                act(o, i, ACT.Copy)
+        for e in range(4):
+            act(v("cc", e, 128, 4), ind(v("J", 0, 128), v("off1")), ACT.Identity, bias=float(e), scale=4.0)
+        masked(COLUMNS, 0, 96)
+        owned(0, 96)
+        select(COLUMNS, 6, "F2", "sel2", 104, "cc", "cap2", "off2", gap2)
+        cp(v("key"), ind(v("Kw"), v("off2")))
+        act(v("H1", 0, 32), ind(v("J"), v("off2")), ACT.Identity, bias=BASE)
+        act(v("kp"), ind(v("Kp"), v("off2")), ACT.Copy)
+        act(v("W2"), ind(v("J"), v("off2")), ACT.Identity, bias=BASE + 2049.0, scale=-1.0)
+        for b in range(4):
+            act(v("Dp", C * b, C * b + C), bank(4 + b, 0, C), ACT.Copy)
+        tt(v("km"), v("key"), v("mask", 0, 32), A.mult)
+        tt(v("LL", 0, 32), v("H1", 1, 33), v("H1", 0, 32), A.subtract)
+        scan(v("ko"), v("rs16", 0, 32), v("km"), 0.0, A.mult, A.add)
+        tt(v("LL", 32, 64), v("H1", 1, 33), v("H1", 0, 32), A.subtract)
+        for q in range(2):
+            ts(v("dk", 32 * q, 32 * q + 32), v("key"), v("ko", 16 * q + 15, 16 * q + 16), None, A.subtract)
+        tt(v("turn"), v("key", 0, 24), v("kp", 1, 25), A.is_lt)
+        tt(v("FL"), v("dk"), v("tie2"), A.is_gt)
+        tt(v("c1"), v("turn"), v("W2", 1, 25), A.mult)
+        tt(v("PR"), v("FL"), v("LL"), A.mult)
+        tt(v("cod", 0, 24), v("c1"), v("H1", 0, 24), A.max)
+        for q in range(2):
+            red(v("Pp", q, q + 1), v("PR", 32 * q, 32 * q + 32))
+        cp(v("off3"), v("Pp"))
+        cp(ind(v("Ww"), v("off3")), v("cod"))
+        scan(v("us"), v("dec"), v("Ww", 0, C), 0.0, A.add, A.max)
+        scan(v("wr"), v("r2"), v("us"), 0.0, A.add, A.min)
+        w = v("wr", 15, C, 16)
+        ts(v("rr"), w, MAGIC, MAGIC, A.add, A.subtract)
+        tt(v("ya"), w, v("rr"), A.subtract)
+        tt(v("yb"), v("rr"), w, A.subtract)
+        tt(v("oo"), v("ya"), v("yb"), A.max)
+        cp(v("ord%d" % r), v("oo"))
+        remote(r, v("lst%d" % r, 0, 10), v("ord%d" % r, 0, 10), "lis%d" % r, False)
+        for t in (2, 3, 0, 1):
+            ts(v("offo", 18 * t, 18 * t + 18), v("oo", 10, 28), 4.0, float(t), A.mult, A.add)
+
+    def nothing():
+        pass
+
+    def layer(r):
+        X, Y = "X%d" % r, "X%d" % (r + 1)
+        runs = ((K, K + 128, 0), (K + 128, C, 4), (0, K, 0))
+
+        def gather(a, b):
+            for t in (2, 0, 3, 1):
+                m = 18 * t + (a - K) // 16
+                o, i = v("Et", 4 * a + t, 4 * b, 4), ind(v(X), v("offo", m, m + (b - a) // 16))
+                if t < 2:
+                    cp(o, i)
+                else:
+                    act(o, i, ACT.Copy)
+
+        def product(a, b, k):
+            quant(v("qe", a, b), v("se", a, b), v("Et", 4 * a, 4 * b))
+            for j in range(4):
+                mm(bank(k + j, 0, b - a), v("qw", 128 * j, 128 * j + 128), v("sw", 128 * j, 128 * j + 128), v("qe", a, b), v("se", a, b))
+
+        def relu(a, b, k):
+            for j in range(4):
+                act(v("Rr", C * j + a, C * j + b), bank(k + j, 0, b - a), ACT.Relu, scale=0.015625)
+
+        def add(a, b):
+            for j in range(4):
+                tt(v(Y, 4 * a + j, 4 * b, 4), v("Et", 4 * a + j, 4 * b, 4), v("Rr", C * j + a, C * j + b), A.add)
+        for a, b, k in runs[:2]:
+            gather(a, b)
+            product(a, b, k)
+        if r == R - 1:
+            quant(v("qv"), v("sv"), v("vt"))
+        for a, b, k in runs[:2]:
+            relu(a, b, k)
+            add(a, b)
+        for t in range(4):
+            act(v("Et", t, 4 * K, 4), ind(v("Dp", C * t, C * t + C), v("lst%d" % r, 0, 10)), ACT.Copy)
+        product(*runs[2])
+        state_quant(r + 1, "A")
+        relu(*runs[2])
+        if r + 1 < R:
+            score_copies("A")
+            key_copies("A")
+        else:
+            dma("Y", lambda: T.oc[:, 4 * K:4 * C], lambda: T[QL][:, K:C].bitcast(dt.uint8), [], [v(QL, K, C)])
+            act(v("yt", K, C), bank(4, 0, C - K), ACT.Copy)
+            dma("Y", lambda: T.y[:, K:C], lambda: T.yt[:, K:C], [], [v("yt", K, C)])
+            act(v("olt"), ind(v("J"), v("ord%d" % r)), ACT.Copy)
+            dma("Y", lambda: T.ol[:], lambda: T.olt[0:128:16, :], [], [v("olt")])
+        add(0, K)
+        state_quant(r + 1, "B")
+        if r + 1 < R:
+            score_copies("B")
+            block_maxima(nothing)
+
+    QL, SL = "qx%d" % R, "sx%d" % R
+    state_quant(0, "A")
+    state_quant(0, "B")
+    late0()
+    score_copies("A")
+    score_copies("B")
+    key_copies("A")
+    block_maxima(lambda: quant(v("qo"), v("so"), v("Wt")))
+    for r in range(R):
+        order(r)
+        layer(r)
+    dma("S", lambda: T.oc[:, 0:4 * K], lambda: T[QL][:, 0:K].bitcast(dt.uint8), [], [v(QL, 0, K)])
+
+    def scales(q, k):
+        dma(q, lambda: T.osc[4 * k:4 * k + 4, 0:C], lambda: T[SL][32 * k:32 * k + 4, 0:C], [], [v(SL)])
+    for k in range(4):
+        scales("Y" if k < 2 else "S", k)
+    cp(v("yt", 0, K), bank(0, 0, K))
+    dma("Y", lambda: T.y[:, 0:K], lambda: T.yt[:, 0:K], [], [v("yt", 0, K)])
+
+    def line(o):
+        return ops[o]["q"] if ops[o]["sem"] is None else ops[o]["sem"]
+    known = {q: {} for q in list(queue) + ["-"]}
+    waited = set()
+    for me, op in enumerate(ops):
+        kn, need = known[op["q"]], {}
+        for o in op["deps"]:
+            if ops[o]["sem"] != "none":
+                need[line(o)] = max(need.get(line(o), -1), o)
+        op["waits"] = []
+        for o in sorted(need.values(), reverse=True):
+            if kn.get(line(o), -1) >= o:
+                continue
+            op["waits"].append(o)
+            waited.add(o)
+            kn[line(o)] = o
+            for l, x in ops[o]["knows"].items():
+                kn[l] = max(kn.get(l, -1), x)
+        op["knows"] = dict(kn)
+    count = {q: 0 for q in queue}
+    left = []
+    for me, op in enumerate(ops):
+        if op["q"] == "-":
+            continue
+        for o in op["waits"]:
+            w = ops[o]
+            queue[op["q"]].wait_ge(T.sem["s" + w["q"] if w["sem"] is None else w["sem"]], w["count"])
+        ins = op["fn"]()
+        if op["sem"] is None:
+            if me in waited:
+                count[op["q"]] += 1
+                op["count"] = count[op["q"]]
+                ins.then_inc(T.sem["s" + op["q"]], 1)
+        elif op["sem"] != "none":
+            ins.then_inc(T.sem[op["sem"]], 16)
+            if me not in waited:
+                left.append(op)
+    for op in left:
+        queue[op["q"]].wait_ge(T.sem[op["sem"]], 16)
+    g.wait_ge(T.sem.sent, sent[0])

@@ -1,41 +1,20 @@
-from concourse.mybir import dt, AluOpType, AxisListType, ActivationFunctionType
-
+from concourse.mybir import dt, AluOpType, ActivationFunctionType
 C, K, R = 448, 160, 3
 STEP = [1, 2, 1]
 F32, BF, I32, U16, U8, X4 = "float32", "bfloat16", "int32", "uint16", "uint8", "float8_e4m3fn_x4"
-BIG = 1e29
-TINY = 1e-32
-STEPK = 512.0
-BASE = 2048.0 * 480
-MAGIC = 1.5 * 2.0 ** 34
-
-_SB = {
-    "ut": (512, BF), "vt": (512, BF), "qu": (128, X4), "su": (128, U8), "qu2": (256, X4), "su2": (256, U8),
-    "qv": (128, X4), "sv": (128, U8), "qw": (512, X4), "sw": (512, U8),
-    "Et": (4 * C, BF), "qe": (C, X4), "se": (C, U8), "Rr": (4 * C, F32), "Dp": (4 * C, BF),
-    "pint": (2, I32), "iint": (2, I32), "pf": (2, F32), "fi": (2, F32), "fg": (2, F32), "ni": (2, F32), "kn": (2, F32),
-    "J": (464, F32), "J16": (C, BF), "Jg": (512, BF), "Jb": (128, BF), "oui": (16, I32), "ou": (16, U16),
-    "mask": (C, BF), "rs16": (112, BF), "tie": (112, F32), "tie2": (64, F32), "one": (464, BF),
-    "rsM": (C, BF), "dec": (C, F32), "r2": (C, F32), "zer": (512, BF), "ident": (128, BF),
-    "Wt": (512, BF), "qo": (128, X4), "so": (128, U8), "Ut": (2048, BF), "qd": (512, X4), "sd": (512, U8),
-    "Ms": (C, F32), "Mm": (112, F32), "own": (112, F32), "dd": (112, F32), "sg": (192, BF), "F1": (1024, BF), "F2": (1024, BF),
-    "qf": (256, X4), "sf": (256, U8), "sel1": (120, BF), "sel2": (104, BF), "Rp": (256, BF), "cap1": (256, BF),
-    "cap2": (256, F32), "off1": (2, U16), "off2": (2, U16), "Sp": (512, F32), "Kw": (456, F32), "Kp": (456, F32),
-    "Cd": (128, F32), "cc": (128, F32), "key": (32, F32), "kp": (32, F32), "H1": (40, F32), "W2": (32, F32),
-    "km": (32, F32), "ko": (32, F32), "LL": (64, F32), "dk": (64, F32), "FL": (64, F32), "PR": (64, F32), "turn": (24, F32),
-    "c1": (24, F32), "cod": (32, F32), "Pp": (2, F32), "off3": (2, U16), "Ww": (456, F32), "us": (C, F32),
-    "wr": (C, F32), "rr": (28, F32), "ya": (28, F32), "yb": (28, F32), "oo": (28, F32), "offo": (72, U16),
-    "olt": (C, F32), "yt": (C, F32),
-}
+BIG, TINY, STEPK, BASE, MAGIC = 1e29, 1e-32, 512.0, 2048.0 * 480, 1.5 * 2.0 ** 34
+_SB = {}
+for _d, _l in ((BF, "ut512 vt512 Et1792 Dp1792 Js448 Jg512 Jb128 mask448 rsa112 rsb64 one464 rsM448 zer512 ident128 Wt512 Ut2048 sg320 Fa1024 Fb1024 sela120 selb104 Rp256 capa256"),
+               (X4, "qu128 qup256 qv128 qw512 qe448 qo128 qd512 qf256"), (U8, "su128 sup256 sv128 sw512 se448 so128 sd512 sf256"),
+               (I32, "pint2 iint2 oui16"), (U16, "ou16 offa2 offb2 offc2 offo72"),
+               (F32, "Rr1792 pf2 fi2 fg2 ni2 kn2 J464 tie112 tieb64 dec448 rb448 Ms448 Mm128 own112 dd112 capb256 Sp512 Kw456 Kp456 Cd128 cc128 key32 kp32 Ha40 Wb32 km32 ko32 LL32 dk64 FL64 PR64 turn24 ca24 cod32 Pp64 Ww456 us448 wr448 rr28 ya28 oo28 olt448 yt448")):
+    for _w in _l.split():
+        _n = _w.rstrip("0123456789")
+        _SB[_n] = (int(_w[len(_n):]), _d)
 for _r in range(R + 1):
-    _SB["X%d" % _r] = (4 * C, BF)
-    _SB["qx%d" % _r] = (C, X4)
-    _SB["sx%d" % _r] = (C, U8)
+    _SB.update({"X%d" % _r: (4 * C, BF), "qx%d" % _r: (C, X4), "sx%d" % _r: (C, U8)})
 for _r in range(R):
-    _SB["lq%d" % _r] = (C, X4)
-    _SB["ls%d" % _r] = (C, U8)
-    _SB["lst%d" % _r] = (16, U16)
-    _SB["ord%d" % _r] = (28, U16)
+    _SB.update({"lq%d" % _r: (C, X4), "ls%d" % _r: (C, U8), "lst%d" % _r: (16, U16), "ord%d" % _r: (28, U16)})
 SCRATCH = {k: ("sbuf", [128, n], d) for k, (n, d) in _SB.items()}
 SCRATCH["ps"] = ("psum", [128, 4096], F32)
 SEMAPHORES = (["sV", "sS", "sP", "sG", "sent"] + ["dm%d" % i for i in range(20)]
@@ -69,12 +48,7 @@ def rank_program(g, core, T, topo):
     def bits(x):
         if x[0] == "ps":
             return 1 << (x[1] // 512)
-        if x[3] == 1:
-            return ((1 << (x[2] - x[1])) - 1) << x[1]
-        m = 0
-        for c in range(x[1], x[2], x[3]):
-            m |= 1 << c
-        return m
+        return sum(1 << c for c in range(x[1], x[2], x[3])) if x[3] > 1 else ((1 << (x[2] - x[1])) - 1) << x[1]
 
     def record(q, fn, outs, ins, sem=None, count=0):
         rd, wr = [], []
@@ -92,24 +66,15 @@ def rank_program(g, core, T, topo):
             for x in lst:
                 m = bits(x)
                 for (o, m2, w2) in acc.get(x[0], []):
-                    if not m & m2:
-                        continue
-                    if x[0] == "ps":
-                        if ops[o]["q"] != q:
-                            deps.add(o)
-                    elif w or w2:
+                    if m & m2 and (ops[o]["q"] != q if x[0] == "ps" else w or w2):
                         deps.add(o)
         for lst, w in ((rd, False), (wr, True)):
             for x in lst:
                 acc.setdefault(x[0], []).append((me, bits(x), w))
         ops.append({"q": q, "fn": fn, "deps": deps, "sem": sem, "count": count})
-        return me
 
-    def ts(o, i, s1, s2, op0, op1=None):
-        if op1 is None:
-            record("V", lambda: g.vector.tensor_scalar(ap(o), ap(i), ap(s1), None, op0), [o], [i, s1])
-        else:
-            record("V", lambda: g.vector.tensor_scalar(ap(o), ap(i), ap(s1), ap(s2), op0, op1), [o], [i, s1, s2])
+    def ts(o, i, s1, s2, *op):
+        record("V", lambda: g.vector.tensor_scalar(ap(o), ap(i), ap(s1), ap(s2), *op), [o], [i, s1, s2])
 
     def tt(o, a, b, op):
         record("V", lambda: g.vector.tensor_tensor(ap(o), ap(a), ap(b), op), [o], [a, b])
@@ -119,9 +84,6 @@ def rank_program(g, core, T, topo):
 
     def scan(o, d0, d1, init, op0, op1):
         record("V", lambda: g.vector.tensor_tensor_scan(ap(o), ap(d0), ap(d1), ap(init), op0, op1), [o], [d0, d1, init])
-
-    def red(o, i):
-        record("V", lambda: g.vector.tensor_reduce(ap(o), ap(i), AxisListType.X, A.add), [o], [i])
 
     def fill(o, c):
         record("V", lambda: g.vector.memset(ap(o), c), [o], [])
@@ -140,16 +102,13 @@ def rank_program(g, core, T, topo):
     def mm(o, wq, ws_, xq, xs, start=True, stop=True):
         record("P", lambda: g.tensor.matmul_mx(ap(o), ap(wq), ap(ws_), ap(xq), ap(xs), start, stop), [o], [wq, ws_, xq, xs])
 
-    def iota(o, pat, base, ch, small=False):
-        if small:
-            record("G", lambda: g.iota(ap(o), pat, base, ch, allow_small_or_imprecise_dtypes=True), [o], [])
-        else:
-            record("G", lambda: g.iota(ap(o), pat, base, ch), [o], [])
+    def iota(o, pat, ch=0):
+        kw = {} if _SB[o[0]][1] == I32 else {"allow_small_or_imprecise_dtypes": True}
+        record("G", lambda: g.iota(ap(o), pat, 0, ch, **kw), [o], [])
 
     def dma(q, out, in_, outs, ins):
-        s = "dm%d" % ndma[0]
         ndma[0] += 1
-        return record(q, lambda: queue[q].dma_start(out(), in_()), outs, ins, sem=s, count=16)
+        record(q, lambda: queue[q].dma_start(out(), in_()), outs, ins, sem="dm%d" % ndma[0], count=16)
 
     def partner(r):
         return T.cores[rank ^ STEP[r]]
@@ -157,8 +116,7 @@ def rank_program(g, core, T, topo):
     def remote(r, dst, src, sem, codes):
         p = partner(r)
         rid, pid, _ = topo.addr(p)
-        n = len(topo.engines(core, p))
-        sent[0] += n
+        sent[0] += len(topo.engines(core, p))
 
         def go():
             o, i = ap(dst), ap(src)
@@ -171,7 +129,6 @@ def rank_program(g, core, T, topo):
         record("-", None, outs, [], sem=sem, count=writes * len(topo.engines(partner(r), core)))
 
     PARTS = {"A": (K, C, 4), "B": (0, K, 0)}
-
     dma("S", lambda: T.ut[:], lambda: T.u[:], [v("ut")], [])
     dma("Y", lambda: T.X0[:, 4 * K:4 * C], lambda: T.x[:, 4 * K:4 * C], [v("X0", 4 * K, 4 * C)], [])
     dma("S", lambda: T.X0[:, 0:4 * K], lambda: T.x[:, 0:4 * K], [v("X0", 0, 4 * K)], [])
@@ -181,11 +138,12 @@ def rank_program(g, core, T, topo):
     for r in range(R):
         arrival(r, [v("lq%d" % r), v("ls%d" % r)], "arr%d" % r, 4)
         arrival(r, [v("lst%d" % r)], "lis%d" % r, 1)
-
-    iota(v("pint"), [[16, 2]], 0, 1)
-    iota(v("oui"), [[1, 2], [16, 8]], 0, 0)
-    iota(v("J16"), [[0, C // 16], [1, 16]], 0, 0, True)
-    iota(v("Jg"), [[16, 8], [0, 64]], 0, 0, True)
+    iota(v("pint"), [[16, 2]], 1)
+    iota(v("oui"), [[1, 2], [16, 8]])
+    iota(v("Js"), [[0, C // 16], [1, 16]])
+    iota(v("Jg"), [[16, 8], [0, 64]])
+    iota(v("Jb"), [[1, 128]])
+    iota(v("Fa", 512, 1024), [[0, 512]])
     fill(v("zer"), 0.0)
     fill(v("one"), 1.0)
     fill(v("rsM"), 0.0)
@@ -202,42 +160,20 @@ def rank_program(g, core, T, topo):
     tt(v("fg", 0, 1), v("pf", 0, 1), v("fi", 0, 1), A.subtract)
     cp(v("ou"), v("oui"))
     ts(v("kn"), v("ni"), 1.0, STEPK, A.add, A.mult)
-    fill(v("F1"), 0.0)
-    ts(v("mask"), v("J16"), v("fi", 0, 1), None, A.is_equal)
+    ts(v("tie"), v("Js", 0, 112), v("fi", 0, 1), -TINY, A.is_gt, A.mult)
+    cp(v("Rp", 0, 129, 128), v("kn"))
+    ts(v("mask"), v("Js"), v("fi", 0, 1), None, A.is_equal)
+    ts(v("Wt"), v("Jg"), v("fg", 0, 1), None, A.is_equal)
     for b in range(4):
         act(v("Ut", 513 * b, 512 * b + 512, 4), v("ident"), ACT.Copy)
     quant(v("qu"), v("su"), v("ut"))
-    ts(v("rs16"), v("J16", 0, 112), 0.0, None, A.not_equal)
-    record("V", lambda: g.vector.tensor_copy(T.qu2[:, 0:256].bitcast(dt.uint32), T.qu[:, 0:128].bitcast(dt.uint32).indirect(T.ou[:, 0:16])),
-           [v("qu2")], [v("qu"), v("ou")])
-    act(v("su2"), ind(v("su"), v("ou")), ACT.Copy)
+    ts(v("rsa"), v("Js", 0, 112), 0.0, None, A.not_equal)
+    record("V", lambda: g.vector.tensor_copy(T.qup[:, 0:256].bitcast(dt.uint32), T.qu[:, 0:128].bitcast(dt.uint32).indirect(T.ou[:, 0:16])),
+           [v("qup")], [v("qu"), v("ou")])
+    act(v("sup"), ind(v("su"), v("ou")), ACT.Copy)
+    act(v("Fa", 0, 512), v("zer"), ACT.Copy)
     for h in range(2):
-        act(v("F2", 512 * h, 512 * h + 512), v("zer"), ACT.Copy)
-
-    def late0():
-        ts(v("Wt"), v("Jg"), v("fg", 0, 1), None, A.is_equal)
-        fill(v("Sp", 0, 1), BIG)
-        ts(v("tie"), v("J16", 0, 112), v("fi", 0, 1), -TINY, A.is_gt, A.mult)
-
-    def late1():
-        fill(v("sel1", 112, 120), -STEPK)
-        cp(v("Jb"), v("J", 0, 128))
-        cp(v("Rp", 0, 129, 128), v("kn"))
-        fill(v("sel2", 96, 104), -STEPK)
-        fill(v("H1", 32, 33), BASE + 456.0)
-        for e in range(4):
-            act(v("Sp", 128 * e + 112, 128 * e + 120), v("zer", 0, 8), ACT.Copy)
-        act(v("Kw", C, 456), v("zer", 0, 8), ACT.Identity, bias=-BIG)
-        act(v("Kp", 0, 1), v("zer", 0, 1), ACT.Copy)
-        act(v("Kp", C + 1, 456), v("zer", 0, 7), ACT.Copy)
-        act(v("cod", 24, 32), v("zer", 0, 8), ACT.Copy)
-
-    def late2():
-        quant(v("qd"), v("sd"), v("Ut"))
-        for q in range(2):
-            ts(v("tie2", 32 * q, 32 * q + 32), v("J", 0, 32), v("ni", q, q + 1), -TINY, A.is_lt, A.mult)
-        act(v("dec"), v("zer", 0, C), ACT.Identity, bias=-2047.0)
-        act(v("r2"), v("mask"), ACT.Identity, bias=-2048.0, scale=4194304.0)
+        act(v("Fb", 512 * h, 512 * h + 512), v("zer"), ACT.Copy)
 
     def state_quant(r, part):
         a, b, k = PARTS[part]
@@ -247,7 +183,7 @@ def rank_program(g, core, T, topo):
             remote(r, v("lq%d" % r, a, b), qx, "arr%d" % r, True)
             remote(r, v("ls%d" % r, a, b), sx, "arr%d" % r, False)
             for j, c in ((0, 0), (1, 0), (2, 128)):
-                mm(bank(k + j, 0, b - a), v("qu2", c, c + 128), v("su2", c, c + 128), qx, sx)
+                mm(bank(k + j, 0, b - a), v("qup", c, c + 128), v("sup", c, c + 128), qx, sx)
         else:
             mm(bank(k, 0, b - a), v("qv"), v("sv"), qx, sx)
 
@@ -267,25 +203,22 @@ def rank_program(g, core, T, topo):
         act(v("Kp", a + 1, b + 1), bank(k + 2, 0, b - a), ACT.Copy)
 
     def part_of(src, c0, c1):
-        name, a0, s0 = src
-        return (name, a0 + s0 * c0, a0 + s0 * (c1 - 1) + 1, s0)
+        return (src[0], src[1] + src[2] * c0, src[1] + src[2] * (c1 - 1) + 1, src[2])
 
-    def masked(src, c0, c1):
-        tt(v("Mm", c0, c1), part_of(src, c0, c1), v("mask", c0, c1), A.mult)
+    def masked(c0, c1):
+        tt(v("Mm", c0, c1), part_of(BLOCKS, c0, c1), v("mask", c0, c1), A.mult)
 
     def owned(c0, c1):
-        scan(v("own", c0, c1), v("rs16", c0, c1), v("Mm", c0, c1), 0.0, A.mult, A.add)
+        scan(v("own", c0, c1), v("rsa", c0, c1), v("Mm", c0, c1), 0.0, A.mult, A.add)
 
     BLOCKS, COLUMNS = ("Ms", 3, 4), ("Cd", 0, 1)
 
-    def block_maxima(between):
+    def block_maxima():
         maxima("A")
-        between()
-        masked(BLOCKS, 48, 112)
+        masked(48, 112)
         maxima("B")
         owned(48, 112)
-        masked(BLOCKS, 0, 48)
-        owned(0, 48)
+        masked(0, 48)
 
     def select(src, nq, F, sel, w, vals, cap, off, gap):
         n = 16 * nq
@@ -298,15 +231,29 @@ def rank_program(g, core, T, topo):
 
         def me(q):
             return v("own", 16 * q + 15, 16 * q + 16)
-        for q in reversed(range(nq)):
+
+        def flags(q):
+            if q > 0:
+                ts(slot(q, 0, 16 * q), part_of(src, 0, 16 * q), me(q), None, A.is_lt)
+            if q < nq - 1:
+                ts(slot(q, 16 * q + 16, n), part_of(src, 16 * q + 16, n), me(q), None, A.is_le)
+
+        def diff(q):
             act(v("dd", 16 * q, 16 * q + 16), part_of(src, 16 * q, 16 * q + 16), ACT.Identity, bias=me(q), scale=-1.0)
-        act(v("sg", 0, n - 16), part_of(src, 16, n), ACT.Sign, bias=me(0), scale=-1.0)
-        act(v("sg", 96, 96 + n - 16), part_of(src, 0, n - 16), ACT.Sign, bias=me(nq - 1), scale=-1.0)
-        act(slot(0, 16, n), v("sg", 0, n - 16), ACT.Sign, bias=1.0)
-        act(slot(nq - 1, 0, n - 16), v("sg", 96, 96 + n - 16), ACT.Relu)
-        for q in (3, 4, 1, 2, 5)[:nq - 2]:
-            ts(slot(q, 0, 16 * q), part_of(src, 0, 16 * q), me(q), None, A.is_lt)
-            ts(slot(q, 16 * q + 16, n), part_of(src, 16 * q + 16, n), me(q), None, A.is_le)
+        if nq == 7:
+            for q in (6, 5, 4, 3):
+                diff(q)
+            act(v("sg", 192, 192 + n), part_of(src, 0, n), ACT.Sign, bias=me(5), scale=-1.0)
+            act(v("sg", 96, 96 + n - 16), part_of(src, 0, n - 16), ACT.Sign, bias=me(6), scale=-1.0)
+            flags(3)
+            owned(0, 48)
+            act(slot(5, 0, 80), v("sg", 192, 272), ACT.Relu)
+            act(slot(5, 96, n), v("sg", 288, 304), ACT.Sign, bias=1.0)
+            act(slot(6, 0, n - 16), v("sg", 96, 96 + n - 16), ACT.Relu)
+        for q in range(3 if nq == 7 else nq):
+            diff(q)
+        for q in ((4, 1, 2, 0) if nq == 7 else (1, 2, 3, 4, 0, 5)):
+            flags(q)
         tt(slot("tie", 0, n), v("dd", 0, n), v("tie", 0, n), A.is_gt)
         for h in range(2):
             quant(v("qf", 128 * h, 128 * h + 128), v("sf", 128 * h, 128 * h + 128), v(F, 512 * h, 512 * h + 512))
@@ -321,76 +268,80 @@ def rank_program(g, core, T, topo):
 
     def order(r):
         def gap1():
-            key_copies("B")
+            score_copies("B")
             if r == 0:
-                late1()
+                quant(v("qd"), v("sd"), v("Ut"))
+                for e in range(4):
+                    act(v("Sp", 128 * e + 112, 128 * e + 120), v("zer", 0, 8), ACT.Copy)
+            key_copies("B")
 
         def gap2():
+            for e in range(4):
+                act(v("cc", e, 128, 4), ind(v("J", 0, 128), v("offa")), ACT.Identity, bias=float(e), scale=4.0)
             if r == 0:
-                late2()
+                key_copies("A")
+                fill(v("selb", 96, 104), -STEPK)
+                fill(v("Ha", 32, 33), BASE + 456.0)
+                for q in range(2):
+                    ts(v("tieb", 32 * q, 32 * q + 32), v("J", 0, 32), v("ni", q, q + 1), -TINY, A.is_lt, A.mult)
+                ts(v("rsb"), v("J", 0, 64), 32.0, None, A.not_equal)
+                act(v("Kw", C, 456), v("zer", 0, 8), ACT.Identity, bias=-BIG)
+                act(v("Kp", 0, 1), v("zer", 0, 1), ACT.Copy)
+                act(v("Kp", C + 1, 456), v("zer", 0, 7), ACT.Copy)
             act(v("Ww"), v("zer", 0, 456), ACT.Copy)
             for b in range(4):
                 mm(bank(4 + b, 0, C), v("qd", 128 * b, 128 * b + 128), v("sd", 128 * b, 128 * b + 128), v("lq%d" % r), v("ls%d" % r))
-        select(BLOCKS, 7, "F1", "sel1", 120, "Jb", "cap1", "off1", gap1)
+        select(BLOCKS, 7, "Fa", "sela", 120, "Jb", "capa", "offa", gap1)
         for e in range(4):
-            o, i = v("Cd", e, 128, 4), ind(v("Sp", 128 * e, 128 * e + 120), v("off1"))
-            if e < 2:
-                cp(o, i)
-            else:
-                act(o, i, ACT.Copy)
-        for e in range(4):
-            act(v("cc", e, 128, 4), ind(v("J", 0, 128), v("off1")), ACT.Identity, bias=float(e), scale=4.0)
-        masked(COLUMNS, 0, 96)
+            i = ind(v("Sp", 128 * e, 128 * e + 120), v("offa"))
+            tt(v("Mm", e, 128, 4), i, v("mask", e, 128, 4), A.mult)
+            act(v("Cd", e, 128, 4), i, ACT.Copy)
         owned(0, 96)
-        select(COLUMNS, 6, "F2", "sel2", 104, "cc", "cap2", "off2", gap2)
-        cp(v("key"), ind(v("Kw"), v("off2")))
-        act(v("H1", 0, 32), ind(v("J"), v("off2")), ACT.Identity, bias=BASE)
-        act(v("kp"), ind(v("Kp"), v("off2")), ACT.Copy)
-        act(v("W2"), ind(v("J"), v("off2")), ACT.Identity, bias=BASE + 2049.0, scale=-1.0)
+        select(COLUMNS, 6, "Fb", "selb", 104, "cc", "capb", "offb", gap2)
+        tt(v("km"), ind(v("Kw"), v("offb")), v("mask", 0, 32), A.mult)
+        cp(v("key"), ind(v("Kw"), v("offb")))
+        act(v("Ha", 0, 32), ind(v("J"), v("offb")), ACT.Identity, bias=BASE)
+        act(v("kp"), ind(v("Kp"), v("offb")), ACT.Copy)
+        act(v("Wb"), ind(v("J"), v("offb")), ACT.Identity, bias=BASE + 2049.0, scale=-1.0)
+        if r == 0:
+            act(v("cod", 24, 32), v("zer", 0, 8), ACT.Copy)
+            act(v("dec"), v("zer", 0, C), ACT.Identity, bias=-2047.0)
+            act(v("rb"), v("mask"), ACT.Identity, bias=-2048.0, scale=4194304.0)
         for b in range(4):
             act(v("Dp", C * b, C * b + C), bank(4 + b, 0, C), ACT.Copy)
-        tt(v("km"), v("key"), v("mask", 0, 32), A.mult)
-        tt(v("LL", 0, 32), v("H1", 1, 33), v("H1", 0, 32), A.subtract)
-        scan(v("ko"), v("rs16", 0, 32), v("km"), 0.0, A.mult, A.add)
-        tt(v("LL", 32, 64), v("H1", 1, 33), v("H1", 0, 32), A.subtract)
+        scan(v("ko"), v("rsa", 0, 32), v("km"), 0.0, A.mult, A.add)
+        tt(v("LL"), v("Ha", 1, 33), v("Ha", 0, 32), A.subtract)
         for q in range(2):
             ts(v("dk", 32 * q, 32 * q + 32), v("key"), v("ko", 16 * q + 15, 16 * q + 16), None, A.subtract)
         tt(v("turn"), v("key", 0, 24), v("kp", 1, 25), A.is_lt)
-        tt(v("FL"), v("dk"), v("tie2"), A.is_gt)
-        tt(v("c1"), v("turn"), v("W2", 1, 25), A.mult)
-        tt(v("PR"), v("FL"), v("LL"), A.mult)
-        tt(v("cod", 0, 24), v("c1"), v("H1", 0, 24), A.max)
+        tt(v("FL"), v("dk"), v("tieb"), A.is_gt)
+        tt(v("ca"), v("turn"), v("Wb", 1, 25), A.mult)
         for q in range(2):
-            red(v("Pp", q, q + 1), v("PR", 32 * q, 32 * q + 32))
-        cp(v("off3"), v("Pp"))
-        cp(ind(v("Ww"), v("off3")), v("cod"))
+            tt(v("PR", 32 * q, 32 * q + 32), v("FL", 32 * q, 32 * q + 32), v("LL"), A.mult)
+        tt(v("cod", 0, 24), v("ca"), v("Ha", 0, 24), A.max)
+        scan(v("Pp"), v("rsb"), v("PR"), 0.0, A.mult, A.add)
+        cp(v("offc"), v("Pp", 31, 64, 32))
+        cp(ind(v("Ww"), v("offc")), v("cod"))
         scan(v("us"), v("dec"), v("Ww", 0, C), 0.0, A.add, A.max)
-        scan(v("wr"), v("r2"), v("us"), 0.0, A.add, A.min)
+        scan(v("wr"), v("rb"), v("us"), 0.0, A.add, A.min)
         w = v("wr", 15, C, 16)
         ts(v("rr"), w, MAGIC, MAGIC, A.add, A.subtract)
         tt(v("ya"), w, v("rr"), A.subtract)
-        tt(v("yb"), v("rr"), w, A.subtract)
-        tt(v("oo"), v("ya"), v("yb"), A.max)
+        act(v("oo"), v("ya"), ACT.Abs)
         cp(v("ord%d" % r), v("oo"))
         remote(r, v("lst%d" % r, 0, 10), v("ord%d" % r, 0, 10), "lis%d" % r, False)
-        for t in (2, 3, 0, 1):
+        for t in (2, 0, 3, 1):
             ts(v("offo", 18 * t, 18 * t + 18), v("oo", 10, 28), 4.0, float(t), A.mult, A.add)
-
-    def nothing():
-        pass
 
     def layer(r):
         X, Y = "X%d" % r, "X%d" % (r + 1)
         runs = ((K, K + 128, 0), (K + 128, C, 4), (0, K, 0))
 
-        def gather(a, b):
-            for t in (2, 0, 3, 1):
-                m = 18 * t + (a - K) // 16
-                o, i = v("Et", 4 * a + t, 4 * b, 4), ind(v(X), v("offo", m, m + (b - a) // 16))
-                if t < 2:
-                    cp(o, i)
-                else:
-                    act(o, i, ACT.Copy)
+        def move(o, i, on_vector):
+            if on_vector:
+                cp(o, i)
+            else:
+                act(o, i, ACT.Copy)
 
         def product(a, b, k):
             quant(v("qe", a, b), v("se", a, b), v("Et", 4 * a, 4 * b))
@@ -401,20 +352,22 @@ def rank_program(g, core, T, topo):
             for j in range(4):
                 act(v("Rr", C * j + a, C * j + b), bank(k + j, 0, b - a), ACT.Relu, scale=0.015625)
 
-        def add(a, b):
-            for j in range(4):
+        def add(a, b, js=range(4)):
+            for j in js:
                 tt(v(Y, 4 * a + j, 4 * b, 4), v("Et", 4 * a + j, 4 * b, 4), v("Rr", C * j + a, C * j + b), A.add)
         for a, b, k in runs[:2]:
-            gather(a, b)
+            for t in (2, 0, 3, 1):
+                m = 18 * t + (a - K) // 16
+                move(v("Et", 4 * a + t, 4 * b, 4), ind(v(X), v("offo", m, m + (b - a) // 16)), t < 2)
             product(a, b, k)
-        if r == R - 1:
-            quant(v("qv"), v("sv"), v("vt"))
-        for a, b, k in runs[:2]:
-            relu(a, b, k)
-            add(a, b)
+        relu(*runs[0])
+        add(K, K + 128)
+        relu(*runs[1])
+        add(K + 128, C, range(3))
         for t in range(4):
-            act(v("Et", t, 4 * K, 4), ind(v("Dp", C * t, C * t + C), v("lst%d" % r, 0, 10)), ACT.Copy)
+            move(v("Et", t, 4 * K, 4), ind(v("Dp", C * t, C * t + C), v("lst%d" % r, 0, 10)), t < 1)
         product(*runs[2])
+        add(K + 128, C, range(3, 4))
         state_quant(r + 1, "A")
         relu(*runs[2])
         if r + 1 < R:
@@ -428,18 +381,19 @@ def rank_program(g, core, T, topo):
             dma("Y", lambda: T.ol[:], lambda: T.olt[0:128:16, :], [], [v("olt")])
         add(0, K)
         state_quant(r + 1, "B")
+        if r == R - 2:
+            quant(v("qv"), v("sv"), v("vt"))
         if r + 1 < R:
-            score_copies("B")
-            block_maxima(nothing)
+            block_maxima()
 
     QL, SL = "qx%d" % R, "sx%d" % R
     state_quant(0, "A")
     state_quant(0, "B")
-    late0()
+    fill(v("Sp", 0, 1), BIG)
+    fill(v("sela", 112, 120), -STEPK)
+    quant(v("qo"), v("so"), v("Wt"))
     score_copies("A")
-    score_copies("B")
-    key_copies("A")
-    block_maxima(lambda: quant(v("qo"), v("so"), v("Wt")))
+    block_maxima()
     for r in range(R):
         order(r)
         layer(r)
@@ -448,7 +402,7 @@ def rank_program(g, core, T, topo):
     def scales(q, k):
         dma(q, lambda: T.osc[4 * k:4 * k + 4, 0:C], lambda: T[SL][32 * k:32 * k + 4, 0:C], [], [v(SL)])
     for k in range(4):
-        scales("Y" if k < 2 else "S", k)
+        scales("Y" if k < 1 else "S", k)
     cp(v("yt", 0, K), bank(0, 0, K))
     dma("Y", lambda: T.y[:, 0:K], lambda: T.yt[:, 0:K], [], [v("yt", 0, K)])
 

@@ -2,23 +2,30 @@ from concourse.mybir import dt, AluOpType, ActivationFunctionType
 C, K, R = 448, 160, 3
 STEP = [1, 2, 1]
 F32, BF, I32, U16, U8, X4 = "float32", "bfloat16", "int32", "uint16", "uint8", "float8_e4m3fn_x4"
-BIG, TINY, STEPK, BASE, MAGIC = 1e29, 1e-32, 512.0, 2048.0 * 480, 1.5 * 2.0 ** 34
+BIG, TINY, STEPK, TURN, MID = 1e29, 1e-32, 512.0, 1024.0, 228.0
+W = 456
 _SB = {}
-for _d, _l in ((BF, "ut512 vt512 Et1792 Dp1792 Js448 Jg512 Jb128 mask448 rsa112 rsb64 one464 rsM448 zer512 ident128 Wt512 Ut2048 sg320 Fa1024 Fb1024 sela120 selb104 Rp256 capa256"),
+for _d, _l in ((BF, "ut512 vt512 Et1792 Dp1792 Js128 Jg512 Jb128 mask128 rsa112 rsb49 one464 rsM448 zer512 ident128 Wt512 Ut2048 sg448 "
+                    "Fa1024 Fb1024 sela120 selb104 Rp256 cap256 cc128 rb448 dd112 tie112 dk48 tieb48"),
                (X4, "qu128 qup256 qv128 qw512 qe448 qo128 qd512 qf256"), (U8, "su128 sup256 sv128 sw512 se448 so128 sd512 sf256"),
-               (I32, "pint2 iint2 oui16"), (U16, "ou16 offa2 offb2 offc2 offo72"),
-               (F32, "Rr1792 pf2 fi2 fg2 ni2 kn2 J464 tie112 tieb64 dec448 rb448 Ms448 Mm128 own112 dd112 capb256 Sp512 Kw456 Kp456 Cd128 cc128 key32 kp32 Ha40 Wb32 km32 ko32 LL32 dk64 FL64 PR64 turn24 ca24 cod32 Pp64 Ww456 us448 wr448 rr28 ya28 oo28 olt448 yt448")):
+               (I32, "pint2 iint4 oui16"), (U16, "ou16 offa2 offb2 offp2 offc4"),
+               (F32, "Rr1792 pf2 fi4 fg2 ni2 kn2 r4a4 r4b4 r4c4 ab2 J464 Ms448 Mm128 own112 Sp512 Kw456 Cd128 key32 kp32 Ha32 Wb32 km32 ko32 "
+                     "LL48 FL48 PR49 turn24 ca24 cod64 Pp49 Ww912 us448 wr448 oo112 ola448 olt448 yt448")):
     for _w in _l.split():
         _n = _w.rstrip("0123456789")
         _SB[_n] = (int(_w[len(_n):]), _d)
 for _r in range(R + 1):
     _SB.update({"X%d" % _r: (4 * C, BF), "qx%d" % _r: (C, X4), "sx%d" % _r: (C, U8)})
 for _r in range(R):
-    _SB.update({"lq%d" % _r: (C, X4), "ls%d" % _r: (C, U8), "lst%d" % _r: (16, U16), "ord%d" % _r: (28, U16)})
+    _SB.update({"lq%d" % _r: (C, X4), "ls%d" % _r: (C, U8), "lst%d" % _r: (K // 4, U16), "ord%d" % _r: (C // 4, U16)})
 SCRATCH = {k: ("sbuf", [128, n], d) for k, (n, d) in _SB.items()}
 SCRATCH["ps"] = ("psum", [128, 4096], F32)
 SEMAPHORES = (["sV", "sS", "sP", "sG", "sent"] + ["dm%d" % i for i in range(20)]
               + ["arr%d" % r for r in range(R)] + ["lis%d" % r for r in range(R)])
+CYCLE, WAIT, LOAD, LIST, CODES = 0.85e-3, 0.19, 2.0, 1.8, 5.5
+OPT = {"g": (64, 56, 48),
+       "V": "g0 q0 g1 q1 a00 a01 a02 a03 g2 a10 q2 a11 a12 a13 a20 qA a21 a22 a23 mA qB",
+       "S": "G0 G1 R00 R01 R02 R03 G2 R10 R11 R12 R13 R20 R21 R22 R23", "sa": (5, 6), "sb": (), "wait": WAIT, "list": LIST, "codes": CODES, "usplit": 0, "passes": 3, "wr": (2, 0, 1)}
 
 
 def rank_program(g, core, T, topo):
@@ -27,7 +34,7 @@ def rank_program(g, core, T, topo):
         return
     A, ACT = AluOpType, ActivationFunctionType
     queue = {"V": g.vector, "S": g.scalar, "P": g.tensor, "G": g, "Y": g.sync}
-    ops, acc, ndma, sent = [], {}, [0], [0]
+    ops, acc, ndma, sent, writes, rows = [], {}, [0], [0], {}, {}
 
     def v(name, a=0, b=None, s=1):
         return (name, a, _SB[name][0] if b is None else b, s)
@@ -45,12 +52,25 @@ def rank_program(g, core, T, topo):
             return ap(x[1]).indirect(ap(x[2]))
         return T[x[0]][:, x[1]:x[2]] if x[3] == 1 else T[x[0]][:, x[1]:x[2]:x[3]]
 
+    def size(x):
+        return 16 * size(x[2]) if x[0] == "@" else len(range(x[1], x[2], x[3]))
+
     def bits(x):
         if x[0] == "ps":
             return 1 << (x[1] // 512)
         return sum(1 << c for c in range(x[1], x[2], x[3])) if x[3] > 1 else ((1 << (x[2] - x[1])) - 1) << x[1]
 
-    def record(q, fn, outs, ins, sem=None, count=0):
+    def cycles(o, ins, per=None):
+        views = [x for x in [o] + ins if isinstance(x, tuple)]
+        if o[0] == "@":
+            return 60 + 4 * size(o)
+        if any(x[0] == "@" for x in views):
+            return 70 + 1.5 * size(o)
+        if per is None:
+            per = 0.5 if all(x[0] != "ps" and _SB[x[0]][1] in (BF, U16) for x in views) else 1
+        return max(64, per * size(o))
+
+    def record(q, fn, outs, ins, hold, sem=None, count=0, done=None, after=()):
         rd, wr = [], []
         for x in ins:
             if isinstance(x, tuple):
@@ -61,35 +81,44 @@ def rank_program(g, core, T, topo):
                 rd.append(x[2])
             else:
                 wr.append(x)
-        me, deps = len(ops), set()
+        me, deps, behind = len(ops), set(), set(after)
         for lst, w in ((rd, False), (wr, True)):
             for x in lst:
                 m = bits(x)
                 for (o, m2, w2) in acc.get(x[0], []):
-                    if m & m2 and (ops[o]["q"] != q if x[0] == "ps" else w or w2):
-                        deps.add(o)
+                    if m & m2:
+                        if ops[o]["q"] != q if x[0] == "ps" else w or w2:
+                            deps.add(o)
+                        elif w:
+                            behind.add(o)
         for lst, w in ((rd, False), (wr, True)):
             for x in lst:
                 acc.setdefault(x[0], []).append((me, bits(x), w))
-        ops.append({"q": q, "fn": fn, "deps": deps, "sem": sem, "count": count})
+        ops.append({"q": q, "fn": fn, "deps": deps, "behind": behind, "sem": sem, "count": count, "hold": hold * CYCLE,
+                    "done": hold * CYCLE if done is None else done})
+
+    def row(name):
+        if name in rows:
+            ops[-1]["behind"].add(rows[name])
+        rows[name] = len(ops) - 1
 
     def ts(o, i, s1, s2, *op):
-        record("V", lambda: g.vector.tensor_scalar(ap(o), ap(i), ap(s1), ap(s2), *op), [o], [i, s1, s2])
+        record("V", lambda: g.vector.tensor_scalar(ap(o), ap(i), ap(s1), ap(s2), *op), [o], [i, s1, s2], cycles(o, [i, s1, s2]))
 
     def tt(o, a, b, op):
-        record("V", lambda: g.vector.tensor_tensor(ap(o), ap(a), ap(b), op), [o], [a, b])
+        record("V", lambda: g.vector.tensor_tensor(ap(o), ap(a), ap(b), op), [o], [a, b], cycles(o, [a, b], 2))
 
     def cp(o, i):
-        record("V", lambda: g.vector.tensor_copy(ap(o), ap(i)), [o], [i])
+        record("V", lambda: g.vector.tensor_copy(ap(o), ap(i)), [o], [i], cycles(o, [i]))
 
     def scan(o, d0, d1, init, op0, op1):
-        record("V", lambda: g.vector.tensor_tensor_scan(ap(o), ap(d0), ap(d1), ap(init), op0, op1), [o], [d0, d1, init])
+        record("V", lambda: g.vector.tensor_tensor_scan(ap(o), ap(d0), ap(d1), ap(init), op0, op1), [o], [d0, d1, init], cycles(o, [d0, d1]))
 
     def fill(o, c):
-        record("V", lambda: g.vector.memset(ap(o), c), [o], [])
+        record("V", lambda: g.vector.memset(ap(o), c), [o], [], cycles(o, []))
 
     def quant(q, s, i):
-        record("V", lambda: g.vector.quantize_mx(ap(q), ap(s), ap(i)), [q, s], [i])
+        record("V", lambda: g.vector.quantize_mx(ap(q), ap(s), ap(i)), [q, s], [i], 15 + size(q))
 
     def act(o, i, f, bias=None, scale=None):
         kw = {}
@@ -97,23 +126,26 @@ def rank_program(g, core, T, topo):
             kw["bias"] = ap(bias)
         if scale is not None:
             kw["scale"] = scale
-        record("S", lambda: g.scalar.activation(ap(o), ap(i), f, **kw), [o], [i, bias])
+        record("S", lambda: g.scalar.activation(ap(o), ap(i), f, **kw), [o], [i, bias], cycles(o, [i], 1))
+
+    def sfill(o, c):
+        act(o, v("zer", 0, size(o)), ACT.Identity, bias=c)
 
     def mm(o, wq, ws_, xq, xs, start=True, stop=True):
-        record("P", lambda: g.tensor.matmul_mx(ap(o), ap(wq), ap(ws_), ap(xq), ap(xs), start, stop), [o], [wq, ws_, xq, xs])
+        record("P", lambda: g.tensor.matmul_mx(ap(o), ap(wq), ap(ws_), ap(xq), ap(xs), start, stop), [o], [wq, ws_, xq, xs], 16 + size(o))
 
     def iota(o, pat, ch=0):
         kw = {} if _SB[o[0]][1] == I32 else {"allow_small_or_imprecise_dtypes": True}
-        record("G", lambda: g.iota(ap(o), pat, 0, ch, **kw), [o], [])
+        record("G", lambda: g.iota(ap(o), pat, 0, ch, **kw), [o], [], 160 + 2 * size(o))
 
-    def dma(q, out, in_, outs, ins):
+    def dma(q, out, in_, outs, ins, done=LOAD):
         ndma[0] += 1
-        record(q, lambda: queue[q].dma_start(out(), in_()), outs, ins, sem="dm%d" % ndma[0], count=16)
+        record(q, lambda: queue[q].dma_start(out(), in_()), outs, ins, 60, sem="dm%d" % ndma[0], count=16, done=done)
 
     def partner(r):
         return T.cores[rank ^ STEP[r]]
 
-    def remote(r, dst, src, sem, codes):
+    def remote(r, dst, src, sem, codes, done):
         p = partner(r)
         rid, pid, _ = topo.addr(p)
         sent[0] += len(topo.engines(core, p))
@@ -123,311 +155,330 @@ def rank_program(g, core, T, topo):
             if codes:
                 o, i = o.bitcast(dt.uint8), i.bitcast(dt.uint8)
             g.remote_dma(o, i, T.sem[sem], T.sem.sent, pid, rid, topo.mask(core, p))
-        record("G", go, [], [src], sem="none")
+        writes.setdefault(sem, []).append(len(ops))
+        record("G", go, [], [src], 300, sem="none", done=done)
 
-    def arrival(r, outs, sem, writes):
-        record("-", None, outs, [], sem=sem, count=writes * len(topo.engines(partner(r), core)))
+    def arrival(r, outs, sem):
+        record("-", None, outs, [], 0, sem=sem, count=len(writes[sem]) * len(topo.engines(partner(r), core)), after=writes[sem])
 
     PARTS = {"A": (K, C, 4), "B": (0, K, 0)}
     dma("S", lambda: T.ut[:], lambda: T.u[:], [v("ut")], [])
-    dma("Y", lambda: T.X0[:, 4 * K:4 * C], lambda: T.x[:, 4 * K:4 * C], [v("X0", 4 * K, 4 * C)], [])
-    dma("S", lambda: T.X0[:, 0:4 * K], lambda: T.x[:, 0:4 * K], [v("X0", 0, 4 * K)], [])
+    dma("Y", lambda: T.X0[:, 4 * K:4 * C], lambda: T.x[:, 4 * K:4 * C], [v("X0", 4 * K, 4 * C)], [], LOAD + 0.6)
+    dma("S", lambda: T.X0[:, 0:4 * K], lambda: T.x[:, 0:4 * K], [v("X0", 0, 4 * K)], [], LOAD + 1.0)
+    ops[2]["behind"].add(0)
     dma("Y", lambda: T.qw[:].bitcast(dt.uint8), lambda: T.wc[:], [v("qw")], [v("X0")])
-    dma("Y", lambda: T.sw[:], lambda: T.ws[:], [v("sw")], [])
-    dma("Y", lambda: T.vt[:], lambda: T.v[:], [v("vt")], [])
-    for r in range(R):
-        arrival(r, [v("lq%d" % r), v("ls%d" % r)], "arr%d" % r, 4)
-        arrival(r, [v("lst%d" % r)], "lis%d" % r, 1)
+    dma("Y", lambda: T.sw[:], lambda: T.ws[:], [v("sw")], [v("X0")])
+    dma("Y", lambda: T.vt[:], lambda: T.v[:], [v("vt")], [v("X0")])
     iota(v("pint"), [[16, 2]], 1)
     iota(v("oui"), [[1, 2], [16, 8]])
-    iota(v("Js"), [[0, C // 16], [1, 16]])
+    iota(v("Js"), [[0, 8], [1, 16]])
     iota(v("Jg"), [[16, 8], [0, 64]])
-    iota(v("Jb"), [[1, 128]])
-    iota(v("Fa", 512, 1024), [[0, 512]])
-    fill(v("zer"), 0.0)
+    for z in ("zer", "rsM", "Ut", "Fa", "Fb"):
+        for c in range(0, _SB[z][0], 512):
+            if z in ("Ut", "Fb"):
+                act(v(z, c, c + 512), v("zer"), ACT.Copy)
+            else:
+                fill(v(z, c, min(c + 512, _SB[z][0])), 0.0)
     fill(v("one"), 1.0)
-    fill(v("rsM"), 0.0)
-    for b in range(4):
-        act(v("Ut", 512 * b, 512 * b + 512), v("zer"), ACT.Copy)
-    ts(v("iint", 0, 1), v("pint", 0, 1), 15, None, A.bitwise_and)
-    cp(v("pf", 0, 1), v("pint", 0, 1))
-    scan(v("J"), v("one"), v("zer", 0, 464), -1.0, A.add, A.add)
-    cp(v("fi", 0, 1), v("iint", 0, 1))
     fill(v("rsM", 4, C, 4), -4 * BIG)
+    scan(v("J"), v("one"), v("zer", 0, 464), -1.0, A.add, A.add)
+    act(v("Jb"), v("J", 0, 128), ACT.Copy)
+    ts(v("iint", 0, 1), v("pint", 0, 1), 15, None, A.bitwise_and)
+    ts(v("iint", 1, 2), v("pint", 0, 1), 3, None, A.bitwise_and)
+    ts(v("iint", 2, 3), v("pint", 0, 1), 12, 2, A.bitwise_and, A.logical_shift_right)
+    cp(v("pf", 0, 1), v("pint", 0, 1))
+    cp(v("fi", 0, 3), v("iint", 0, 3))
+    P16, P4, PQ = v("fi", 0, 1), v("fi", 1, 2), v("fi", 2, 3)
     ts(v("ident"), v("J", 0, 128), v("pf", 0, 1), None, A.is_equal)
     for q in range(2):
-        ts(v("ni", q, q + 1), v("fi", 0, 1), 16.0 * q, None, A.add)
-    tt(v("fg", 0, 1), v("pf", 0, 1), v("fi", 0, 1), A.subtract)
+        ts(v("ni", q, q + 1), P16, 16.0 * q, None, A.add)
+    tt(v("fg", 0, 1), v("pf", 0, 1), P16, A.subtract)
     cp(v("ou"), v("oui"))
     ts(v("kn"), v("ni"), 1.0, STEPK, A.add, A.mult)
-    ts(v("tie"), v("Js", 0, 112), v("fi", 0, 1), -TINY, A.is_gt, A.mult)
+    ts(v("tie"), v("Js", 0, 112), P16, -TINY, A.is_gt, A.mult)
     cp(v("Rp", 0, 129, 128), v("kn"))
-    ts(v("mask"), v("Js"), v("fi", 0, 1), None, A.is_equal)
+    ts(v("mask"), v("Js"), P16, None, A.is_equal)
     ts(v("Wt"), v("Jg"), v("fg", 0, 1), None, A.is_equal)
     for b in range(4):
         act(v("Ut", 513 * b, 512 * b + 512, 4), v("ident"), ACT.Copy)
-    quant(v("qu"), v("su"), v("ut"))
     ts(v("rsa"), v("Js", 0, 112), 0.0, None, A.not_equal)
+    quant(v("qo"), v("so"), v("Wt"))
+    for b in range(4):
+        quant(v("qd", 128 * b, 128 * b + 128), v("sd", 128 * b, 128 * b + 128), v("Ut", 512 * b, 512 * b + 512))
+    sfill(v("Sp", 0, 1), BIG)
+    for e in range(4):
+        sfill(v("Sp", 128 * e + 112, 128 * e + 120), 0.0)
+    sfill(v("sela", 112, 120), -STEPK)
+    sfill(v("selb", 96, 104), -STEPK)
+    sfill(v("Kw", C, W), -BIG)
+    sfill(v("cod", 24, 64), 0.0)
+    for q in range(2):
+        ts(v("tieb", 24 * q, 24 * q + 24), v("J", 0, 24), v("ni", q, q + 1), -TINY, A.is_lt, A.mult)
+    ts(v("rsb"), v("J", 0, 49), 24.0, None, A.not_equal)
+    ts(v("PR", 48, 49), P16, -8.0, 0.0, A.add, A.max)
+    ts(v("r4a"), v("J", 0, 4), PQ, 4 * TURN, A.is_equal, A.mult)
+    ts(v("r4b"), v("J", 0, 4), -1.0, PQ, A.add, A.is_equal)
+    ts(v("r4b"), v("r4b"), -TURN, None, A.mult)
+    tt(v("r4c"), v("r4a"), v("r4b"), A.add)
+    for e in range(4):
+        act(v("rb", e, C, 4), v("zer", 0, C // 4), ACT.Identity, bias=v("r4c", e, e + 1))
+    ts(v("ab", 0, 1), PQ, 3.0, TURN, A.is_lt, A.mult)
+    ts(v("ab", 0, 1), v("ab", 0, 1), -TURN / 2, None, A.add)
+    ts(v("ab", 1, 2), P4, 2 * TURN, None, A.add)
+    quant(v("qu"), v("su"), v("ut"))
     record("V", lambda: g.vector.tensor_copy(T.qup[:, 0:256].bitcast(dt.uint32), T.qu[:, 0:128].bitcast(dt.uint32).indirect(T.ou[:, 0:16])),
-           [v("qup")], [v("qu"), v("ou")])
+           [v("qup")], [v("qu"), v("ou")], 450)
     act(v("sup"), ind(v("su"), v("ou")), ACT.Copy)
-    act(v("Fa", 0, 512), v("zer"), ACT.Copy)
-    for h in range(2):
-        act(v("Fb", 512 * h, 512 * h + 512), v("zer"), ACT.Copy)
+    quant(v("qv"), v("sv"), v("vt"))
 
     def state_quant(r, part):
         a, b, k = PARTS[part]
         qx, sx = v("qx%d" % r, a, b), v("sx%d" % r, a, b)
         quant(qx, sx, v("X%d" % r, 4 * a, 4 * b))
-        if r < R:
-            remote(r, v("lq%d" % r, a, b), qx, "arr%d" % r, True)
-            remote(r, v("ls%d" % r, a, b), sx, "arr%d" % r, False)
-            for j, c in ((0, 0), (1, 0), (2, 128)):
-                mm(bank(k + j, 0, b - a), v("qup", c, c + 128), v("sup", c, c + 128), qx, sx)
-        else:
+        first = len(ops) - 1
+        if r == R:
             mm(bank(k, 0, b - a), v("qv"), v("sv"), qx, sx)
-
-    def maxima(part):
-        a, b, k = PARTS[part]
+            return first, None
+        remote(r, v("lq%d" % r, a, b), qx, "arr%d" % r, True, OPT["codes"])
+        remote(r, v("ls%d" % r, a, b), sx, "arr%d" % r, False, OPT["codes"])
+        for j in range(2):
+            mm(bank(k + j, 0, b - a), v("qup", 128 * j, 128 * j + 128), v("sup", 128 * j, 128 * j + 128), qx, sx)
         scan(v("Ms", a, b), v("rsM", a, b), bank(k, 0, b - a), BIG if a == 0 else 0.0, A.add, A.max)
-
-    def score_copies(part):
-        a, b, k = PARTS[part]
+        second = len(ops) - 1
         for e in range(4):
             s = 1 if a == 0 and e == 0 else 0
-            act(v("Sp", 128 * e + a // 4 + s, 128 * e + b // 4), bank(k + 1, e + 4 * s, b - a, 4), ACT.Copy)
-
-    def key_copies(part):
-        a, b, k = PARTS[part]
-        act(v("Kw", a, b), bank(k + 2, 0, b - a), ACT.Copy)
-        act(v("Kp", a + 1, b + 1), bank(k + 2, 0, b - a), ACT.Copy)
+            act(v("Sp", 128 * e + a // 4 + s, 128 * e + b // 4), bank(k, e + 4 * s, b - a, 4), ACT.Copy)
+        act(v("Kw", a, b), bank(k + 1, 0, b - a), ACT.Copy)
+        return first, second
 
     def part_of(src, c0, c1):
         return (src[0], src[1] + src[2] * c0, src[1] + src[2] * (c1 - 1) + 1, src[2])
-
-    def masked(c0, c1):
-        tt(v("Mm", c0, c1), part_of(BLOCKS, c0, c1), v("mask", c0, c1), A.mult)
 
     def owned(c0, c1):
         scan(v("own", c0, c1), v("rsa", c0, c1), v("Mm", c0, c1), 0.0, A.mult, A.add)
 
     BLOCKS, COLUMNS = ("Ms", 3, 4), ("Cd", 0, 1)
 
-    def block_maxima():
-        maxima("A")
-        masked(48, 112)
-        maxima("B")
-        owned(48, 112)
-        masked(0, 48)
-
-    def select(src, nq, F, sel, w, vals, cap, off, gap):
+    def select(src, halves, cuts, on_scalar, F, sel, w, vals):
+        nq = len(halves[0]) + len(halves[1]) - 1
         n = 16 * nq
-        place = {q: q - 1 for q in range(1, nq - 1)}
-        place.update({0: nq - 2, nq - 1: nq - 1, "tie": nq})
 
         def slot(q, c0, c1):
-            o = 512 * (place[q] // 4) + place[q] % 4
+            h = 0 if q in halves[0] else 1
+            o = 512 * h + halves[h].index(q)
             return v(F, o + 4 * c0, o + 4 * (c1 - 1) + 1, 4)
-
-        def me(q):
-            return v("own", 16 * q + 15, 16 * q + 16)
-
-        def flags(q):
-            if q > 0:
-                ts(slot(q, 0, 16 * q), part_of(src, 0, 16 * q), me(q), None, A.is_lt)
+        for q in range(nq):
+            me = v("own", 16 * q + 15, 16 * q + 16)
+            act(v("dd", 16 * q, 16 * q + 16), part_of(src, 16 * q, 16 * q + 16), ACT.Identity, bias=me, scale=-1.0)
+            lo = cuts if 16 * q > cuts else 0
+            if lo:
+                ts(slot(q, 0, lo), part_of(src, 0, lo), me, None, A.is_lt)
+            if q in on_scalar:
+                o = 112 * on_scalar.index(q)
+                hi = n if q < nq - 1 else n - 16
+                l2 = lo if 16 * q > lo else 16 * q + 16
+                act(v("sg", o + l2, o + hi), part_of(src, l2, hi), ACT.Sign, bias=me, scale=-1.0)
+                if 16 * q > lo:
+                    act(slot(q, lo, 16 * q), v("sg", o + lo, o + 16 * q), ACT.Relu)
+                if q < nq - 1:
+                    act(slot(q, 16 * q + 16, n), v("sg", o + 16 * q + 16, o + n), ACT.Sign, bias=1.0)
+                continue
+            if 16 * q > lo:
+                ts(slot(q, lo, 16 * q), part_of(src, lo, 16 * q), me, None, A.is_lt)
             if q < nq - 1:
-                ts(slot(q, 16 * q + 16, n), part_of(src, 16 * q + 16, n), me(q), None, A.is_le)
-
-        def diff(q):
-            act(v("dd", 16 * q, 16 * q + 16), part_of(src, 16 * q, 16 * q + 16), ACT.Identity, bias=me(q), scale=-1.0)
-        if nq == 7:
-            for q in (6, 5, 4, 3):
-                diff(q)
-            act(v("sg", 192, 192 + n), part_of(src, 0, n), ACT.Sign, bias=me(5), scale=-1.0)
-            act(v("sg", 96, 96 + n - 16), part_of(src, 0, n - 16), ACT.Sign, bias=me(6), scale=-1.0)
-            flags(3)
-            owned(0, 48)
-            act(slot(5, 0, 80), v("sg", 192, 272), ACT.Relu)
-            act(slot(5, 96, n), v("sg", 288, 304), ACT.Sign, bias=1.0)
-            act(slot(6, 0, n - 16), v("sg", 96, 96 + n - 16), ACT.Relu)
-        for q in range(3 if nq == 7 else nq):
-            diff(q)
-        for q in ((4, 1, 2, 0) if nq == 7 else (1, 2, 3, 4, 0, 5)):
-            flags(q)
-        tt(slot("tie", 0, n), v("dd", 0, n), v("tie", 0, n), A.is_gt)
+                ts(slot(q, 16 * q + 16, n), part_of(src, 16 * q + 16, n), me, None, A.is_le)
+        for c0, c1 in ((cuts, n), (0, cuts)):
+            if c1 > c0:
+                tt(slot("tie", c0, c1), v("dd", c0, c1), v("tie", c0, c1), A.is_gt)
         for h in range(2):
             quant(v("qf", 128 * h, 128 * h + 128), v("sf", 128 * h, 128 * h + 128), v(F, 512 * h, 512 * h + 512))
             mm(bank(3, 0, 128), v("qo"), v("so"), v("qf", 128 * h, 128 * h + 128), v("sf", 128 * h, 128 * h + 128), h == 0, h == 1)
-        gap()
         ts(v(sel, 0, n), bank(3, 0, n), 23.5, -STEPK, A.is_lt, A.mult)
         for q in range(2):
             scan(v("Rp", 128 * q + 1, 128 * q + w), v(sel, 0, w - 1), v("zer", 0, w - 1), v("kn", q, q + 1), A.add, A.max)
         for q in range(2):
-            scan(v(cap, 128 * q, 128 * q + w), v("Rp", 128 * q, 128 * q + w), v(vals, 0, w), 0.0, A.add, A.min)
-        cp(v(off), v(cap, w - 1, w + 128, 128))
+            scan(v("cap", 128 * q, 128 * q + w), v("Rp", 128 * q, 128 * q + w), v(vals, 0, w), 0.0, A.add, A.min)
+        return v("cap", w - 1, w + 128, 128)
+
+    RUNS = ((K, K + 128, 0), (K + 128, C, 4), (0, K, 0))
 
     def order(r):
-        def gap1():
-            score_copies("B")
-            if r == 0:
-                quant(v("qd"), v("sd"), v("Ut"))
-                for e in range(4):
-                    act(v("Sp", 128 * e + 112, 128 * e + 120), v("zer", 0, 8), ACT.Copy)
-            key_copies("B")
-
-        def gap2():
-            for e in range(4):
-                act(v("cc", e, 128, 4), ind(v("J", 0, 128), v("offa")), ACT.Identity, bias=float(e), scale=4.0)
-            if r == 0:
-                key_copies("A")
-                fill(v("selb", 96, 104), -STEPK)
-                fill(v("Ha", 32, 33), BASE + 456.0)
-                for q in range(2):
-                    ts(v("tieb", 32 * q, 32 * q + 32), v("J", 0, 32), v("ni", q, q + 1), -TINY, A.is_lt, A.mult)
-                ts(v("rsb"), v("J", 0, 64), 32.0, None, A.not_equal)
-                act(v("Kw", C, 456), v("zer", 0, 8), ACT.Identity, bias=-BIG)
-                act(v("Kp", 0, 1), v("zer", 0, 1), ACT.Copy)
-                act(v("Kp", C + 1, 456), v("zer", 0, 7), ACT.Copy)
-            act(v("Ww"), v("zer", 0, 456), ACT.Copy)
-            for b in range(4):
-                mm(bank(4 + b, 0, C), v("qd", 128 * b, 128 * b + 128), v("sd", 128 * b, 128 * b + 128), v("lq%d" % r), v("ls%d" % r))
-        select(BLOCKS, 7, "Fa", "sela", 120, "Jb", "capa", "offa", gap1)
+        for c0, c1 in ((48, 112), (0, 48)):
+            tt(v("Mm", c0, c1), part_of(BLOCKS, c0, c1), v("mask", c0, c1), A.mult)
+            owned(c0, c1)
+        cp(v("offa"), select(BLOCKS, ((3, 4, 5, 6), (0, 1, 2, "tie")), 48, OPT["sa"], "Fa", "sela", 120, "Jb"))
         for e in range(4):
             i = ind(v("Sp", 128 * e, 128 * e + 120), v("offa"))
             tt(v("Mm", e, 128, 4), i, v("mask", e, 128, 4), A.mult)
             act(v("Cd", e, 128, 4), i, ACT.Copy)
+        for e in range(4):
+            act(v("cc", e, 128, 4), ind(v("J", 0, 128), v("offa")), ACT.Identity, bias=e - MID, scale=4.0)
         owned(0, 96)
-        select(COLUMNS, 6, "Fb", "selb", 104, "cc", "capb", "offb", gap2)
+        heads = select(COLUMNS, ((1, 2, 3, 4), (0, 5, "tie")), 0, OPT["sb"], "Fb", "selb", 104, "cc")
+        ts(v("offb"), heads, MID, None, A.add)
+        ts(v("offp"), heads, MID - 1, None, A.add)
+        arrival(r, [v("lq%d" % r), v("ls%d" % r)], "arr%d" % r)
+        for b in range(4):
+            mm(bank(4 + b, 0, C), v("qd", 128 * b, 128 * b + 128), v("sd", 128 * b, 128 * b + 128), v("lq%d" % r), v("ls%d" % r))
+            act(v("Dp", b, 4 * C, 4), bank(4 + b, 0, C), ACT.Copy)
         tt(v("km"), ind(v("Kw"), v("offb")), v("mask", 0, 32), A.mult)
         cp(v("key"), ind(v("Kw"), v("offb")))
-        act(v("Ha", 0, 32), ind(v("J"), v("offb")), ACT.Identity, bias=BASE)
-        act(v("kp"), ind(v("Kp"), v("offb")), ACT.Copy)
-        act(v("Wb"), ind(v("J"), v("offb")), ACT.Identity, bias=BASE + 2049.0, scale=-1.0)
-        if r == 0:
-            act(v("cod", 24, 32), v("zer", 0, 8), ACT.Copy)
-            act(v("dec"), v("zer", 0, C), ACT.Identity, bias=-2047.0)
-            act(v("rb"), v("mask"), ACT.Identity, bias=-2048.0, scale=4194304.0)
-        for b in range(4):
-            act(v("Dp", C * b, C * b + C), bank(4 + b, 0, C), ACT.Copy)
+        act(v("Ha"), ind(v("J"), v("offb")), ACT.Copy)
+        act(v("kp"), ind(v("Kw"), v("offp")), ACT.Copy)
+        act(v("Wb"), ind(v("J"), v("offb")), ACT.Identity, bias=TURN + 1, scale=-1.0)
         scan(v("ko"), v("rsa", 0, 32), v("km"), 0.0, A.mult, A.add)
-        tt(v("LL"), v("Ha", 1, 33), v("Ha", 0, 32), A.subtract)
         for q in range(2):
-            ts(v("dk", 32 * q, 32 * q + 32), v("key"), v("ko", 16 * q + 15, 16 * q + 16), None, A.subtract)
+            tt(v("LL", 24 * q, 24 * q + 24), v("Ha", 1, 25), v("Ha", 0, 24), A.subtract)
+            ts(v("dk", 24 * q, 24 * q + 24), v("key", 0, 24), v("ko", 16 * q + 15, 16 * q + 16), None, A.subtract)
         tt(v("turn"), v("key", 0, 24), v("kp", 1, 25), A.is_lt)
         tt(v("FL"), v("dk"), v("tieb"), A.is_gt)
         tt(v("ca"), v("turn"), v("Wb", 1, 25), A.mult)
-        for q in range(2):
-            tt(v("PR", 32 * q, 32 * q + 32), v("FL", 32 * q, 32 * q + 32), v("LL"), A.mult)
+        tt(v("PR", 0, 48), v("FL"), v("LL"), A.mult)
         tt(v("cod", 0, 24), v("ca"), v("Ha", 0, 24), A.max)
         scan(v("Pp"), v("rsb"), v("PR"), 0.0, A.mult, A.add)
-        cp(v("offc"), v("Pp", 31, 64, 32))
+        for h in range(2):
+            ts(v("offc", 2 * h, 2 * h + 2), v("Pp", 23, 49, 25), float(W * h), None, A.add)
+            sfill(v("Ww", W * h, W * h + W), 1.0)
         cp(ind(v("Ww"), v("offc")), v("cod"))
-        scan(v("us"), v("dec"), v("Ww", 0, C), 0.0, A.add, A.max)
-        scan(v("wr"), v("rb"), v("us"), 0.0, A.add, A.min)
-        w = v("wr", 15, C, 16)
-        ts(v("rr"), w, MAGIC, MAGIC, A.add, A.subtract)
-        tt(v("ya"), w, v("rr"), A.subtract)
-        act(v("oo"), v("ya"), ACT.Abs)
-        cp(v("ord%d" % r), v("oo"))
-        remote(r, v("lst%d" % r, 0, 10), v("ord%d" % r, 0, 10), "lis%d" % r, False)
-        for t in (2, 0, 3, 1):
-            ts(v("offo", 18 * t, 18 * t + 18), v("oo", 10, 28), 4.0, float(t), A.mult, A.add)
+        if OPT["usplit"]:
+            scan(v("us", 0, K), v("Ww", W, W + K), v("Ww", 0, K), 0.0, A.mult, A.add)
+            scan(v("us", K, C), v("Ww", W + K, W + C), v("Ww", K, C), v("us", K - 1, K), A.mult, A.add)
+        else:
+            scan(v("us"), v("Ww", W, W + C), v("Ww", 0, C), 0.0, A.mult, A.add)
+        for a, b, k in [RUNS[i] for i in OPT["wr"]]:
+            scan(v("wr", a, b), v("rb", a, b), v("us", a, b), 0.0, A.add, A.min)
+            row("wr")
+            act(v("oo", a // 4, b // 4), v("wr", a + 3, b, 4), ACT.Abs, bias=v("ab", 0, 1))
+            ts(v("ord%d" % r, a // 4, b // 4), v("oo", a // 4, b // 4), -4.0, v("ab", 1, 2), A.mult, A.add)
+        remote(r, v("lst%d" % r), v("ord%d" % r, 0, K // 4), "lis%d" % r, False, OPT["list"])
+        arrival(r, [v("lst%d" % r)], "lis%d" % r)
 
     def layer(r):
         X, Y = "X%d" % r, "X%d" % (r + 1)
-        runs = ((K, K + 128, 0), (K + 128, C, 4), (0, K, 0))
-
-        def move(o, i, on_vector):
-            if on_vector:
-                cp(o, i)
-            else:
-                act(o, i, ACT.Copy)
-
-        def product(a, b, k):
+        at = {}
+        for i, (a, b, k) in enumerate(RUNS):
+            n = OPT["g"][i]
+            win, lst = (v(X), "ord%d" % r) if a else (v("Dp"), "lst%d" % r)
+            cp(v("Et", 4 * a, 4 * (a + n)), ind(win, v(lst, a // 4, (a + n) // 4)))
+            act(v("Et", 4 * (a + n), 4 * b), ind(win, v(lst, (a + n) // 4, b // 4)), ACT.Copy)
             quant(v("qe", a, b), v("se", a, b), v("Et", 4 * a, 4 * b))
+            at.update({"g%d" % i: len(ops) - 3, "G%d" % i: len(ops) - 2, "q%d" % i: len(ops) - 1})
             for j in range(4):
                 mm(bank(k + j, 0, b - a), v("qw", 128 * j, 128 * j + 128), v("sw", 128 * j, 128 * j + 128), v("qe", a, b), v("se", a, b))
-
-        def relu(a, b, k):
-            for j in range(4):
+                row("products")
                 act(v("Rr", C * j + a, C * j + b), bank(k + j, 0, b - a), ACT.Relu, scale=0.015625)
-
-        def add(a, b, js=range(4)):
-            for j in js:
                 tt(v(Y, 4 * a + j, 4 * b, 4), v("Et", 4 * a + j, 4 * b, 4), v("Rr", C * j + a, C * j + b), A.add)
-        for a, b, k in runs[:2]:
-            for t in (2, 0, 3, 1):
-                m = 18 * t + (a - K) // 16
-                move(v("Et", 4 * a + t, 4 * b, 4), ind(v(X), v("offo", m, m + (b - a) // 16)), t < 2)
-            product(a, b, k)
-        relu(*runs[0])
-        add(K, K + 128)
-        relu(*runs[1])
-        add(K + 128, C, range(3))
-        for t in range(4):
-            move(v("Et", t, 4 * K, 4), ind(v("Dp", C * t, C * t + C), v("lst%d" % r, 0, 10)), t < 1)
-        product(*runs[2])
-        add(K + 128, C, range(3, 4))
-        state_quant(r + 1, "A")
-        relu(*runs[2])
-        if r + 1 < R:
-            score_copies("A")
-            key_copies("A")
-        else:
-            dma("Y", lambda: T.oc[:, 4 * K:4 * C], lambda: T[QL][:, K:C].bitcast(dt.uint8), [], [v(QL, K, C)])
-            act(v("yt", K, C), bank(4, 0, C - K), ACT.Copy)
-            dma("Y", lambda: T.y[:, K:C], lambda: T.yt[:, K:C], [], [v("yt", K, C)])
-            act(v("olt"), ind(v("J"), v("ord%d" % r)), ACT.Copy)
-            dma("Y", lambda: T.ol[:], lambda: T.olt[0:128:16, :], [], [v("olt")])
-        add(0, K)
-        state_quant(r + 1, "B")
-        if r == R - 2:
-            quant(v("qv"), v("sv"), v("vt"))
-        if r + 1 < R:
-            block_maxima()
+                at.update({"R%d%d" % (i, j): len(ops) - 2, "a%d%d" % (i, j): len(ops) - 1})
+            if b == C:
+                at["qA"], at["mA"] = state_quant(r + 1, "A")
+        at["qB"], at["mB"] = state_quant(r + 1, "B")
+        for names in (OPT["V"], OPT["S"]):
+            names = [at[w] for w in names.split() if at[w] is not None]
+            for o, me in zip(names, names[1:]):
+                ops[me]["behind"].add(o)
 
-    QL, SL = "qx%d" % R, "sx%d" % R
     state_quant(0, "A")
     state_quant(0, "B")
-    fill(v("Sp", 0, 1), BIG)
-    fill(v("sela", 112, 120), -STEPK)
-    quant(v("qo"), v("so"), v("Wt"))
-    score_copies("A")
-    block_maxima()
     for r in range(R):
         order(r)
         layer(r)
-    dma("S", lambda: T.oc[:, 0:4 * K], lambda: T[QL][:, 0:K].bitcast(dt.uint8), [], [v(QL, 0, K)])
+    QL, SL = "qx%d" % R, "sx%d" % R
+    act(v("ola"), v("us"), ACT.Abs, bias=-TURN / 2)
+    act(v("olt"), v("ola"), ACT.Identity, bias=TURN / 2, scale=-1.0)
+    dma("Y", lambda: T.ol[:], lambda: T.olt[0:128:16, :], [], [v("olt")])
 
-    def scales(q, k):
-        dma(q, lambda: T.osc[4 * k:4 * k + 4, 0:C], lambda: T[SL][32 * k:32 * k + 4, 0:C], [], [v(SL)])
+    def store(part):
+        a, b, k = PARTS[part]
+        dma("Y" if a else "S", lambda: T.oc[:, 4 * a:4 * b], lambda: T[QL][:, a:b].bitcast(dt.uint8), [], [v(QL, a, b)])
+        if a:
+            act(v("yt", a, b), bank(k, 0, b - a), ACT.Copy)
+        else:
+            cp(v("yt", a, b), bank(k, 0, b - a))
+        dma("Y", lambda: T.y[:, a:b], lambda: T.yt[:, a:b], [], [v("yt", a, b)])
+
+    def scales(k):
+        dma("Y" if k < 1 else "S", lambda: T.osc[4 * k:4 * k + 4, 0:C], lambda: T[SL][32 * k:32 * k + 4, 0:C], [], [v(SL)])
+    store("A")
+    store("B")
     for k in range(4):
-        scales("Y" if k < 1 else "S", k)
-    cp(v("yt", 0, K), bank(0, 0, K))
-    dma("Y", lambda: T.y[:, 0:K], lambda: T.yt[:, 0:K], [], [v("yt", 0, K)])
+        scales(k)
+
+    wait = OPT["wait"]
+    users = [[] for _ in ops]
+    for me, op in enumerate(ops):
+        for o in op["deps"] | op["behind"]:
+            users[o].append(me)
+
+    def gap(o, me):
+        if o in ops[me]["deps"]:
+            return ops[o]["done"] + wait
+        return ops[o]["done"] if ops[me]["q"] == "-" else ops[o]["hold"]
+    def lay(turn, before, least, first):
+        at, busy = {}, {q: [] for q in QUEUES}
+        for me in turn:
+            t = max([first(me)] + [at[o] + least(o, me) for o in before(me)])
+            taken, hold = busy[ops[me]["q"]], ops[me]["hold"]
+            i = 0
+            while i < len(taken) and taken[i][0] < t + hold - 1e-9:
+                t = max(t, taken[i][1])
+                i += 1
+            taken.insert(i, (t, t + hold))
+            at[me] = t
+        return at
+    QUEUES, every = list(queue) + ["-"], range(len(ops))
+    tail = [0.0] * len(ops)
+    sort, seen = [], set()
+    for me in every:
+        stack = [me]
+        while stack:
+            o = stack[-1]
+            todo = [x for x in ops[o]["deps"] | ops[o]["behind"] if x not in seen]
+            if todo:
+                stack.extend(todo)
+                continue
+            stack.pop()
+            if o not in seen:
+                seen.add(o)
+                sort.append(o)
+    for me in reversed(sort):
+        tail[me] = max([ops[me]["done"]] + [gap(me, u) + tail[u] for u in users[me]])
+    turn, best = sorted(every, key=lambda o: (-tail[o], o)), None
+    for _ in range(OPT["passes"]):
+        at = lay(turn, lambda o: ops[o]["deps"] | ops[o]["behind"], gap, lambda o: 0.0)
+        end = max(at[o] + ops[o]["done"] for o in every)
+        if best is None or end < best[0] - 1e-9:
+            best = (end, at)
+        late = lay(sorted(every, key=lambda o: (-at[o] - ops[o]["hold"], -o)), lambda o: users[o],
+                   lambda u, o: gap(o, u) + ops[u]["hold"] - ops[o]["hold"], lambda o: ops[o]["done"] - ops[o]["hold"])
+        turn = sorted(every, key=lambda o: (-late[o] - ops[o]["hold"], o))
+    issue = sorted(every, key=lambda o: (best[1][o], o))
+    place = {o: i for i, o in enumerate(issue)}
 
     def line(o):
         return ops[o]["q"] if ops[o]["sem"] is None else ops[o]["sem"]
-    known = {q: {} for q in list(queue) + ["-"]}
+    known = {q: {} for q in QUEUES}
     waited = set()
-    for me, op in enumerate(ops):
+    for me in issue:
+        op = ops[me]
         kn, need = known[op["q"]], {}
         for o in op["deps"]:
             if ops[o]["sem"] != "none":
-                need[line(o)] = max(need.get(line(o), -1), o)
+                need[line(o)] = max(need.get(line(o), -1), place[o])
         op["waits"] = []
-        for o in sorted(need.values(), reverse=True):
-            if kn.get(line(o), -1) >= o:
+        for i in sorted(need.values(), reverse=True):
+            o = issue[i]
+            if kn.get(line(o), -1) >= i:
                 continue
             op["waits"].append(o)
             waited.add(o)
-            kn[line(o)] = o
+            kn[line(o)] = i
             for l, x in ops[o]["knows"].items():
                 kn[l] = max(kn.get(l, -1), x)
         op["knows"] = dict(kn)
     count = {q: 0 for q in queue}
     left = []
-    for me, op in enumerate(ops):
+    for me in issue:
+        op = ops[me]
         if op["q"] == "-":
             continue
         for o in op["waits"]:

@@ -2,30 +2,46 @@ from concourse.mybir import dt, AluOpType, ActivationFunctionType
 C, K, R = 448, 160, 3
 STEP = [1, 2, 1]
 F32, BF, I32, U16, U8, X4 = "float32", "bfloat16", "int32", "uint16", "uint8", "float8_e4m3fn_x4"
-BIG, TINY, STEPK, TURN, MID = 1e29, 1e-32, 512.0, 1024.0, 228.0
-W = 456
+BIG, TINY, STEPK, TURN, HOLD, MID = 2.0 ** 96, 1e-32, 512.0, 2 * C - 1, 1024.0, 228.0
 _SB = {}
-for _d, _l in ((BF, "ut512 vt512 Et1792 Dp1792 Js128 Jg512 Jb128 mask128 rsa112 rsb49 one464 rsM448 zer512 ident128 Wt512 Ut2048 sg448 "
-                    "Fa1024 Fb1024 sela120 selb104 Rp256 cap256 cc128 rb448 dd112 tie112 dk48 tieb48"),
+for _d, _l in ((BF, "ut512 vt512 Dp3584 Js128 Jg128 Jq192 Jb128 mask128 maskk32 rsa112 rsb75 rs_448 m_32 rsM448 rsQ192 mneg192 zer512 ident128 blk128 Wt512 "
+                    "Ut516 sg448 sh192 Fa1024 Fb1024 sela120 selb104 Rp256 cap256 cc128 rb448 dd112 tie112 dk49 tieb49 pb4"),
                (X4, "qu128 qup256 qv128 qw512 qe448 qo128 qd512 qf256"), (U8, "su128 sup256 sv128 sw512 se448 so128 sd512 sf256"),
-               (I32, "pint2 iint4 oui16"), (U16, "ou16 offa2 offb2 offp2 offc4"),
-               (F32, "Rr1792 pf2 fi4 fg2 ni2 kn2 r4a4 r4b4 r4c4 ab2 J464 Ms448 Mm128 own112 Sp512 Kw456 Cd128 key32 kp32 Ha32 Wb32 km32 ko32 "
-                     "LL48 FL48 PR49 turn24 ca24 cod64 Pp49 Ww912 us448 wr448 oo112 ola448 olt448 yt448")):
+               (I32, "pint2 iint4 oui16"), (U16, "ou16 offa2 offz2 offb2 offp2 offc4"),
+               (F32, "Rr1792 pf2 fi4 ni2 nk2 kn2 r4a4 r4b4 r4c4 ab4 J464 Ms448 Mq192 Mm128 own112 ownq192 Sp512 Kw456 Cd128 key32 kp32 Ha32 Wb32 "
+                     "km32 ko32 LL49 FL49 PR75 turn24 ca24 cod48 Pp75 r4m4 Tm448 Zm480 Mc32 ownc24 Ww896 us448 wr448 oo112 ola448 olt448 yt448")):
     for _w in _l.split():
         _n = _w.rstrip("0123456789")
-        _SB[_n] = (int(_w[len(_n):]), _d)
+        _SB[_n.replace("_", "4")] = (int(_w[len(_n):]), _d)
 for _r in range(R + 1):
-    _SB.update({"X%d" % _r: (4 * C, BF), "qx%d" % _r: (C, X4), "sx%d" % _r: (C, U8)})
+    _SB.update({"X%d" % _r: (8 * C if _r < R else 4 * C, BF), "qx%d" % _r: (C, X4), "sx%d" % _r: (C, U8)})
 for _r in range(R):
     _SB.update({"lq%d" % _r: (C, X4), "ls%d" % _r: (C, U8), "lst%d" % _r: (K // 4, U16), "ord%d" % _r: (C // 4, U16)})
-SCRATCH = {k: ("sbuf", [128, n], d) for k, (n, d) in _SB.items()}
+_IN = {}
+for _b, _l in (("small", "pf fi ni nk kn r4a r4b r4c r4m ab"), ("runs", "key kp Ha Wb km ko turn ca")):
+    _SB[_b] = (0, F32)
+    for _n in _l.split():
+        _IN[_n] = (_b, _SB[_b][0])
+        _SB[_b] = (_SB[_b][0] + (_SB[_n][0] + 7) // 8 * 8, F32)
+SCRATCH = {k: ("sbuf", [128, n], d) for k, (n, d) in _SB.items() if k not in _IN}
 SCRATCH["ps"] = ("psum", [128, 4096], F32)
-SEMAPHORES = (["sV", "sS", "sP", "sG", "sent"] + ["dm%d" % i for i in range(20)]
+SEMAPHORES = (["sV", "sS", "sP", "sG", "sent"] + ["dm%d" % i for i in range(24)]
               + ["arr%d" % r for r in range(R)] + ["lis%d" % r for r in range(R)])
-CYCLE, WAIT, LOAD, LIST, CODES = 0.85e-3, 0.19, 2.0, 1.8, 5.5
-OPT = {"g": (64, 56, 48),
-       "V": "g0 q0 g1 q1 a00 a01 a02 a03 g2 a10 q2 a11 a12 a13 a20 qA a21 a22 a23 mA qB",
-       "S": "G0 G1 R00 R01 R02 R03 G2 R10 R11 R12 R13 R20 R21 R22 R23", "sa": (5, 6), "sb": (), "wait": WAIT, "list": LIST, "codes": CODES, "usplit": 0, "passes": 3, "wr": (2, 0, 1)}
+CYCLE, WAIT, LOAD, LIST, CODES = 1e-3, 0.2, 2.0, 1.8, 4.0
+OPT = {"g": (56, 72, 48), "h": (0, 0, 0), "lazy": 0.0, "split": 1, "fv": "", "cyc": CYCLE, "load": LOAD, "spare": (99, 99), "sest": 0, "pest": 1.3, "k2": 0, "tsplit": 1, "la": (), "pf": 0,
+       "V": "Faq xA0 xA1 z3 z2 Fas z1 Far0 Far1 z0 Fac0 Fac1 xB0 oz oa xB1 mc c0 c1 ow Fbl1 Fbg1 Fbl2 Fbg2 Fbl3 Fbg3 Fbl4 Fbg4 Fbg0 Fbt0 Fbp Fbq "
+            "xA2 xA3 xB2 xB3 Fbs e0 Fbr0 Fbr1 e1 Fbc0 Fbc1 e2 ob op km e3 dk fl pr pp d00 oc d01 sc d10 "
+            "u0 d11 d20 w0 w2 u1 t0 t2 w1 g0 t1 d21 q0 g1 d30 d31 q1 a00 a01 a02 a03 g2 a10 q2 a11 a12 a13 qC a20 qA a21 a22 a23 "
+            "+mA qB +kA +nA +oA +nB +mB +oB +Fab3 +Fab4 +Fab5 +Fab6 +Fag0 +Fag1 +Fal1 +Fal2 +Fag2 +Fat1 +Fat0 +Fap",
+       "S": "TB0 TB1 TB2 TB3 KB c2 c3 C0 C1 FbD0 FbD1 FbD2 FbD3 FbD4 FbD5 FbS5 C2 FbL5 C3 H KP WB DK D0 D1 D2 D3 "
+            "G0 G1 R00 R01 R02 R03 R10 G2 R11 R12 R13 +W0 R20 R21 R22 R23 +W1 +PA0 +PA1 +PA2 +FaS3 +FaS4 +FaS5 +FaS6 +FaD3 +FaD4 +FaD5 +FaD6 "
+            "+FaG3 +FaL4 +FaG4 +FaL5 +FaD0 +FaD1 +FaD2 +FaG5 +FaL6 +PA3 +TA0 +TA1 +TA2 +TA3 +PB0 +PB1 +PB2 +PB3",
+       "V0": "pu fA fB pk mA nA nB kA mB oB oA Fag0 Fag1 Fal1 Fal2 Fag2 Fab3 Fab4 Fab5 Fab6 Fag3 Fal4 Fag4 Fat0 Fat1 Fap Faq",
+       "S0": "PU PK PA0 PA1 PA2 PA3 TA0 TA1 TA2 TA3 FaD0 FaD1 FaD2 FaS5 FaS6 FaD3 FaD4 FaD5 FaD6 FaL5 FaG5 FaL6 PB0 PB1 PB2 PB3 TB0",
+       "P": "Fam0 Fam1 Fbm0 Fbm1 n0 n1 n2 n3 m00 m01 m02 m03 m10 m11 m12 m13 m20 m21 m22 m23 +sA +sB +sK +Fam0",
+       "P0": "sA sB sK Fam0",
+       "sa0": (5, 6), "sa": (3, 4, 5, 6), "sb": (5,), "cd": 2, "dkS": 1, "cut": K + 128, "wait": WAIT, "list": LIST, "codes": CODES,
+       "passes": 3, "dadd": 0, "mirD": "V", "mirX": "V", "dlat": 2.0}
 
 
 def rank_program(g, core, T, topo):
@@ -33,11 +49,13 @@ def rank_program(g, core, T, topo):
     if rank is None:
         return
     A, ACT = AluOpType, ActivationFunctionType
+    CYCLE, LOAD = OPT["cyc"], OPT["load"]
     queue = {"V": g.vector, "S": g.scalar, "P": g.tensor, "G": g, "Y": g.sync}
-    ops, acc, ndma, sent, writes, rows = [], {}, [0], [0], {}, {}
+    ops, acc, ndma, sent, writes, lazy = [], {}, [0], [0], {}, set()
 
     def v(name, a=0, b=None, s=1):
-        return (name, a, _SB[name][0] if b is None else b, s)
+        buf, o = _IN.get(name, (name, 0))
+        return (buf, o + a, o + (_SB[name][0] if b is None else b), s)
 
     def bank(k, a, b, s=1):
         return ("ps", 512 * k + a, 512 * k + b, s)
@@ -58,7 +76,8 @@ def rank_program(g, core, T, topo):
     def bits(x):
         if x[0] == "ps":
             return 1 << (x[1] // 512)
-        return sum(1 << c for c in range(x[1], x[2], x[3])) if x[3] > 1 else ((1 << (x[2] - x[1])) - 1) << x[1]
+        n, s = size(x), abs(x[3])
+        return ((1 << s * n) - 1) // ((1 << s) - 1) << min(x[1], x[1] + x[3] * (n - 1))
 
     def cycles(o, ins, per=None):
         views = [x for x in [o] + ins if isinstance(x, tuple)]
@@ -96,51 +115,54 @@ def rank_program(g, core, T, topo):
                 acc.setdefault(x[0], []).append((me, bits(x), w))
         ops.append({"q": q, "fn": fn, "deps": deps, "behind": behind, "sem": sem, "count": count, "hold": hold * CYCLE,
                     "done": hold * CYCLE if done is None else done})
+        return me
 
-    def row(name):
-        if name in rows:
-            ops[-1]["behind"].add(rows[name])
-        rows[name] = len(ops) - 1
+    def row(calls):
+        for o, me in zip(calls, calls[1:]):
+            ops[me]["behind"].add(o)
 
     def ts(o, i, s1, s2, *op):
-        record("V", lambda: g.vector.tensor_scalar(ap(o), ap(i), ap(s1), ap(s2), *op), [o], [i, s1, s2], cycles(o, [i, s1, s2]))
+        return record("V", lambda: g.vector.tensor_scalar(ap(o), ap(i), ap(s1), ap(s2), *op), [o], [i, s1, s2], cycles(o, [i, s1, s2]))
 
     def tt(o, a, b, op):
-        record("V", lambda: g.vector.tensor_tensor(ap(o), ap(a), ap(b), op), [o], [a, b], cycles(o, [a, b], 2))
+        return record("V", lambda: g.vector.tensor_tensor(ap(o), ap(a), ap(b), op), [o], [a, b], cycles(o, [a, b], 1 if a[0] == "ps" else 2))
 
     def cp(o, i):
-        record("V", lambda: g.vector.tensor_copy(ap(o), ap(i)), [o], [i], cycles(o, [i]))
+        return record("V", lambda: g.vector.tensor_copy(ap(o), ap(i)), [o], [i], cycles(o, [i]))
 
     def scan(o, d0, d1, init, op0, op1):
-        record("V", lambda: g.vector.tensor_tensor_scan(ap(o), ap(d0), ap(d1), ap(init), op0, op1), [o], [d0, d1, init], cycles(o, [d0, d1]))
+        return record("V", lambda: g.vector.tensor_tensor_scan(ap(o), ap(d0), ap(d1), ap(init), op0, op1), [o], [d0, d1, init], cycles(o, [d0, d1]))
 
     def fill(o, c):
-        record("V", lambda: g.vector.memset(ap(o), c), [o], [], cycles(o, []))
+        return record("V", lambda: g.vector.memset(ap(o), c), [o], [], cycles(o, []))
 
     def quant(q, s, i):
-        record("V", lambda: g.vector.quantize_mx(ap(q), ap(s), ap(i)), [q, s], [i], 15 + size(q))
+        return record("V", lambda: g.vector.quantize_mx(ap(q), ap(s), ap(i)), [q, s], [i], 15 + size(q))
 
     def act(o, i, f, bias=None, scale=None):
         kw = {}
         if bias is not None:
             kw["bias"] = ap(bias)
         if scale is not None:
-            kw["scale"] = scale
-        record("S", lambda: g.scalar.activation(ap(o), ap(i), f, **kw), [o], [i, bias], cycles(o, [i], 1))
+            kw["scale"] = ap(scale)
+        return record("S", lambda: g.scalar.activation(ap(o), ap(i), f, **kw), [o], [i, bias, scale], cycles(o, [i], 1) if i[0] == "@" or not OPT["sest"] else 65 + size(o))
+
+    def move(q, o, i):
+        return cp(o, i) if q == "V" else act(o, i, ACT.Copy)
 
     def sfill(o, c):
-        act(o, v("zer", 0, size(o)), ACT.Identity, bias=c)
+        return act(o, v("zer", 0, size(o)), ACT.Identity, bias=c)
 
     def mm(o, wq, ws_, xq, xs, start=True, stop=True):
-        record("P", lambda: g.tensor.matmul_mx(ap(o), ap(wq), ap(ws_), ap(xq), ap(xs), start, stop), [o], [wq, ws_, xq, xs], 16 + size(o))
+        return record("P", lambda: g.tensor.matmul_mx(ap(o), ap(wq), ap(ws_), ap(xq), ap(xs), start, stop), [o], [wq, ws_, xq, xs], OPT["pest"] * (16 + size(o)))
 
     def iota(o, pat, ch=0):
         kw = {} if _SB[o[0]][1] == I32 else {"allow_small_or_imprecise_dtypes": True}
-        record("G", lambda: g.iota(ap(o), pat, 0, ch, **kw), [o], [], 160 + 2 * size(o))
+        return record("G", lambda: g.iota(ap(o), pat, 0, ch, **kw), [o], [], 160 + 2 * size(o))
 
-    def dma(q, out, in_, outs, ins, done=LOAD):
+    def dma(q, out, in_, outs, ins, done=LOAD, **kw):
         ndma[0] += 1
-        record(q, lambda: queue[q].dma_start(out(), in_()), outs, ins, 60, sem="dm%d" % ndma[0], count=16, done=done)
+        return record(q, lambda: queue[q].dma_start(out(), in_(), **kw), outs, ins, 700 if q == "G" else 60, sem="dm%d" % ndma[0], count=16, done=done)
 
     def partner(r):
         return T.cores[rank ^ STEP[r]]
@@ -155,101 +177,136 @@ def rank_program(g, core, T, topo):
             if codes:
                 o, i = o.bitcast(dt.uint8), i.bitcast(dt.uint8)
             g.remote_dma(o, i, T.sem[sem], T.sem.sent, pid, rid, topo.mask(core, p))
-        writes.setdefault(sem, []).append(len(ops))
-        record("G", go, [], [src], 300, sem="none", done=done)
+        writes.setdefault(sem, []).append(record("G", go, [], [src], 300, sem="none", done=done))
 
     def arrival(r, outs, sem):
         record("-", None, outs, [], 0, sem=sem, count=len(writes[sem]) * len(topo.engines(partner(r), core)), after=writes[sem])
 
+    def mirror(name, t, a, b):
+        return v(name, 4 * (TURN - a) + t, 4 * (TURN - b) + t, -4)
+
+    products, at, ahead, named = [], {}, {}, []
     PARTS = {"A": (K, C, 4), "B": (0, K, 0)}
-    dma("S", lambda: T.ut[:], lambda: T.u[:], [v("ut")], [])
     dma("Y", lambda: T.X0[:, 4 * K:4 * C], lambda: T.x[:, 4 * K:4 * C], [v("X0", 4 * K, 4 * C)], [], LOAD + 0.6)
-    dma("S", lambda: T.X0[:, 0:4 * K], lambda: T.x[:, 0:4 * K], [v("X0", 0, 4 * K)], [], LOAD + 1.0)
-    ops[2]["behind"].add(0)
-    dma("Y", lambda: T.qw[:].bitcast(dt.uint8), lambda: T.wc[:], [v("qw")], [v("X0")])
-    dma("Y", lambda: T.sw[:], lambda: T.ws[:], [v("sw")], [v("X0")])
-    dma("Y", lambda: T.vt[:], lambda: T.v[:], [v("vt")], [v("X0")])
-    iota(v("pint"), [[16, 2]], 1)
-    iota(v("oui"), [[1, 2], [16, 8]])
-    iota(v("Js"), [[0, 8], [1, 16]])
-    iota(v("Jg"), [[16, 8], [0, 64]])
-    for z in ("zer", "rsM", "Ut", "Fa", "Fb"):
+    row([dma("S", lambda: T.ut[:], lambda: T.u[:], [v("ut")], []),
+         dma("S", lambda: T.X0[:, 0:4 * K], lambda: T.x[:, 0:4 * K], [v("X0", 0, 4 * K)], [], LOAD + 1.0)])
+    if OPT["dadd"]:
+        dma("G", lambda: T.sw[:], lambda: T.ws[:], [v("sw")], [])
+
+    def late_loads():
+        dma("Y", lambda: T.qw[:].bitcast(dt.uint8), lambda: T.wc[:], [v("qw")], [v("offa")], 2 * LOAD)
+        if not OPT["dadd"]:
+            dma("Y", lambda: T.sw[:], lambda: T.ws[:], [v("sw")], [v("offa")], 2 * LOAD)
+        dma("Y", lambda: T.vt[:], lambda: T.v[:], [v("vt")], [v("offb")], 8 * LOAD)
+        quant(v("qv"), v("sv"), v("vt"))
+    constants = len(ops)
+    row([iota(v("pint"), [[16, 2]], 1), iota(v("oui"), [[1, 2], [16, 8]]), iota(v("Js"), [[0, 8], [1, 16]]),
+         iota(v("Jq"), [[0, 3], [1, 16], [0, 4]]), iota(v("Jg"), [[16, 8], [0, 16]]), iota(v("J"), [[1, 464]])])
+    fill(v("zer"), 0.0)
+    for z in ("rsM", "rsQ", "Fa", "Fb", "Ut"):
         for c in range(0, _SB[z][0], 512):
-            if z in ("Ut", "Fb"):
-                act(v(z, c, c + 512), v("zer"), ACT.Copy)
-            else:
-                fill(v(z, c, min(c + 512, _SB[z][0])), 0.0)
-    fill(v("one"), 1.0)
-    fill(v("rsM", 4, C, 4), -4 * BIG)
-    scan(v("J"), v("one"), v("zer", 0, 464), -1.0, A.add, A.add)
+            (fill if z + str(c) in OPT["fv"] else sfill)(v(z, c, min(c + 512, _SB[z][0])), 0.0)
+    sfill(v("rsM", 4, C, 4), -4 * BIG)
+    sfill(v("rsQ", 0, 192, 64), -4 * BIG)
     act(v("Jb"), v("J", 0, 128), ACT.Copy)
     ts(v("iint", 0, 1), v("pint", 0, 1), 15, None, A.bitwise_and)
     ts(v("iint", 1, 2), v("pint", 0, 1), 3, None, A.bitwise_and)
     ts(v("iint", 2, 3), v("pint", 0, 1), 12, 2, A.bitwise_and, A.logical_shift_right)
+    ts(v("iint", 3, 4), v("pint", 0, 1), 7, None, A.bitwise_and)
     cp(v("pf", 0, 1), v("pint", 0, 1))
-    cp(v("fi", 0, 3), v("iint", 0, 3))
-    P16, P4, PQ = v("fi", 0, 1), v("fi", 1, 2), v("fi", 2, 3)
+    cp(v("fi"), v("iint"))
+    P16, P4, PQ, P8 = (v("fi", i, i + 1) for i in range(4))
+    cp(v("pb", 0, 1), P16)
+    tt(v("pb", 1, 2), v("pf", 0, 1), P16, A.subtract)
     ts(v("ident"), v("J", 0, 128), v("pf", 0, 1), None, A.is_equal)
     for q in range(2):
-        ts(v("ni", q, q + 1), P16, 16.0 * q, None, A.add)
-    tt(v("fg", 0, 1), v("pf", 0, 1), P16, A.subtract)
+        ts(v("Rp", 128 * q, 128 * q + 1), P16, 16.0 * q + 1, STEPK, A.add, A.mult)
+    ts(v("nk", 0, 1), P8, 16.0, None, A.add)
+    NK = (P16, v("nk", 0, 1))
     cp(v("ou"), v("oui"))
-    ts(v("kn"), v("ni"), 1.0, STEPK, A.add, A.mult)
-    ts(v("tie"), v("Js", 0, 112), P16, -TINY, A.is_gt, A.mult)
-    cp(v("Rp", 0, 129, 128), v("kn"))
-    ts(v("mask"), v("Js"), P16, None, A.is_equal)
-    ts(v("Wt"), v("Jg"), v("fg", 0, 1), None, A.is_equal)
+    ts(v("tie"), v("Js", 0, 112), v("pb", 0, 1), -TINY, A.is_gt, A.mult)
+    ts(v("mask"), v("Js"), v("pb", 0, 1), None, A.is_equal)
+    ts(v("mneg"), v("Jq"), v("pb", 0, 1), -4 * BIG, A.not_equal, A.mult)
+    ts(v("mneg", 0, 1), v("mask", 0, 1), 5 * BIG, -4 * BIG, A.mult, A.add)
+    ts(v("blk"), v("Jg"), v("pb", 1, 2), None, A.is_equal)
+    act(v("Ut", 3, 515, 4), v("ident"), ACT.Copy)
     for b in range(4):
-        act(v("Ut", 513 * b, 512 * b + 512, 4), v("ident"), ACT.Copy)
+        act(v("Wt", b, 512, 4), v("blk"), ACT.Copy)
+        at["e%d" % b] = quant(v("qd", 128 * b, 128 * b + 128), v("sd", 128 * b, 128 * b + 128), v("Ut", 3 - b, 515 - b))
+        sfill(v("Sp", 128 * b + 112, 128 * b + 120), 0.0)
     ts(v("rsa"), v("Js", 0, 112), 0.0, None, A.not_equal)
     quant(v("qo"), v("so"), v("Wt"))
-    for b in range(4):
-        quant(v("qd", 128 * b, 128 * b + 128), v("sd", 128 * b, 128 * b + 128), v("Ut", 512 * b, 512 * b + 512))
     sfill(v("Sp", 0, 1), BIG)
-    for e in range(4):
-        sfill(v("Sp", 128 * e + 112, 128 * e + 120), 0.0)
     sfill(v("sela", 112, 120), -STEPK)
     sfill(v("selb", 96, 104), -STEPK)
-    sfill(v("Kw", C, W), -BIG)
-    sfill(v("cod", 24, 64), 0.0)
+    sfill(v("Kw", C, 456), 0.0)
+    sfill(v("cod"), 0.0)
+    sfill(v("Zm", C, 480), 0.0)
     for q in range(2):
-        ts(v("tieb", 24 * q, 24 * q + 24), v("J", 0, 24), v("ni", q, q + 1), -TINY, A.is_lt, A.mult)
-    ts(v("rsb"), v("J", 0, 49), 24.0, None, A.not_equal)
-    ts(v("PR", 48, 49), P16, -8.0, 0.0, A.add, A.max)
-    ts(v("r4a"), v("J", 0, 4), PQ, 4 * TURN, A.is_equal, A.mult)
-    ts(v("r4b"), v("J", 0, 4), -1.0, PQ, A.add, A.is_equal)
-    ts(v("r4b"), v("r4b"), -TURN, None, A.mult)
+        ts(v("tieb", 25 - 25 * q, 49 - 25 * q), v("J", 0, 24), NK[q], TINY, A.is_lt, A.mult)
+        ts(v("maskk", 16 * q, 16 * q + 16), v("J", 16 * q, 16 * q + 16), NK[q], None, A.is_equal)
+    ts(v("rsb"), v("J", 0, 75), 25.0, None, A.not_equal)
+    sfill(v("dk", 24, 25), -1.0)
+    sfill(v("tieb", 24, 25), 0.0)
+    ts(v("LL", 24, 25), P16, 7.5, float(C), A.is_gt, A.mult)
+    ts(v("PR", 49, 75), v("J", 49, 75), 74.0, float(C), A.is_equal, A.mult)
+    ts(v("r4m"), v("Js", 0, 4), P4, -4 * BIG, A.not_equal, A.mult)
+    ts(v("r4a"), v("Js", 0, 4), PQ, 4 * HOLD, A.is_equal, A.mult)
+    ts(v("r4b"), v("Js", 0, 4), -1.0, PQ, A.add, A.is_equal)
+    ts(v("r4b"), v("r4b"), -HOLD, None, A.mult)
     tt(v("r4c"), v("r4a"), v("r4b"), A.add)
     for e in range(4):
         act(v("rb", e, C, 4), v("zer", 0, C // 4), ACT.Identity, bias=v("r4c", e, e + 1))
-    ts(v("ab", 0, 1), PQ, 3.0, TURN, A.is_lt, A.mult)
-    ts(v("ab", 0, 1), v("ab", 0, 1), -TURN / 2, None, A.add)
-    ts(v("ab", 1, 2), P4, 2 * TURN, None, A.add)
+    ts(v("m4"), v("rb", 0, 32), 1.0, -4 * BIG, A.is_lt, A.mult)
+    ts(v("ab", 0, 1), PQ, 3.0, 4 * HOLD, A.is_lt, A.mult)
+    tt(v("ab", 1, 2), v("ab", 0, 1), P4, A.add)
+    if not OPT["mirD"]:
+        ts(v("ab", 2, 3), v("ab", 0, 1), -2.0 * TURN, None, A.add)
+        ts(v("ab", 3, 4), P4, 2.0 * TURN, None, A.add)
+    lazy.update(range(constants, len(ops)))
     quant(v("qu"), v("su"), v("ut"))
-    record("V", lambda: g.vector.tensor_copy(T.qup[:, 0:256].bitcast(dt.uint32), T.qu[:, 0:128].bitcast(dt.uint32).indirect(T.ou[:, 0:16])),
-           [v("qup")], [v("qu"), v("ou")], 450)
-    act(v("sup"), ind(v("su"), v("ou")), ACT.Copy)
-    quant(v("qv"), v("sv"), v("vt"))
+    def pick(j):
+        return (record("V", lambda: g.vector.tensor_copy(T.qup[:, 128 * j:128 * j + 128].bitcast(dt.uint32),
+                                                         T.qu[:, 0:128].bitcast(dt.uint32).indirect(T.ou[:, 8 * j:8 * j + 8])),
+                       [v("qup", 128 * j, 128 * j + 128)], [v("qu"), v("ou")], 260),
+                act(v("sup", 128 * j, 128 * j + 128), ind(v("su"), v("ou", 8 * j, 8 * j + 8)), ACT.Copy))
+    picks = pick(0) + pick(1)
 
     def state_quant(r, part):
         a, b, k = PARTS[part]
-        qx, sx = v("qx%d" % r, a, b), v("sx%d" % r, a, b)
-        quant(qx, sx, v("X%d" % r, 4 * a, 4 * b))
-        first = len(ops) - 1
+        X, qx, sx = "X%d" % r, v("qx%d" % r, a, b), v("sx%d" % r, a, b)
+        m = OPT["cut"] if a and r and OPT["split"] else a
+        at["qC"] = quant(v(qx[0], a, m), v(sx[0], a, m), v(X, 4 * a, 4 * m)) if m > a else at.get("qC") if r else None
+        first = quant(v(qx[0], m, b), v(sx[0], m, b), v(X, 4 * m, 4 * b))
         if r == R:
             mm(bank(k, 0, b - a), v("qv"), v("sv"), qx, sx)
             return first, None
         remote(r, v("lq%d" % r, a, b), qx, "arr%d" % r, True, OPT["codes"])
         remote(r, v("ls%d" % r, a, b), sx, "arr%d" % r, False, OPT["codes"])
-        for j in range(2):
-            mm(bank(k + j, 0, b - a), v("qup", 128 * j, 128 * j + 128), v("sup", 128 * j, 128 * j + 128), qx, sx)
-        scan(v("Ms", a, b), v("rsM", a, b), bank(k, 0, b - a), BIG if a == 0 else 0.0, A.add, A.max)
-        second = len(ops) - 1
+        ahead["s" + part] = mm(bank(k, 0, b - a), v("qup", 0, 128), v("sup", 0, 128), qx, sx)
+        def planes():
+            for e in range(4):
+                s = 1 if a == 0 and e == 0 else 0
+                ahead["P%s%d" % (part, e)] = act(v("Sp", 128 * e + a // 4 + s, 128 * e + b // 4), bank(k, e + 4 * s, b - a, 4), ACT.Copy)
+        if a and r and OPT["pf"]:
+            planes()
+        ahead["n" + part] = tt(v("Mq", a, min(b, 192)), bank(k, 0, min(b, 192) - a), v("mneg", a, min(b, 192)), A.add)
+        ahead["m" + part] = scan(v("Ms", a, b), v("rsM", a, b), bank(k, 0, b - a), BIG if a == 0 else 0.0, A.add, A.max)
+        if not (a and r and OPT["pf"]):
+            planes()
         for e in range(4):
-            s = 1 if a == 0 and e == 0 else 0
-            act(v("Sp", 128 * e + a // 4 + s, 128 * e + b // 4), bank(k, e + 4 * s, b - a, 4), ACT.Copy)
-        act(v("Kw", a, b), bank(k + 1, 0, b - a), ACT.Copy)
-        return first, second
+            if OPT["mirX"]:
+                ahead["x%s%d" % (part, e)] = move(OPT["mirX"], mirror(X, e, a, b), v(X, 4 * a + e, 4 * b, 4))
+            if OPT["tsplit"] or not a:
+                z = b if OPT["tsplit"] else C
+                ahead["T%s%d" % (part, e)] = act(v("Tm", a + e, z, 4), v("Sp", 128 * e + a // 4, 128 * e + z // 4), ACT.Identity, bias=v("r4m", e, e + 1))
+        if OPT["k2"]:
+            ahead["k" + part + "m"] = mm(bank(k + 1, 0, b - a), v("qup", 128, 256), v("sup", 128, 256), qx, sx)
+            ahead["K" + part] = act(v("Kw", a, b), bank(k + 1, 0, b - a), ACT.Copy)
+        elif a == 0:
+            ahead["sK"] = mm(bank(1, 0, C), v("qup", 128, 256), v("sup", 128, 256), v(qx[0]), v(sx[0]))
+            ahead["KB"] = act(v("Kw", 0, C), bank(1, 0, C), ACT.Copy)
+        return first, ahead["m" + part]
 
     def part_of(src, c0, c1):
         return (src[0], src[1] + src[2] * c0, src[1] + src[2] * (c1 - 1) + 1, src[2])
@@ -259,7 +316,7 @@ def rank_program(g, core, T, topo):
 
     BLOCKS, COLUMNS = ("Ms", 3, 4), ("Cd", 0, 1)
 
-    def select(src, halves, cuts, on_scalar, F, sel, w, vals):
+    def select(src, mine, halves, cuts, on_scalar, F, sel, w, vals):
         nq = len(halves[0]) + len(halves[1]) - 1
         n = 16 * nq
 
@@ -268,120 +325,147 @@ def rank_program(g, core, T, topo):
             o = 512 * h + halves[h].index(q)
             return v(F, o + 4 * c0, o + 4 * (c1 - 1) + 1, 4)
         for q in range(nq):
-            me = v("own", 16 * q + 15, 16 * q + 16)
-            act(v("dd", 16 * q, 16 * q + 16), part_of(src, 16 * q, 16 * q + 16), ACT.Identity, bias=me, scale=-1.0)
-            lo = cuts if 16 * q > cuts else 0
-            if lo:
-                ts(slot(q, 0, lo), part_of(src, 0, lo), me, None, A.is_lt)
+            me = mine(q)
+            at[F + "D%d" % q] = act(v("dd", 16 * q, 16 * q + 16), part_of(src, 16 * q, 16 * q + 16), ACT.Identity, bias=me, scale=-1.0)
+            lo = cuts if 16 * q >= cuts else 0
+            if lo and q in OPT["la"] and on_scalar is OPT["sa"]:
+                at[F + "B%d" % q] = act(v("sh", lo * (6 - q), lo * (7 - q)), part_of(src, 0, lo), ACT.Sign, bias=me, scale=-1.0)
+                at[F + "E%d" % q] = act(slot(q, 0, lo), v("sh", lo * (6 - q), lo * (7 - q)), ACT.Relu)
+            elif lo:
+                at[F + "b%d" % q] = ts(slot(q, 0, lo), part_of(src, 0, lo), me, None, A.is_lt)
             if q in on_scalar:
                 o = 112 * on_scalar.index(q)
                 hi = n if q < nq - 1 else n - 16
                 l2 = lo if 16 * q > lo else 16 * q + 16
-                act(v("sg", o + l2, o + hi), part_of(src, l2, hi), ACT.Sign, bias=me, scale=-1.0)
+                at[F + "S%d" % q] = act(v("sg", o + l2, o + hi), part_of(src, l2, hi), ACT.Sign, bias=me, scale=-1.0)
                 if 16 * q > lo:
-                    act(slot(q, lo, 16 * q), v("sg", o + lo, o + 16 * q), ACT.Relu)
+                    at[F + "L%d" % q] = act(slot(q, lo, 16 * q), v("sg", o + lo, o + 16 * q), ACT.Relu)
                 if q < nq - 1:
-                    act(slot(q, 16 * q + 16, n), v("sg", o + 16 * q + 16, o + n), ACT.Sign, bias=1.0)
+                    at[F + "G%d" % q] = act(slot(q, 16 * q + 16, n), v("sg", o + 16 * q + 16, o + n), ACT.Sign, bias=1.0)
                 continue
             if 16 * q > lo:
-                ts(slot(q, lo, 16 * q), part_of(src, lo, 16 * q), me, None, A.is_lt)
+                at[F + "l%d" % q] = ts(slot(q, lo, 16 * q), part_of(src, lo, 16 * q), me, None, A.is_lt)
             if q < nq - 1:
-                ts(slot(q, 16 * q + 16, n), part_of(src, 16 * q + 16, n), me, None, A.is_le)
+                at[F + "g%d" % q] = ts(slot(q, 16 * q + 16, n), part_of(src, 16 * q + 16, n), me, None, A.is_le)
         for c0, c1 in ((cuts, n), (0, cuts)):
             if c1 > c0:
-                tt(slot("tie", c0, c1), v("dd", c0, c1), v("tie", c0, c1), A.is_gt)
+                at[F + "t%d" % (c0 > 0)] = tt(slot("tie", c0, c1), v("dd", c0, c1), v("tie", c0, c1), A.is_gt)
         for h in range(2):
-            quant(v("qf", 128 * h, 128 * h + 128), v("sf", 128 * h, 128 * h + 128), v(F, 512 * h, 512 * h + 512))
-            mm(bank(3, 0, 128), v("qo"), v("so"), v("qf", 128 * h, 128 * h + 128), v("sf", 128 * h, 128 * h + 128), h == 0, h == 1)
-        ts(v(sel, 0, n), bank(3, 0, n), 23.5, -STEPK, A.is_lt, A.mult)
+            at[F + "pq"[h]] = quant(v("qf", 128 * h, 128 * h + 128), v("sf", 128 * h, 128 * h + 128), v(F, 512 * h, 512 * h + 512))
+            at[F + "m%d" % h] = mm(bank(3, 0, 128), v("qo"), v("so"), v("qf", 128 * h, 128 * h + 128), v("sf", 128 * h, 128 * h + 128), h == 0, h == 1)
+        at[F + "s"] = ts(v(sel, 0, n), bank(3, 0, n), 23.5, -STEPK, A.is_lt, A.mult)
         for q in range(2):
-            scan(v("Rp", 128 * q + 1, 128 * q + w), v(sel, 0, w - 1), v("zer", 0, w - 1), v("kn", q, q + 1), A.add, A.max)
+            at[F + "r%d" % q] = scan(v("Rp", 128 * q + 1, 128 * q + w), v(sel, 0, w - 1), v("zer", 0, w - 1), v("Rp", 128 * q, 128 * q + 1), A.add, A.max)
         for q in range(2):
-            scan(v("cap", 128 * q, 128 * q + w), v("Rp", 128 * q, 128 * q + w), v(vals, 0, w), 0.0, A.add, A.min)
+            at[F + "c%d" % q] = scan(v("cap", 128 * q, 128 * q + w), v("Rp", 128 * q, 128 * q + w), v(vals, 0, w), 0.0, A.add, A.min)
         return v("cap", w - 1, w + 128, 128)
 
-    RUNS = ((K, K + 128, 0), (K + 128, C, 4), (0, K, 0))
+    RUNS = ((K, OPT["cut"], 0), (OPT["cut"], C, 4), (0, K, 0))
 
     def order(r):
-        for c0, c1 in ((48, 112), (0, 48)):
-            tt(v("Mm", c0, c1), part_of(BLOCKS, c0, c1), v("mask", c0, c1), A.mult)
-            owned(c0, c1)
-        cp(v("offa"), select(BLOCKS, ((3, 4, 5, 6), (0, 1, 2, "tie")), 48, OPT["sa"], "Fa", "sela", 120, "Jb"))
+        at["kA"] = tt(v("Mm", 48, 112), part_of(BLOCKS, 48, 112), v("mask", 48, 112), A.mult)
+        at["oA"] = scan(v("own", 48, 112), v("rsa", 48, 112), v("Mm", 48, 112), 0.0, A.mult, A.add)
+        at["oB"] = scan(v("ownq"), v("rsQ"), v("Mq"), 0.0, A.add, A.max)
         for e in range(4):
-            i = ind(v("Sp", 128 * e, 128 * e + 120), v("offa"))
-            tt(v("Mm", e, 128, 4), i, v("mask", e, 128, 4), A.mult)
-            act(v("Cd", e, 128, 4), i, ACT.Copy)
+            c = e * C // 4
+            at["z%d" % e] = scan(v("Zm", c, c + C // 4), v("rsM", c, c + C // 4), v("Tm", c, c + C // 4), -4 * BIG, A.add, A.max)
+        at.update(ahead)
+        blocks = select(BLOCKS, lambda q: v("own", 16 * q + 15, 16 * q + 16) if q > 2 else v("ownq", 64 * q + 63, 64 * q + 64),
+                        ((3, 4, 5, 6), (0, 1, 2, "tie")), 48, OPT["sa" if r else "sa0"], "Fa", "sela", 120, "Jb")
+        at["oz"] = ts(v("offz"), blocks, 4.0, 3.0, A.mult, A.add)
+        at["oa"] = cp(v("offa"), blocks)
+        at["mc"] = tt(v("Mc"), ind(v("Zm"), v("offz")), v("m4"), A.add)
+        at["ow"] = scan(v("ownc"), v("rsM", 0, 24), v("Mc", 0, 24), -4 * BIG, A.add, A.max)
         for e in range(4):
-            act(v("cc", e, 128, 4), ind(v("J", 0, 128), v("offa")), ACT.Identity, bias=e - MID, scale=4.0)
-        owned(0, 96)
-        heads = select(COLUMNS, ((1, 2, 3, 4), (0, 5, "tie")), 0, OPT["sb"], "Fb", "selb", 104, "cc")
-        ts(v("offb"), heads, MID, None, A.add)
-        ts(v("offp"), heads, MID - 1, None, A.add)
+            at["c%d" % e] = move("V" if e < OPT["cd"] else "S", v("Cd", e, 128, 4), ind(v("Sp", 128 * e, 128 * e + 120), v("offa")))
+        for e in range(4):
+            at["C%d" % e] = act(v("cc", e, 128, 4), ind(v("J", 0, 128), v("offa")), ACT.Identity, bias=e - MID, scale=4.0)
+        heads = select(COLUMNS, lambda q: v("ownc", 4 * q + 3, 4 * q + 4), ((1, 2, 3, 4), (0, 5, "tie")), 0, OPT["sb"], "Fb", "selb", 104, "cc")
+        at["ob"] = ts(v("offb"), heads, MID, None, A.add)
+        at["op"] = ts(v("offp"), heads, MID - 1, None, A.add)
         arrival(r, [v("lq%d" % r), v("ls%d" % r)], "arr%d" % r)
         for b in range(4):
-            mm(bank(4 + b, 0, C), v("qd", 128 * b, 128 * b + 128), v("sd", 128 * b, 128 * b + 128), v("lq%d" % r), v("ls%d" % r))
-            act(v("Dp", b, 4 * C, 4), bank(4 + b, 0, C), ACT.Copy)
-        tt(v("km"), ind(v("Kw"), v("offb")), v("mask", 0, 32), A.mult)
+            at["n%d" % b] = mm(bank(4 + b, 0, C), v("qd", 128 * b, 128 * b + 128), v("sd", 128 * b, 128 * b + 128), v("lq%d" % r), v("ls%d" % r))
+            at["D%d" % b] = act(v("Dp", b, 4 * C, 4), bank(4 + b, 0, C), ACT.Copy)
+            for h in range(2 if OPT["mirD"] else 0):
+                c = h * C // 2
+                at["d%d%d" % (b, h)] = cp(mirror("Dp", b, c, c + C // 2), v("Dp", 4 * c + b, 4 * c + 2 * C, 4))
+        at["km"] = tt(v("km"), ind(v("Kw"), v("offb")), v("maskk"), A.mult)
         cp(v("key"), ind(v("Kw"), v("offb")))
-        act(v("Ha"), ind(v("J"), v("offb")), ACT.Copy)
-        act(v("kp"), ind(v("Kw"), v("offp")), ACT.Copy)
-        act(v("Wb"), ind(v("J"), v("offb")), ACT.Identity, bias=TURN + 1, scale=-1.0)
+        at["H"] = act(v("Ha"), ind(v("J"), v("offb")), ACT.Copy)
+        at["KP"] = act(v("kp"), ind(v("Kw"), v("offp")), ACT.Copy)
+        at["WB"] = act(v("Wb"), ind(v("J"), v("offb")), ACT.Identity, bias=TURN + 1.0, scale=-1.0)
         scan(v("ko"), v("rsa", 0, 32), v("km"), 0.0, A.mult, A.add)
         for q in range(2):
-            tt(v("LL", 24 * q, 24 * q + 24), v("Ha", 1, 25), v("Ha", 0, 24), A.subtract)
-            ts(v("dk", 24 * q, 24 * q + 24), v("key", 0, 24), v("ko", 16 * q + 15, 16 * q + 16), None, A.subtract)
+            o = 25 - 25 * q
+            tt(v("LL", o, o + 24), v("Ha", 1, 25), v("Ha", 0, 24), A.subtract)
+            if q:
+                at["DK"] = act(v("dk", o, o + 24), v("key", 0, 24), ACT.Identity, bias=v("ko", 16 * q + 15, 16 * q + 16), scale=-1.0)
+            else:
+                at["dk"] = ts(v("dk", o, o + 24), v("key", 0, 24), -1.0, v("ko", 16 * q + 15, 16 * q + 16), A.mult, A.add)
         tt(v("turn"), v("key", 0, 24), v("kp", 1, 25), A.is_lt)
-        tt(v("FL"), v("dk"), v("tieb"), A.is_gt)
+        at["fl"] = tt(v("FL"), v("dk"), v("tieb"), A.is_lt)
         tt(v("ca"), v("turn"), v("Wb", 1, 25), A.mult)
-        tt(v("PR", 0, 48), v("FL"), v("LL"), A.mult)
-        tt(v("cod", 0, 24), v("ca"), v("Ha", 0, 24), A.max)
-        scan(v("Pp"), v("rsb"), v("PR"), 0.0, A.mult, A.add)
+        at["pr"] = tt(v("PR", 0, 49), v("FL"), v("LL"), A.mult)
+        tt(v("cod", 16, 40), v("ca"), v("Ha", 0, 24), A.max)
+        at["pp"] = scan(v("Pp"), v("rsb"), v("PR"), 0.0, A.mult, A.add)
+        at["oc"] = cp(v("offc", 0, 3), v("Pp", 74, 23, -25))
         for h in range(2):
-            ts(v("offc", 2 * h, 2 * h + 2), v("Pp", 23, 49, 25), float(W * h), None, A.add)
-            sfill(v("Ww", W * h, W * h + W), 1.0)
-        cp(ind(v("Ww"), v("offc")), v("cod"))
-        if OPT["usplit"]:
-            scan(v("us", 0, K), v("Ww", W, W + K), v("Ww", 0, K), 0.0, A.mult, A.add)
-            scan(v("us", K, C), v("Ww", W + K, W + C), v("Ww", K, C), v("us", K - 1, K), A.mult, A.add)
-        else:
-            scan(v("us"), v("Ww", W, W + C), v("Ww", 0, C), 0.0, A.mult, A.add)
-        for a, b, k in [RUNS[i] for i in OPT["wr"]]:
-            scan(v("wr", a, b), v("rb", a, b), v("us", a, b), 0.0, A.add, A.min)
-            row("wr")
-            act(v("oo", a // 4, b // 4), v("wr", a + 3, b, 4), ACT.Abs, bias=v("ab", 0, 1))
-            ts(v("ord%d" % r, a // 4, b // 4), v("oo", a // 4, b // 4), -4.0, v("ab", 1, 2), A.mult, A.add)
+            at["W%d" % h] = sfill(v("Ww", C * h, C * h + C), 1.0)
+        at["sc"] = cp(ind(v("Ww"), v("offc", 0, 3)), v("cod"))
+        cut = OPT["cut"]
+        at["u0"] = scan(v("us", 0, cut), v("Ww", C, C + cut), v("Ww", 0, cut), 0.0, A.mult, A.add)
+        at["u1"] = scan(v("us", cut, C), v("Ww", C + cut, 2 * C), v("Ww", cut, C), v("us", cut - 1, cut), A.mult, A.add) if cut < C else None
+        for i, (a, b, k) in enumerate(RUNS):
+            at["w%d" % i] = scan(v("wr", a, b), v("rb", a, b), v("us", a, b), 0.0, A.add, A.min)
+            if OPT["mirX" if a else "mirD"]:
+                at["t%d" % i] = ts(v("ord%d" % r, a // 4, b // 4), v("wr", a + 3, b, 4), 4.0, v("ab", 1, 2), A.mult, A.add)
+            else:
+                at["A%d" % i] = act(v("oo", a // 4, b // 4), v("wr", a + 3, b, 4), ACT.Abs, bias=v("ab", 2, 3), scale=4.0)
+                at["t%d" % i] = ts(v("ord%d" % r, a // 4, b // 4), v("oo", a // 4, b // 4), -1.0, v("ab", 3, 4), A.mult, A.add)
         remote(r, v("lst%d" % r), v("ord%d" % r, 0, K // 4), "lis%d" % r, False, OPT["list"])
         arrival(r, [v("lst%d" % r)], "lis%d" % r)
 
+
     def layer(r):
         X, Y = "X%d" % r, "X%d" % (r + 1)
-        at = {}
         for i, (a, b, k) in enumerate(RUNS):
-            n = OPT["g"][i]
-            win, lst = (v(X), "ord%d" % r) if a else (v("Dp"), "lst%d" % r)
-            cp(v("Et", 4 * a, 4 * (a + n)), ind(win, v(lst, a // 4, (a + n) // 4)))
-            act(v("Et", 4 * (a + n), 4 * b), ind(win, v(lst, (a + n) // 4, b // 4)), ACT.Copy)
-            quant(v("qe", a, b), v("se", a, b), v("Et", 4 * a, 4 * b))
-            at.update({"g%d" % i: len(ops) - 3, "G%d" % i: len(ops) - 2, "q%d" % i: len(ops) - 1})
+            win, lst = (v(X, 0, 8 * C if OPT["mirX"] else 4 * C), "ord%d" % r) if a else (v("Dp", 0, 8 * C if OPT["mirD"] else 4 * C), "lst%d" % r)
+            m = [a, a + OPT["g"][i], b - OPT["h"][i], b]
+            for name, q, c0, c1 in zip("gGI", "VSS", m, m[1:]):
+                at["%s%d" % (name, i)] = move(q, v(Y, 4 * c0, 4 * c1), ind(win, v(lst, c0 // 4, c1 // 4))) if c1 > c0 else None
+            at["q%d" % i] = quant(v("qe", a, b), v("se", a, b), v(Y, 4 * a, 4 * b))
             for j in range(4):
-                mm(bank(k + j, 0, b - a), v("qw", 128 * j, 128 * j + 128), v("sw", 128 * j, 128 * j + 128), v("qe", a, b), v("se", a, b))
-                row("products")
-                act(v("Rr", C * j + a, C * j + b), bank(k + j, 0, b - a), ACT.Relu, scale=0.015625)
-                tt(v(Y, 4 * a + j, 4 * b, 4), v("Et", 4 * a + j, 4 * b, 4), v("Rr", C * j + a, C * j + b), A.add)
-                at.update({"R%d%d" % (i, j): len(ops) - 2, "a%d%d" % (i, j): len(ops) - 1})
+                at["m%d%d" % (i, j)] = mm(bank(k + j, 0, b - a), v("qw", 128 * j, 128 * j + 128), v("sw", 128 * j, 128 * j + 128), v("qe", a, b), v("se", a, b))
+                at["R%d%d" % (i, j)] = act(v("Rr", 4 * a + j, 4 * b, 4), bank(k + j, 0, b - a), ACT.Relu, scale=0.015625)
+                if i == 0 and OPT["dadd"]:
+                    at["a%d%d" % (i, j)] = None
+                else:
+                    at["a%d%d" % (i, j)] = tt(v(Y, 4 * a + j, 4 * b, 4), v(Y, 4 * a + j, 4 * b, 4), v("Rr", 4 * a + j, 4 * b, 4), A.add)
+            if i == 0 and OPT["dadd"]:
+                add_by_dma(v(Y, 4 * a, 4 * b), v("Rr", 4 * a, 4 * b))
             if b == C:
-                at["qA"], at["mA"] = state_quant(r + 1, "A")
-        at["qB"], at["mB"] = state_quant(r + 1, "B")
-        for names in (OPT["V"], OPT["S"]):
-            names = [at[w] for w in names.split() if at[w] is not None]
-            for o, me in zip(names, names[1:]):
-                ops[me]["behind"].add(o)
+                at["qA"] = state_quant(r + 1, "A")[0]
+        at["qB"] = state_quant(r + 1, "B")[0]
 
-    state_quant(0, "A")
-    state_quant(0, "B")
+    def add_by_dma(y, x):
+        dma("G", lambda: ap(y), lambda: ap(x), [y], [y, x], OPT["dlat"], accum_op=A.add)
+
+    a0, b0 = state_quant(0, "A"), state_quant(0, "B")
+    at.update({"pu": picks[0], "PU": picks[1], "pk": picks[2], "PK": picks[3], "fA": a0[0], "fB": b0[0]})
     for r in range(R):
         order(r)
+        if r == 0:
+            late_loads()
         layer(r)
+        named.append(dict(at))
+        at.clear()
+    for r in range(R):
+        for names in (OPT["V"], OPT["S"], OPT["P"]):
+            calls = [(named + [{}])[r + 1].get(w[1:]) if w[0] == "+" else named[r].get(w) for w in names.split()]
+            row([o for o in calls if o is not None])
+    for names in (OPT["V0"], OPT["S0"], OPT["P0"]):
+        row([named[0][w] for w in names.split() if w in named[0]])
     QL, SL = "qx%d" % R, "sx%d" % R
     act(v("ola"), v("us"), ACT.Abs, bias=-TURN / 2)
     act(v("olt"), v("ola"), ACT.Identity, bias=TURN / 2, scale=-1.0)
@@ -390,10 +474,7 @@ def rank_program(g, core, T, topo):
     def store(part):
         a, b, k = PARTS[part]
         dma("Y" if a else "S", lambda: T.oc[:, 4 * a:4 * b], lambda: T[QL][:, a:b].bitcast(dt.uint8), [], [v(QL, a, b)])
-        if a:
-            act(v("yt", a, b), bank(k, 0, b - a), ACT.Copy)
-        else:
-            cp(v("yt", a, b), bank(k, 0, b - a))
+        move("S" if a else "V", v("yt", a, b), bank(k, 0, b - a))
         dma("Y", lambda: T.y[:, a:b], lambda: T.yt[:, a:b], [], [v("yt", a, b)])
 
     def scales(k):
@@ -404,6 +485,7 @@ def rank_program(g, core, T, topo):
         scales(k)
 
     wait = OPT["wait"]
+    QUEUES, every = list(queue) + ["-"], range(len(ops))
     users = [[] for _ in ops]
     for me, op in enumerate(ops):
         for o in op["deps"] | op["behind"]:
@@ -411,35 +493,32 @@ def rank_program(g, core, T, topo):
 
     def gap(o, me):
         if o in ops[me]["deps"]:
-            return ops[o]["done"] + wait
+            return ops[o]["done"] + wait + (OPT["lazy"] if o in lazy and me not in lazy else 0.0)
         return ops[o]["done"] if ops[me]["q"] == "-" else ops[o]["hold"]
+
     def lay(turn, before, least, first):
         at, busy = {}, {q: [] for q in QUEUES}
         for me in turn:
             t = max([first(me)] + [at[o] + least(o, me) for o in before(me)])
             taken, hold = busy[ops[me]["q"]], ops[me]["hold"]
-            i = 0
+            i = len(taken)
+            while i and taken[i - 1][1] > t:
+                i -= 1
             while i < len(taken) and taken[i][0] < t + hold - 1e-9:
                 t = max(t, taken[i][1])
                 i += 1
             taken.insert(i, (t, t + hold))
             at[me] = t
         return at
-    QUEUES, every = list(queue) + ["-"], range(len(ops))
+    missing = [len(op["deps"] | op["behind"]) for op in ops]
+    sort = [o for o in every if not missing[o]]
+    for o in sort:
+        for u in users[o]:
+            missing[u] -= 1
+            if not missing[u]:
+                sort.append(u)
+    assert len(sort) == len(ops)
     tail = [0.0] * len(ops)
-    sort, seen = [], set()
-    for me in every:
-        stack = [me]
-        while stack:
-            o = stack[-1]
-            todo = [x for x in ops[o]["deps"] | ops[o]["behind"] if x not in seen]
-            if todo:
-                stack.extend(todo)
-                continue
-            stack.pop()
-            if o not in seen:
-                seen.add(o)
-                sort.append(o)
     for me in reversed(sort):
         tail[me] = max([ops[me]["done"]] + [gap(me, u) + tail[u] for u in users[me]])
     turn, best = sorted(every, key=lambda o: (-tail[o], o)), None
@@ -457,13 +536,22 @@ def rank_program(g, core, T, topo):
     def line(o):
         return ops[o]["q"] if ops[o]["sem"] is None else ops[o]["sem"]
     known = {q: {} for q in QUEUES}
-    waited = set()
+    waited, wanted = set(), {}
+    for op in ops:
+        for o in op["deps"]:
+            if ops[o]["sem"] is None:
+                wanted.setdefault((op["q"], ops[o]["q"]), set()).add(o)
     for me in issue:
         op = ops[me]
         kn, need = known[op["q"]], {}
         for o in op["deps"]:
             if ops[o]["sem"] != "none":
                 need[line(o)] = max(need.get(line(o), -1), place[o])
+        for l in need:
+            if kn.get(l, -1) < need[l]:
+                spare = OPT["spare"][0 if l == op["q"] else 1]
+                need[l] = max([need[l]] + [place[o] for o in wanted.get((op["q"], l), ())
+                                           if best[1][o] + ops[o]["done"] + wait + spare <= best[1][me]])
         op["waits"] = []
         for i in sorted(need.values(), reverse=True):
             o = issue[i]

from concourse.mybir import dt, AluOpType, ActivationFunctionType
C, K, R = 448, 160, 3
STEP = [1, 2, 1]
F32, BF, I32, U16, U8, X4 = "float32", "bfloat16", "int32", "uint16", "uint8", "float8_e4m3fn_x4"
BIG, TINY, STEPK, TURN, HOLD, MID = 2.0 ** 96, 1e-32, 512.0, 2 * C - 1, 1024.0, 228.0
_SB = {}
for _d, _l in ((BF, "ut512 vt512 Dp3584 Js128 Jg128 Jq192 Jb128 mask128 maskk32 rsa112 rsb75 rs_448 m_32 rsM448 rsQ192 mneg192 zer512 ident128 blk128 Wt512 "
                    "Ut516 sg448 sh192 Fa1024 Fb1024 sela120 selb104 Rp256 cap256 cc128 rb448 dd112 tie112 dk49 tieb49 pb4"),
               (X4, "qu128 qup256 qv128 qw512 qe448 qo128 qd512 qf256"), (U8, "su128 sup256 sv128 sw512 se448 so128 sd512 sf256"),
               (I32, "pint2 iint4 oui16"), (U16, "ou16 offa2 offz2 offb2 offp2 offc4"),
               (F32, "Rr1792 pf2 fi4 ni2 nk2 kn2 r4a4 r4b4 r4c4 ab4 J464 Ms448 Mq192 Mm128 own112 ownq192 Sp512 Kw456 Cd128 key32 kp32 Ha32 Wb32 "
                     "km32 ko32 LL49 FL49 PR75 turn24 ca24 cod48 Pp75 r4m4 Tm448 Zm480 Mc32 ownc24 Ww896 us448 wr448 oo112 ola448 olt448 yt448")):
    for _w in _l.split():
        _n = _w.rstrip("0123456789")
        _SB[_n.replace("_", "4")] = (int(_w[len(_n):]), _d)
for _r in range(R + 1):
    _SB.update({"X%d" % _r: (8 * C if _r < R else 4 * C, BF), "qx%d" % _r: (C, X4), "sx%d" % _r: (C, U8)})
for _r in range(R):
    _SB.update({"lq%d" % _r: (C, X4), "ls%d" % _r: (C, U8), "lst%d" % _r: (K // 4, U16), "ord%d" % _r: (C // 4, U16)})
_IN = {}
for _b, _l in (("small", "pf fi ni nk kn r4a r4b r4c r4m ab"), ("runs", "key kp Ha Wb km ko turn ca")):
    _SB[_b] = (0, F32)
    for _n in _l.split():
        _IN[_n] = (_b, _SB[_b][0])
        _SB[_b] = (_SB[_b][0] + (_SB[_n][0] + 7) // 8 * 8, F32)
SCRATCH = {k: ("sbuf", [128, n], d) for k, (n, d) in _SB.items() if k not in _IN}
SCRATCH["ps"] = ("psum", [128, 4096], F32)
SEMAPHORES = (["sV", "sS", "sP", "sG", "sent"] + ["dm%d" % i for i in range(24)]
              + ["arr%d" % r for r in range(R)] + ["lis%d" % r for r in range(R)])
CYCLE, WAIT, LOAD, LIST, CODES = 1e-3, 0.2, 2.0, 1.8, 4.0
OPT = {"g": (56, 72, 48), "h": (0, 0, 0), "lazy": 0.0, "split": 1, "fv": "", "cyc": CYCLE, "load": LOAD, "spare": (99, 99), "sest": 0, "pest": 1.3, "k2": 0, "tsplit": 1, "la": (), "pf": 0,
       "V": "Faq xA0 xA1 z3 z2 Fas z1 Far0 Far1 z0 Fac0 Fac1 xB0 oz oa xB1 mc c0 c1 ow Fbl1 Fbg1 Fbl2 Fbg2 Fbl3 Fbg3 Fbl4 Fbg4 Fbg0 Fbt0 Fbp Fbq "
            "xA2 xA3 xB2 xB3 Fbs e0 Fbr0 Fbr1 e1 Fbc0 Fbc1 e2 ob op km e3 dk fl pr pp d00 oc d01 sc d10 "
            "u0 d11 d20 w0 w2 u1 t0 t2 w1 g0 t1 d21 q0 g1 d30 d31 q1 a00 a01 a02 a03 g2 a10 q2 a11 a12 a13 qC a20 qA a21 a22 a23 "
            "+mA qB +kA +nA +oA +nB +mB +oB +Fab3 +Fab4 +Fab5 +Fab6 +Fag0 +Fag1 +Fal1 +Fal2 +Fag2 +Fat1 +Fat0 +Fap",
       "S": "TB0 TB1 TB2 TB3 KB c2 c3 C0 C1 FbD0 FbD1 FbD2 FbD3 FbD4 FbD5 FbS5 C2 FbL5 C3 H KP WB DK D0 D1 D2 D3 "
            "G0 G1 R00 R01 R02 R03 R10 G2 R11 R12 R13 +W0 R20 R21 R22 R23 +W1 +PA0 +PA1 +PA2 +FaS3 +FaS4 +FaS5 +FaS6 +FaD3 +FaD4 +FaD5 +FaD6 "
            "+FaG3 +FaL4 +FaG4 +FaL5 +FaD0 +FaD1 +FaD2 +FaG5 +FaL6 +PA3 +TA0 +TA1 +TA2 +TA3 +PB0 +PB1 +PB2 +PB3",
       "V0": "pu fA fB pk mA nA nB kA mB oB oA Fag0 Fag1 Fal1 Fal2 Fag2 Fab3 Fab4 Fab5 Fab6 Fag3 Fal4 Fag4 Fat0 Fat1 Fap Faq",
       "S0": "PU PK PA0 PA1 PA2 PA3 TA0 TA1 TA2 TA3 FaD0 FaD1 FaD2 FaS5 FaS6 FaD3 FaD4 FaD5 FaD6 FaL5 FaG5 FaL6 PB0 PB1 PB2 PB3 TB0",
       "P": "Fam0 Fam1 Fbm0 Fbm1 n0 n1 n2 n3 m00 m01 m02 m03 m10 m11 m12 m13 m20 m21 m22 m23 +sA +sB +sK +Fam0",
       "P0": "sA sB sK Fam0",
       "sa0": (5, 6), "sa": (3, 4, 5, 6), "sb": (5,), "cd": 2, "dkS": 1, "cut": K + 128, "wait": WAIT, "list": LIST, "codes": CODES,
       "passes": 3, "dadd": 0, "mirD": "V", "mirX": "V", "dlat": 2.0}


def rank_program(g, core, T, topo):
    rank = T.rank_of(core)
    if rank is None:
        return
    A, ACT = AluOpType, ActivationFunctionType
    CYCLE, LOAD = OPT["cyc"], OPT["load"]
    queue = {"V": g.vector, "S": g.scalar, "P": g.tensor, "G": g, "Y": g.sync}
    ops, acc, ndma, sent, writes, lazy = [], {}, [0], [0], {}, set()

    def v(name, a=0, b=None, s=1):
        buf, o = _IN.get(name, (name, 0))
        return (buf, o + a, o + (_SB[name][0] if b is None else b), s)

    def bank(k, a, b, s=1):
        return ("ps", 512 * k + a, 512 * k + b, s)

    def ind(w, o):
        return ("@", w, o)

    def ap(x):
        if not isinstance(x, tuple):
            return x
        if x[0] == "@":
            return ap(x[1]).indirect(ap(x[2]))
        return T[x[0]][:, x[1]:x[2]] if x[3] == 1 else T[x[0]][:, x[1]:x[2]:x[3]]

    def size(x):
        return 16 * size(x[2]) if x[0] == "@" else len(range(x[1], x[2], x[3]))

    def bits(x):
        if x[0] == "ps":
            return 1 << (x[1] // 512)
        n, s = size(x), abs(x[3])
        return ((1 << s * n) - 1) // ((1 << s) - 1) << min(x[1], x[1] + x[3] * (n - 1))

    def cycles(o, ins, per=None):
        views = [x for x in [o] + ins if isinstance(x, tuple)]
        if o[0] == "@":
            return 60 + 4 * size(o)
        if any(x[0] == "@" for x in views):
            return 70 + 1.5 * size(o)
        if per is None:
            per = 0.5 if all(x[0] != "ps" and _SB[x[0]][1] in (BF, U16) for x in views) else 1
        return max(64, per * size(o))

    def record(q, fn, outs, ins, hold, sem=None, count=0, done=None, after=()):
        rd, wr = [], []
        for x in ins:
            if isinstance(x, tuple):
                rd.extend([x[1], x[2]] if x[0] == "@" else [x])
        for x in outs:
            if x[0] == "@":
                wr.append(x[1])
                rd.append(x[2])
            else:
                wr.append(x)
        me, deps, behind = len(ops), set(), set(after)
        for lst, w in ((rd, False), (wr, True)):
            for x in lst:
                m = bits(x)
                for (o, m2, w2) in acc.get(x[0], []):
                    if m & m2:
                        if ops[o]["q"] != q if x[0] == "ps" else w or w2:
                            deps.add(o)
                        elif w:
                            behind.add(o)
        for lst, w in ((rd, False), (wr, True)):
            for x in lst:
                acc.setdefault(x[0], []).append((me, bits(x), w))
        ops.append({"q": q, "fn": fn, "deps": deps, "behind": behind, "sem": sem, "count": count, "hold": hold * CYCLE,
                    "done": hold * CYCLE if done is None else done})
        return me

    def row(calls):
        for o, me in zip(calls, calls[1:]):
            ops[me]["behind"].add(o)

    def ts(o, i, s1, s2, *op):
        return record("V", lambda: g.vector.tensor_scalar(ap(o), ap(i), ap(s1), ap(s2), *op), [o], [i, s1, s2], cycles(o, [i, s1, s2]))

    def tt(o, a, b, op):
        return record("V", lambda: g.vector.tensor_tensor(ap(o), ap(a), ap(b), op), [o], [a, b], cycles(o, [a, b], 1 if a[0] == "ps" else 2))

    def cp(o, i):
        return record("V", lambda: g.vector.tensor_copy(ap(o), ap(i)), [o], [i], cycles(o, [i]))

    def scan(o, d0, d1, init, op0, op1):
        return record("V", lambda: g.vector.tensor_tensor_scan(ap(o), ap(d0), ap(d1), ap(init), op0, op1), [o], [d0, d1, init], cycles(o, [d0, d1]))

    def fill(o, c):
        return record("V", lambda: g.vector.memset(ap(o), c), [o], [], cycles(o, []))

    def quant(q, s, i):
        return record("V", lambda: g.vector.quantize_mx(ap(q), ap(s), ap(i)), [q, s], [i], 15 + size(q))

    def act(o, i, f, bias=None, scale=None):
        kw = {}
        if bias is not None:
            kw["bias"] = ap(bias)
        if scale is not None:
            kw["scale"] = ap(scale)
        return record("S", lambda: g.scalar.activation(ap(o), ap(i), f, **kw), [o], [i, bias, scale], cycles(o, [i], 1) if i[0] == "@" or not OPT["sest"] else 65 + size(o))

    def move(q, o, i):
        return cp(o, i) if q == "V" else act(o, i, ACT.Copy)

    def sfill(o, c):
        return act(o, v("zer", 0, size(o)), ACT.Identity, bias=c)

    def mm(o, wq, ws_, xq, xs, start=True, stop=True):
        return record("P", lambda: g.tensor.matmul_mx(ap(o), ap(wq), ap(ws_), ap(xq), ap(xs), start, stop), [o], [wq, ws_, xq, xs], OPT["pest"] * (16 + size(o)))

    def iota(o, pat, ch=0):
        kw = {} if _SB[o[0]][1] == I32 else {"allow_small_or_imprecise_dtypes": True}
        return record("G", lambda: g.iota(ap(o), pat, 0, ch, **kw), [o], [], 160 + 2 * size(o))

    def dma(q, out, in_, outs, ins, done=LOAD, **kw):
        ndma[0] += 1
        return record(q, lambda: queue[q].dma_start(out(), in_(), **kw), outs, ins, 700 if q == "G" else 60, sem="dm%d" % ndma[0], count=16, done=done)

    def partner(r):
        return T.cores[rank ^ STEP[r]]

    def remote(r, dst, src, sem, codes, done):
        p = partner(r)
        rid, pid, _ = topo.addr(p)
        sent[0] += len(topo.engines(core, p))

        def go():
            o, i = ap(dst), ap(src)
            if codes:
                o, i = o.bitcast(dt.uint8), i.bitcast(dt.uint8)
            g.remote_dma(o, i, T.sem[sem], T.sem.sent, pid, rid, topo.mask(core, p))
        writes.setdefault(sem, []).append(record("G", go, [], [src], 300, sem="none", done=done))

    def arrival(r, outs, sem):
        record("-", None, outs, [], 0, sem=sem, count=len(writes[sem]) * len(topo.engines(partner(r), core)), after=writes[sem])

    def mirror(name, t, a, b):
        return v(name, 4 * (TURN - a) + t, 4 * (TURN - b) + t, -4)

    products, at, ahead, named = [], {}, {}, []
    PARTS = {"A": (K, C, 4), "B": (0, K, 0)}
    dma("Y", lambda: T.X0[:, 4 * K:4 * C], lambda: T.x[:, 4 * K:4 * C], [v("X0", 4 * K, 4 * C)], [], LOAD + 0.6)
    row([dma("S", lambda: T.ut[:], lambda: T.u[:], [v("ut")], []),
         dma("S", lambda: T.X0[:, 0:4 * K], lambda: T.x[:, 0:4 * K], [v("X0", 0, 4 * K)], [], LOAD + 1.0)])
    if OPT["dadd"]:
        dma("G", lambda: T.sw[:], lambda: T.ws[:], [v("sw")], [])

    def late_loads():
        dma("Y", lambda: T.qw[:].bitcast(dt.uint8), lambda: T.wc[:], [v("qw")], [v("offa")], 2 * LOAD)
        if not OPT["dadd"]:
            dma("Y", lambda: T.sw[:], lambda: T.ws[:], [v("sw")], [v("offa")], 2 * LOAD)
        dma("Y", lambda: T.vt[:], lambda: T.v[:], [v("vt")], [v("offb")], 8 * LOAD)
        quant(v("qv"), v("sv"), v("vt"))
    constants = len(ops)
    row([iota(v("pint"), [[16, 2]], 1), iota(v("oui"), [[1, 2], [16, 8]]), iota(v("Js"), [[0, 8], [1, 16]]),
         iota(v("Jq"), [[0, 3], [1, 16], [0, 4]]), iota(v("Jg"), [[16, 8], [0, 16]]), iota(v("J"), [[1, 464]])])
    fill(v("zer"), 0.0)
    for z in ("rsM", "rsQ", "Fa", "Fb", "Ut"):
        for c in range(0, _SB[z][0], 512):
            (fill if z + str(c) in OPT["fv"] else sfill)(v(z, c, min(c + 512, _SB[z][0])), 0.0)
    sfill(v("rsM", 4, C, 4), -4 * BIG)
    sfill(v("rsQ", 0, 192, 64), -4 * BIG)
    act(v("Jb"), v("J", 0, 128), ACT.Copy)
    ts(v("iint", 0, 1), v("pint", 0, 1), 15, None, A.bitwise_and)
    ts(v("iint", 1, 2), v("pint", 0, 1), 3, None, A.bitwise_and)
    ts(v("iint", 2, 3), v("pint", 0, 1), 12, 2, A.bitwise_and, A.logical_shift_right)
    ts(v("iint", 3, 4), v("pint", 0, 1), 7, None, A.bitwise_and)
    cp(v("pf", 0, 1), v("pint", 0, 1))
    cp(v("fi"), v("iint"))
    P16, P4, PQ, P8 = (v("fi", i, i + 1) for i in range(4))
    cp(v("pb", 0, 1), P16)
    tt(v("pb", 1, 2), v("pf", 0, 1), P16, A.subtract)
    ts(v("ident"), v("J", 0, 128), v("pf", 0, 1), None, A.is_equal)
    for q in range(2):
        ts(v("Rp", 128 * q, 128 * q + 1), P16, 16.0 * q + 1, STEPK, A.add, A.mult)
    ts(v("nk", 0, 1), P8, 16.0, None, A.add)
    NK = (P16, v("nk", 0, 1))
    cp(v("ou"), v("oui"))
    ts(v("tie"), v("Js", 0, 112), v("pb", 0, 1), -TINY, A.is_gt, A.mult)
    ts(v("mask"), v("Js"), v("pb", 0, 1), None, A.is_equal)
    ts(v("mneg"), v("Jq"), v("pb", 0, 1), -4 * BIG, A.not_equal, A.mult)
    ts(v("mneg", 0, 1), v("mask", 0, 1), 5 * BIG, -4 * BIG, A.mult, A.add)
    ts(v("blk"), v("Jg"), v("pb", 1, 2), None, A.is_equal)
    act(v("Ut", 3, 515, 4), v("ident"), ACT.Copy)
    for b in range(4):
        act(v("Wt", b, 512, 4), v("blk"), ACT.Copy)
        at["e%d" % b] = quant(v("qd", 128 * b, 128 * b + 128), v("sd", 128 * b, 128 * b + 128), v("Ut", 3 - b, 515 - b))
        sfill(v("Sp", 128 * b + 112, 128 * b + 120), 0.0)
    ts(v("rsa"), v("Js", 0, 112), 0.0, None, A.not_equal)
    quant(v("qo"), v("so"), v("Wt"))
    sfill(v("Sp", 0, 1), BIG)
    sfill(v("sela", 112, 120), -STEPK)
    sfill(v("selb", 96, 104), -STEPK)
    sfill(v("Kw", C, 456), 0.0)
    sfill(v("cod"), 0.0)
    sfill(v("Zm", C, 480), 0.0)
    for q in range(2):
        ts(v("tieb", 25 - 25 * q, 49 - 25 * q), v("J", 0, 24), NK[q], TINY, A.is_lt, A.mult)
        ts(v("maskk", 16 * q, 16 * q + 16), v("J", 16 * q, 16 * q + 16), NK[q], None, A.is_equal)
    ts(v("rsb"), v("J", 0, 75), 25.0, None, A.not_equal)
    sfill(v("dk", 24, 25), -1.0)
    sfill(v("tieb", 24, 25), 0.0)
    ts(v("LL", 24, 25), P16, 7.5, float(C), A.is_gt, A.mult)
    ts(v("PR", 49, 75), v("J", 49, 75), 74.0, float(C), A.is_equal, A.mult)
    ts(v("r4m"), v("Js", 0, 4), P4, -4 * BIG, A.not_equal, A.mult)
    ts(v("r4a"), v("Js", 0, 4), PQ, 4 * HOLD, A.is_equal, A.mult)
    ts(v("r4b"), v("Js", 0, 4), -1.0, PQ, A.add, A.is_equal)
    ts(v("r4b"), v("r4b"), -HOLD, None, A.mult)
    tt(v("r4c"), v("r4a"), v("r4b"), A.add)
    for e in range(4):
        act(v("rb", e, C, 4), v("zer", 0, C // 4), ACT.Identity, bias=v("r4c", e, e + 1))
    ts(v("m4"), v("rb", 0, 32), 1.0, -4 * BIG, A.is_lt, A.mult)
    ts(v("ab", 0, 1), PQ, 3.0, 4 * HOLD, A.is_lt, A.mult)
    tt(v("ab", 1, 2), v("ab", 0, 1), P4, A.add)
    if not OPT["mirD"]:
        ts(v("ab", 2, 3), v("ab", 0, 1), -2.0 * TURN, None, A.add)
        ts(v("ab", 3, 4), P4, 2.0 * TURN, None, A.add)
    lazy.update(range(constants, len(ops)))
    quant(v("qu"), v("su"), v("ut"))
    def pick(j):
        return (record("V", lambda: g.vector.tensor_copy(T.qup[:, 128 * j:128 * j + 128].bitcast(dt.uint32),
                                                         T.qu[:, 0:128].bitcast(dt.uint32).indirect(T.ou[:, 8 * j:8 * j + 8])),
                       [v("qup", 128 * j, 128 * j + 128)], [v("qu"), v("ou")], 260),
                act(v("sup", 128 * j, 128 * j + 128), ind(v("su"), v("ou", 8 * j, 8 * j + 8)), ACT.Copy))
    picks = pick(0) + pick(1)

    def state_quant(r, part):
        a, b, k = PARTS[part]
        X, qx, sx = "X%d" % r, v("qx%d" % r, a, b), v("sx%d" % r, a, b)
        m = OPT["cut"] if a and r and OPT["split"] else a
        at["qC"] = quant(v(qx[0], a, m), v(sx[0], a, m), v(X, 4 * a, 4 * m)) if m > a else at.get("qC") if r else None
        first = quant(v(qx[0], m, b), v(sx[0], m, b), v(X, 4 * m, 4 * b))
        if r == R:
            mm(bank(k, 0, b - a), v("qv"), v("sv"), qx, sx)
            return first, None
        remote(r, v("lq%d" % r, a, b), qx, "arr%d" % r, True, OPT["codes"])
        remote(r, v("ls%d" % r, a, b), sx, "arr%d" % r, False, OPT["codes"])
        ahead["s" + part] = mm(bank(k, 0, b - a), v("qup", 0, 128), v("sup", 0, 128), qx, sx)
        def planes():
            for e in range(4):
                s = 1 if a == 0 and e == 0 else 0
                ahead["P%s%d" % (part, e)] = act(v("Sp", 128 * e + a // 4 + s, 128 * e + b // 4), bank(k, e + 4 * s, b - a, 4), ACT.Copy)
        if a and r and OPT["pf"]:
            planes()
        ahead["n" + part] = tt(v("Mq", a, min(b, 192)), bank(k, 0, min(b, 192) - a), v("mneg", a, min(b, 192)), A.add)
        ahead["m" + part] = scan(v("Ms", a, b), v("rsM", a, b), bank(k, 0, b - a), BIG if a == 0 else 0.0, A.add, A.max)
        if not (a and r and OPT["pf"]):
            planes()
        for e in range(4):
            if OPT["mirX"]:
                ahead["x%s%d" % (part, e)] = move(OPT["mirX"], mirror(X, e, a, b), v(X, 4 * a + e, 4 * b, 4))
            if OPT["tsplit"] or not a:
                z = b if OPT["tsplit"] else C
                ahead["T%s%d" % (part, e)] = act(v("Tm", a + e, z, 4), v("Sp", 128 * e + a // 4, 128 * e + z // 4), ACT.Identity, bias=v("r4m", e, e + 1))
        if OPT["k2"]:
            ahead["k" + part + "m"] = mm(bank(k + 1, 0, b - a), v("qup", 128, 256), v("sup", 128, 256), qx, sx)
            ahead["K" + part] = act(v("Kw", a, b), bank(k + 1, 0, b - a), ACT.Copy)
        elif a == 0:
            ahead["sK"] = mm(bank(1, 0, C), v("qup", 128, 256), v("sup", 128, 256), v(qx[0]), v(sx[0]))
            ahead["KB"] = act(v("Kw", 0, C), bank(1, 0, C), ACT.Copy)
        return first, ahead["m" + part]

    def part_of(src, c0, c1):
        return (src[0], src[1] + src[2] * c0, src[1] + src[2] * (c1 - 1) + 1, src[2])

    def owned(c0, c1):
        scan(v("own", c0, c1), v("rsa", c0, c1), v("Mm", c0, c1), 0.0, A.mult, A.add)

    BLOCKS, COLUMNS = ("Ms", 3, 4), ("Cd", 0, 1)

    def select(src, mine, halves, cuts, on_scalar, F, sel, w, vals):
        nq = len(halves[0]) + len(halves[1]) - 1
        n = 16 * nq

        def slot(q, c0, c1):
            h = 0 if q in halves[0] else 1
            o = 512 * h + halves[h].index(q)
            return v(F, o + 4 * c0, o + 4 * (c1 - 1) + 1, 4)
        for q in range(nq):
            me = mine(q)
            at[F + "D%d" % q] = act(v("dd", 16 * q, 16 * q + 16), part_of(src, 16 * q, 16 * q + 16), ACT.Identity, bias=me, scale=-1.0)
            lo = cuts if 16 * q >= cuts else 0
            if lo and q in OPT["la"] and on_scalar is OPT["sa"]:
                at[F + "B%d" % q] = act(v("sh", lo * (6 - q), lo * (7 - q)), part_of(src, 0, lo), ACT.Sign, bias=me, scale=-1.0)
                at[F + "E%d" % q] = act(slot(q, 0, lo), v("sh", lo * (6 - q), lo * (7 - q)), ACT.Relu)
            elif lo:
                at[F + "b%d" % q] = ts(slot(q, 0, lo), part_of(src, 0, lo), me, None, A.is_lt)
            if q in on_scalar:
                o = 112 * on_scalar.index(q)
                hi = n if q < nq - 1 else n - 16
                l2 = lo if 16 * q > lo else 16 * q + 16
                at[F + "S%d" % q] = act(v("sg", o + l2, o + hi), part_of(src, l2, hi), ACT.Sign, bias=me, scale=-1.0)
                if 16 * q > lo:
                    at[F + "L%d" % q] = act(slot(q, lo, 16 * q), v("sg", o + lo, o + 16 * q), ACT.Relu)
                if q < nq - 1:
                    at[F + "G%d" % q] = act(slot(q, 16 * q + 16, n), v("sg", o + 16 * q + 16, o + n), ACT.Sign, bias=1.0)
                continue
            if 16 * q > lo:
                at[F + "l%d" % q] = ts(slot(q, lo, 16 * q), part_of(src, lo, 16 * q), me, None, A.is_lt)
            if q < nq - 1:
                at[F + "g%d" % q] = ts(slot(q, 16 * q + 16, n), part_of(src, 16 * q + 16, n), me, None, A.is_le)
        for c0, c1 in ((cuts, n), (0, cuts)):
            if c1 > c0:
                at[F + "t%d" % (c0 > 0)] = tt(slot("tie", c0, c1), v("dd", c0, c1), v("tie", c0, c1), A.is_gt)
        for h in range(2):
            at[F + "pq"[h]] = quant(v("qf", 128 * h, 128 * h + 128), v("sf", 128 * h, 128 * h + 128), v(F, 512 * h, 512 * h + 512))
            at[F + "m%d" % h] = mm(bank(3, 0, 128), v("qo"), v("so"), v("qf", 128 * h, 128 * h + 128), v("sf", 128 * h, 128 * h + 128), h == 0, h == 1)
        at[F + "s"] = ts(v(sel, 0, n), bank(3, 0, n), 23.5, -STEPK, A.is_lt, A.mult)
        for q in range(2):
            at[F + "r%d" % q] = scan(v("Rp", 128 * q + 1, 128 * q + w), v(sel, 0, w - 1), v("zer", 0, w - 1), v("Rp", 128 * q, 128 * q + 1), A.add, A.max)
        for q in range(2):
            at[F + "c%d" % q] = scan(v("cap", 128 * q, 128 * q + w), v("Rp", 128 * q, 128 * q + w), v(vals, 0, w), 0.0, A.add, A.min)
        return v("cap", w - 1, w + 128, 128)

    RUNS = ((K, OPT["cut"], 0), (OPT["cut"], C, 4), (0, K, 0))

    def order(r):
        at["kA"] = tt(v("Mm", 48, 112), part_of(BLOCKS, 48, 112), v("mask", 48, 112), A.mult)
        at["oA"] = scan(v("own", 48, 112), v("rsa", 48, 112), v("Mm", 48, 112), 0.0, A.mult, A.add)
        at["oB"] = scan(v("ownq"), v("rsQ"), v("Mq"), 0.0, A.add, A.max)
        for e in range(4):
            c = e * C // 4
            at["z%d" % e] = scan(v("Zm", c, c + C // 4), v("rsM", c, c + C // 4), v("Tm", c, c + C // 4), -4 * BIG, A.add, A.max)
        at.update(ahead)
        blocks = select(BLOCKS, lambda q: v("own", 16 * q + 15, 16 * q + 16) if q > 2 else v("ownq", 64 * q + 63, 64 * q + 64),
                        ((3, 4, 5, 6), (0, 1, 2, "tie")), 48, OPT["sa" if r else "sa0"], "Fa", "sela", 120, "Jb")
        at["oz"] = ts(v("offz"), blocks, 4.0, 3.0, A.mult, A.add)
        at["oa"] = cp(v("offa"), blocks)
        at["mc"] = tt(v("Mc"), ind(v("Zm"), v("offz")), v("m4"), A.add)
        at["ow"] = scan(v("ownc"), v("rsM", 0, 24), v("Mc", 0, 24), -4 * BIG, A.add, A.max)
        for e in range(4):
            at["c%d" % e] = move("V" if e < OPT["cd"] else "S", v("Cd", e, 128, 4), ind(v("Sp", 128 * e, 128 * e + 120), v("offa")))
        for e in range(4):
            at["C%d" % e] = act(v("cc", e, 128, 4), ind(v("J", 0, 128), v("offa")), ACT.Identity, bias=e - MID, scale=4.0)
        heads = select(COLUMNS, lambda q: v("ownc", 4 * q + 3, 4 * q + 4), ((1, 2, 3, 4), (0, 5, "tie")), 0, OPT["sb"], "Fb", "selb", 104, "cc")
        at["ob"] = ts(v("offb"), heads, MID, None, A.add)
        at["op"] = ts(v("offp"), heads, MID - 1, None, A.add)
        arrival(r, [v("lq%d" % r), v("ls%d" % r)], "arr%d" % r)
        for b in range(4):
            at["n%d" % b] = mm(bank(4 + b, 0, C), v("qd", 128 * b, 128 * b + 128), v("sd", 128 * b, 128 * b + 128), v("lq%d" % r), v("ls%d" % r))
            at["D%d" % b] = act(v("Dp", b, 4 * C, 4), bank(4 + b, 0, C), ACT.Copy)
            for h in range(2 if OPT["mirD"] else 0):
                c = h * C // 2
                at["d%d%d" % (b, h)] = cp(mirror("Dp", b, c, c + C // 2), v("Dp", 4 * c + b, 4 * c + 2 * C, 4))
        at["km"] = tt(v("km"), ind(v("Kw"), v("offb")), v("maskk"), A.mult)
        cp(v("key"), ind(v("Kw"), v("offb")))
        at["H"] = act(v("Ha"), ind(v("J"), v("offb")), ACT.Copy)
        at["KP"] = act(v("kp"), ind(v("Kw"), v("offp")), ACT.Copy)
        at["WB"] = act(v("Wb"), ind(v("J"), v("offb")), ACT.Identity, bias=TURN + 1.0, scale=-1.0)
        scan(v("ko"), v("rsa", 0, 32), v("km"), 0.0, A.mult, A.add)
        for q in range(2):
            o = 25 - 25 * q
            tt(v("LL", o, o + 24), v("Ha", 1, 25), v("Ha", 0, 24), A.subtract)
            if q:
                at["DK"] = act(v("dk", o, o + 24), v("key", 0, 24), ACT.Identity, bias=v("ko", 16 * q + 15, 16 * q + 16), scale=-1.0)
            else:
                at["dk"] = ts(v("dk", o, o + 24), v("key", 0, 24), -1.0, v("ko", 16 * q + 15, 16 * q + 16), A.mult, A.add)
        tt(v("turn"), v("key", 0, 24), v("kp", 1, 25), A.is_lt)
        at["fl"] = tt(v("FL"), v("dk"), v("tieb"), A.is_lt)
        tt(v("ca"), v("turn"), v("Wb", 1, 25), A.mult)
        at["pr"] = tt(v("PR", 0, 49), v("FL"), v("LL"), A.mult)
        tt(v("cod", 16, 40), v("ca"), v("Ha", 0, 24), A.max)
        at["pp"] = scan(v("Pp"), v("rsb"), v("PR"), 0.0, A.mult, A.add)
        at["oc"] = cp(v("offc", 0, 3), v("Pp", 74, 23, -25))
        for h in range(2):
            at["W%d" % h] = sfill(v("Ww", C * h, C * h + C), 1.0)
        at["sc"] = cp(ind(v("Ww"), v("offc", 0, 3)), v("cod"))
        cut = OPT["cut"]
        at["u0"] = scan(v("us", 0, cut), v("Ww", C, C + cut), v("Ww", 0, cut), 0.0, A.mult, A.add)
        at["u1"] = scan(v("us", cut, C), v("Ww", C + cut, 2 * C), v("Ww", cut, C), v("us", cut - 1, cut), A.mult, A.add) if cut < C else None
        for i, (a, b, k) in enumerate(RUNS):
            at["w%d" % i] = scan(v("wr", a, b), v("rb", a, b), v("us", a, b), 0.0, A.add, A.min)
            if OPT["mirX" if a else "mirD"]:
                at["t%d" % i] = ts(v("ord%d" % r, a // 4, b // 4), v("wr", a + 3, b, 4), 4.0, v("ab", 1, 2), A.mult, A.add)
            else:
                at["A%d" % i] = act(v("oo", a // 4, b // 4), v("wr", a + 3, b, 4), ACT.Abs, bias=v("ab", 2, 3), scale=4.0)
                at["t%d" % i] = ts(v("ord%d" % r, a // 4, b // 4), v("oo", a // 4, b // 4), -1.0, v("ab", 3, 4), A.mult, A.add)
        remote(r, v("lst%d" % r), v("ord%d" % r, 0, K // 4), "lis%d" % r, False, OPT["list"])
        arrival(r, [v("lst%d" % r)], "lis%d" % r)


    def layer(r):
        X, Y = "X%d" % r, "X%d" % (r + 1)
        for i, (a, b, k) in enumerate(RUNS):
            win, lst = (v(X, 0, 8 * C if OPT["mirX"] else 4 * C), "ord%d" % r) if a else (v("Dp", 0, 8 * C if OPT["mirD"] else 4 * C), "lst%d" % r)
            m = [a, a + OPT["g"][i], b - OPT["h"][i], b]
            for name, q, c0, c1 in zip("gGI", "VSS", m, m[1:]):
                at["%s%d" % (name, i)] = move(q, v(Y, 4 * c0, 4 * c1), ind(win, v(lst, c0 // 4, c1 // 4))) if c1 > c0 else None
            at["q%d" % i] = quant(v("qe", a, b), v("se", a, b), v(Y, 4 * a, 4 * b))
            for j in range(4):
                at["m%d%d" % (i, j)] = mm(bank(k + j, 0, b - a), v("qw", 128 * j, 128 * j + 128), v("sw", 128 * j, 128 * j + 128), v("qe", a, b), v("se", a, b))
                at["R%d%d" % (i, j)] = act(v("Rr", 4 * a + j, 4 * b, 4), bank(k + j, 0, b - a), ACT.Relu, scale=0.015625)
                if i == 0 and OPT["dadd"]:
                    at["a%d%d" % (i, j)] = None
                else:
                    at["a%d%d" % (i, j)] = tt(v(Y, 4 * a + j, 4 * b, 4), v(Y, 4 * a + j, 4 * b, 4), v("Rr", 4 * a + j, 4 * b, 4), A.add)
            if i == 0 and OPT["dadd"]:
                add_by_dma(v(Y, 4 * a, 4 * b), v("Rr", 4 * a, 4 * b))
            if b == C:
                at["qA"] = state_quant(r + 1, "A")[0]
        at["qB"] = state_quant(r + 1, "B")[0]

    def add_by_dma(y, x):
        dma("G", lambda: ap(y), lambda: ap(x), [y], [y, x], OPT["dlat"], accum_op=A.add)

    a0, b0 = state_quant(0, "A"), state_quant(0, "B")
    at.update({"pu": picks[0], "PU": picks[1], "pk": picks[2], "PK": picks[3], "fA": a0[0], "fB": b0[0]})
    for r in range(R):
        order(r)
        if r == 0:
            late_loads()
        layer(r)
        named.append(dict(at))
        at.clear()
    for r in range(R):
        for names in (OPT["V"], OPT["S"], OPT["P"]):
            calls = [(named + [{}])[r + 1].get(w[1:]) if w[0] == "+" else named[r].get(w) for w in names.split()]
            row([o for o in calls if o is not None])
    for names in (OPT["V0"], OPT["S0"], OPT["P0"]):
        row([named[0][w] for w in names.split() if w in named[0]])
    QL, SL = "qx%d" % R, "sx%d" % R
    act(v("ola"), v("us"), ACT.Abs, bias=-TURN / 2)
    act(v("olt"), v("ola"), ACT.Identity, bias=TURN / 2, scale=-1.0)
    dma("Y", lambda: T.ol[:], lambda: T.olt[0:128:16, :], [], [v("olt")])

    def store(part):
        a, b, k = PARTS[part]
        dma("Y" if a else "S", lambda: T.oc[:, 4 * a:4 * b], lambda: T[QL][:, a:b].bitcast(dt.uint8), [], [v(QL, a, b)])
        move("S" if a else "V", v("yt", a, b), bank(k, 0, b - a))
        dma("Y", lambda: T.y[:, a:b], lambda: T.yt[:, a:b], [], [v("yt", a, b)])

    def scales(k):
        dma("Y" if k < 1 else "S", lambda: T.osc[4 * k:4 * k + 4, 0:C], lambda: T[SL][32 * k:32 * k + 4, 0:C], [], [v(SL)])
    store("A")
    store("B")
    for k in range(4):
        scales(k)

    wait = OPT["wait"]
    QUEUES, every = list(queue) + ["-"], range(len(ops))
    users = [[] for _ in ops]
    for me, op in enumerate(ops):
        for o in op["deps"] | op["behind"]:
            users[o].append(me)

    def gap(o, me):
        if o in ops[me]["deps"]:
            return ops[o]["done"] + wait + (OPT["lazy"] if o in lazy and me not in lazy else 0.0)
        return ops[o]["done"] if ops[me]["q"] == "-" else ops[o]["hold"]

    def lay(turn, before, least, first):
        at, busy = {}, {q: [] for q in QUEUES}
        for me in turn:
            t = max([first(me)] + [at[o] + least(o, me) for o in before(me)])
            taken, hold = busy[ops[me]["q"]], ops[me]["hold"]
            i = len(taken)
            while i and taken[i - 1][1] > t:
                i -= 1
            while i < len(taken) and taken[i][0] < t + hold - 1e-9:
                t = max(t, taken[i][1])
                i += 1
            taken.insert(i, (t, t + hold))
            at[me] = t
        return at
    missing = [len(op["deps"] | op["behind"]) for op in ops]
    sort = [o for o in every if not missing[o]]
    for o in sort:
        for u in users[o]:
            missing[u] -= 1
            if not missing[u]:
                sort.append(u)
    assert len(sort) == len(ops)
    tail = [0.0] * len(ops)
    for me in reversed(sort):
        tail[me] = max([ops[me]["done"]] + [gap(me, u) + tail[u] for u in users[me]])
    turn, best = sorted(every, key=lambda o: (-tail[o], o)), None
    for _ in range(OPT["passes"]):
        at = lay(turn, lambda o: ops[o]["deps"] | ops[o]["behind"], gap, lambda o: 0.0)
        end = max(at[o] + ops[o]["done"] for o in every)
        if best is None or end < best[0] - 1e-9:
            best = (end, at)
        late = lay(sorted(every, key=lambda o: (-at[o] - ops[o]["hold"], -o)), lambda o: users[o],
                   lambda u, o: gap(o, u) + ops[u]["hold"] - ops[o]["hold"], lambda o: ops[o]["done"] - ops[o]["hold"])
        turn = sorted(every, key=lambda o: (-late[o] - ops[o]["hold"], o))
    issue = sorted(every, key=lambda o: (best[1][o], o))
    place = {o: i for i, o in enumerate(issue)}

    def line(o):
        return ops[o]["q"] if ops[o]["sem"] is None else ops[o]["sem"]
    known = {q: {} for q in QUEUES}
    waited, wanted = set(), {}
    for op in ops:
        for o in op["deps"]:
            if ops[o]["sem"] is None:
                wanted.setdefault((op["q"], ops[o]["q"]), set()).add(o)
    for me in issue:
        op = ops[me]
        kn, need = known[op["q"]], {}
        for o in op["deps"]:
            if ops[o]["sem"] != "none":
                need[line(o)] = max(need.get(line(o), -1), place[o])
        for l in need:
            if kn.get(l, -1) < need[l]:
                spare = OPT["spare"][0 if l == op["q"] else 1]
                need[l] = max([need[l]] + [place[o] for o in wanted.get((op["q"], l), ())
                                           if best[1][o] + ops[o]["done"] + wait + spare <= best[1][me]])
        op["waits"] = []
        for i in sorted(need.values(), reverse=True):
            o = issue[i]
            if kn.get(line(o), -1) >= i:
                continue
            op["waits"].append(o)
            waited.add(o)
            kn[line(o)] = i
            for l, x in ops[o]["knows"].items():
                kn[l] = max(kn.get(l, -1), x)
        op["knows"] = dict(kn)
    count = {q: 0 for q in queue}
    left = []
    for me in issue:
        op = ops[me]
        if op["q"] == "-":
            continue
        for o in op["waits"]:
            w = ops[o]
            queue[op["q"]].wait_ge(T.sem["s" + w["q"] if w["sem"] is None else w["sem"]], w["count"])
        ins = op["fn"]()
        if op["sem"] is None:
            if me in waited:
                count[op["q"]] += 1
                op["count"] = count[op["q"]]
                ins.then_inc(T.sem["s" + op["q"]], 1)
        elif op["sem"] != "none":
            ins.then_inc(T.sem[op["sem"]], 16)
            if me not in waited:
                left.append(op)
    for op in left:
        queue[op["q"]].wait_ge(T.sem[op["sem"]], 16)
    g.wait_ge(T.sem.sent, sent[0])
